import numpy as np
import ml_dtypes


def mxq(x, axis, fmt="e4m3"):
    dtype, down = {"e4m3": (ml_dtypes.float8_e4m3fn, 7), "e5m2": (ml_dtypes.float8_e5m2, 14)}[fmt]
    v = np.moveaxis(np.asarray(x, np.float32).astype(ml_dtypes.bfloat16).astype(np.float64), axis, -1)
    blocks = v.reshape(v.shape[:-1] + (-1, 32))
    amax = np.abs(blocks).max(-1, keepdims=True)
    byte = np.maximum(np.where(amax > 0, np.frexp(amax)[1] - 1 + 127, 0) - down, 1)
    scale = np.exp2(byte - 127.0)
    codes = (blocks / scale).astype(np.float32).astype(dtype).astype(np.float64)
    return np.moveaxis((codes * scale).reshape(v.shape), -1, axis)


WIDE = False


def mx_kscale(k):
    if not WIDE:
        return np.ones(k)
    levels = np.array([18, -18])
    if k % 512:
        return np.exp2(np.random.permutation(np.resize(levels, k // 32))).repeat(32)
    a = np.empty((k // 512, 16))
    for p in range(k // 512):
        a[p, :8] = np.random.permutation(np.resize(levels, 8))
        for g in range(8):
            far = levels[np.abs(levels - a[p, g]) >= 10]
            a[p, g + 8] = far[np.random.randint(len(far))]
    return np.exp2(a.ravel()).repeat(32)


def f64(x):
    return np.asarray(x).astype(np.float64)


def striped(idx):
    return np.tile(np.asarray(idx).reshape(-1, 16).T, (8, 1)).astype(np.uint16)


def unstriped(offs):
    return offs[:16].T.reshape(-1).astype(np.int64)


E2M1 = np.array([0.0, 0.5, 1.0, 1.5, 2.0, 3.0, 4.0, 6.0, -0.0, -0.5, -1.0, -1.5, -2.0, -3.0, -4.0, -6.0])


def pack_weight(w, fmt):
    k, n = w.shape
    w = f64(np.asarray(w, np.float32).astype(ml_dtypes.bfloat16)).reshape(k // 32, 32, n)
    amax = np.abs(w).max(1)
    if fmt == "e4m3":
        byte = np.frexp(amax)[1] - 1 + 127 - 7
    else:
        mant, ex = np.frexp(amax / 6.0)
        byte = np.where(mant > 0.5, ex, ex - 1) + 127
    byte = np.clip(np.where(amax > 0, byte, 1), 1, 254)
    scaled = (w * np.exp2(127.0 - byte)[:, None, :]).reshape(k, n).astype(np.float32)
    by_word = np.ascontiguousarray(scaled.reshape(k // 512, 128, 4, n).transpose(0, 1, 3, 2))
    if fmt == "e4m3":
        words = by_word.astype(ml_dtypes.float8_e4m3fn).view(np.uint8)
    else:
        c = by_word.astype(ml_dtypes.float4_e2m1fn).view(np.uint8) & 0xF
        words = (c[..., 0::2] | (c[..., 1::2] << 4)).reshape(k // 512, 128, 2 * n)
    return np.ascontiguousarray(words), np.ascontiguousarray(byte.astype(np.uint8).reshape(k // 512, 16, n))


def unpack_weight(words, scales, fmt):
    g, _, n = scales.shape
    words = np.ascontiguousarray(words).reshape(g, 128, n, -1)
    if fmt == "e4m3":
        vals = words.view(ml_dtypes.float8_e4m3fn).astype(np.float64)
    else:
        nib = np.empty((g, 128, n, 4), np.uint8)
        nib[..., 0::2] = words & 0xF
        nib[..., 1::2] = words >> 4
        vals = E2M1[nib]
    vals = vals * np.repeat(np.exp2(scales.astype(np.float64) - 127.0), 8, axis=1)[..., None]
    return vals.transpose(0, 1, 3, 2).reshape(g * 512, n)


B, N, T, D, R = 1, 512, 2048, 1024, 512


def setup_inputs():
    n = np.random.standard_normal
    idx = np.random.permutation(T)[:B * N]
    s = mx_kscale(D)[:, None]
    z = mx_kscale(R)[:, None]
    r = np.random.uniform(0.5, 2.0, T)
    x = n((B, D, R))
    teach = np.exp(n((B, R, N)))
    teach = teach / teach.sum(-1, keepdims=True)
    wp = pack_weight(n((D, T)) * (0.50 / np.sqrt(D)) / s / r, "e2m1")
    return {
        "xT": (x * s).astype(np.float32),
        "w_words": np.ascontiguousarray(wp[0].reshape(1, 2, 128, T, 2).transpose(0, 2, 3, 1, 4)).reshape(1, 128, T, 4),
        "w_scales": wp[1],
        "y": teach.astype(np.float32),
        "wt": (np.random.uniform(0.5, 1.5, (B, R, 1)) * N / np.sqrt(R) * z).astype(np.float32),
        "ts": np.tile(r, (128, 1)).astype(np.float32),
        "xm": (x.transpose(0, 2, 1) / z).astype(np.float32),
        "offs": striped(idx),
    }


def reference(xT, w_words, w_scales, y, wt, ts, xm, offs):
    idx = unstriped(offs)
    w = unpack_weight(w_words.reshape(1, 128, T, 2, 2).transpose(0, 3, 1, 2, 4).reshape(2, 128, 2 * T), w_scales, "e2m1")
    pick = lambda x: x[:, idx].reshape(x.shape[0], B, N).transpose(1, 0, 2)
    a = mxq(f64(xT), 1, "e4m3").transpose(0, 2, 1) @ pick(w)
    ts_ = pick(f64(ts))[:, :1, :]
    a = a * ts_
    e = np.exp(a - a.max(-1, keepdims=True))
    g = f64(wt) * (e / e.sum(-1, keepdims=True) - f64(y))
    g = g * ts_
    dw = mxq(f64(xm), 1, "e4m3").transpose(0, 2, 1) @ mxq(g, 1, "e5m2")
    gw = np.zeros((D, T))
    gw[:, idx] = dw.transpose(1, 0, 2).reshape(D, B * N)
    return gw

@@ -1,0 +1,216 @@
+from contextlib import ExitStack
+
+import concourse.mybir as mybir
+from concourse.masks import make_identity
+
+N, T, D, R = 512, 2048, 1024, 512
+FLOPS = 2 * 2 * D * R * N
+
+F32 = mybir.dt.float32
+BF16 = mybir.dt.bfloat16
+I32 = mybir.dt.int32
+U32 = mybir.dt.uint32
+U16 = mybir.dt.uint16
+U8 = mybir.dt.uint8
+E4M3 = mybir.dt.float8_e4m3fn_x4
+E5M2 = mybir.dt.float8_e5m2_x4
+E2M1 = mybir.dt.float4_e2m1fn_x4
+ALU = mybir.AluOpType
+ACT = mybir.ActivationFunctionType
+
+P = 128
+PACK = 4
+PASSES = D // (P * PACK)
+BLOCKS = D // P
+WINDOWS = 3
+XM_PIECES = 4
+XM_COLS = D // XM_PIECES
+CAST_SPLIT = 44
+
+
+def tile_attend_gkl_w_ts_kernel(tc, xT, w_words, w_scales, y, wt, ts, xm, offs, out):
+    nc = tc.nc
+    with ExitStack() as ctx:
+        keep = ctx.enter_context(tc.tile_pool(name="keep", bufs=1))
+        ring = ctx.enter_context(tc.tile_pool(name="ring", bufs=3))
+        psum_scores = ctx.enter_context(tc.psum_pool(name="psum_scores", bufs=1))
+        psum_ring = ctx.enter_context(tc.psum_pool(name="psum_ring", bufs=4))
+
+        def held(name, shape, dtype):
+            return keep.tile(shape, dtype, name=name, align_bytes=64)
+
+        offsets = keep.tile([P, N // 16], U16, name="offsets")
+        nc.sync.dma_start(offsets[:], offs)
+
+        scale_pool = held("scale_pool", [P, PASSES * T // 4], I32)
+        nc.vector.memset(scale_pool[:], 0)
+        warm = held("warm", [P, 1], F32)
+        warm_out = held("warm_out", [P, 1], F32)
+        nc.gpsimd.memset(warm[:], 0.0)
+        nc.scalar.activation(warm_out[:], warm[:], ACT.Exp)
+        ident = held("ident", [P, P], F32)
+        make_identity(nc, ident[:])
+
+        ts_cols = held("ts_cols", [P, T // P], F32)
+        nc.sync.dma_start(ts_cols[:], ts[0:1, :].rearrange("o (p c) -> (o p) c", p=P))
+        wt_sb = held("wt_sb", [P, PACK], F32)
+        nc.sync.dma_start(wt_sb[:], wt[0].rearrange("(p t) o -> p (t o)", t=PACK))
+        scale_rows = w_scales.rearrange("o f t -> f o t").bitcast(I32)
+        for q in range(4):
+            nc.sync.dma_start(
+                scale_pool[32 * q : 32 * q + 4, :].rearrange("f (o t) -> f o t", o=PASSES),
+                scale_rows[4 * q : 4 * q + 4],
+            )
+        x_raw = [held("x_raw%d" % o, [P, PACK, R], F32) for o in range(PASSES)]
+        word_pool = held("word_pool", [P, T], I32)
+
+        def load_x(o):
+            nc.sync.dma_start(x_raw[o][:], xT[0, 512 * o : 512 * (o + 1), :].rearrange("(p j) r -> p j r", j=PACK))
+
+        load_x(0)
+        nc.sync.dma_start(word_pool[:], w_words[0].rearrange("p t b -> p (t b)").bitcast(I32))
+        load_x(1)
+        y_sb = held("y_sb", [P, PACK, N], F32)
+        nc.sync.dma_start(y_sb[:], y[0].rearrange("(p t) i -> p t i", t=PACK))
+        xm_rows = xm[0].rearrange("(p j) d -> p j d", j=PACK)
+        xm_raw = [held("xm_raw%d" % c, [P, PACK, XM_COLS], F32) for c in range(XM_PIECES)]
+        for c in range(XM_PIECES):
+            nc.sync.dma_start(xm_raw[c][:], xm_rows[:, :, c * XM_COLS : (c + 1) * XM_COLS])
+
+        windows = [held("window%d" % k, [P, T], F32) for k in range(WINDOWS)]
+        for k in range(WINDOWS):
+            nc.vector.memset(windows[k][:], 0.0)
+
+        ts_pool = held("ts_pool", [P, T], F32)
+        ts_view = ts_pool[:].rearrange("m (p c) -> m p c", p=P)
+        for b in range(4):
+            bank = psum_ring.tile([P, PACK, P], F32, name="bank")
+            for k in range(PACK):
+                c = PACK * b + k
+                nc.tensor.transpose(bank[:, k, :], ts_cols[:, c : c + 1].to_broadcast([P, P]), ident[:])
+            nc.scalar.activation(ts_view[:, :, PACK * b : PACK * (b + 1)], bank[:].rearrange("m k p -> m p k"), ACT.Copy)
+
+        w_scale = held("w_scale", [P, PASSES * N], U8)
+        scale_bytes = scale_pool[:].bitcast(U8)
+        for o in range(PASSES):
+            nc.vector.tensor_copy(w_scale[:, o * N : (o + 1) * N], scale_bytes[:, o * T : (o + 1) * T].indirect(offsets[:]))
+        ts_sel = held("ts_sel", [P, N], F32)
+        nc.vector.tensor_copy(ts_sel[:], ts_pool[:].indirect(offsets[:]))
+        w_pair = held("w_pair", [P, N], U32)
+        nc.vector.tensor_copy(w_pair[:], word_pool[:].bitcast(U32).indirect(offsets[:]))
+        w_code = held("w_code", [P, PASSES * 2 * N], U8)
+        nc.vector.tensor_copy(
+            w_code[:].bitcast(U16).rearrange("p (o i) -> p o i", o=PASSES),
+            w_pair[:].bitcast(U16).rearrange("p (i o) -> p o i", o=PASSES),
+        )
+
+        x_bf = [held("x_bf%d" % o, [P, PACK * P * PACK], BF16) for o in range(PASSES)]
+        x_code = [held("x_code%d" % o, [P, R], U32) for o in range(PASSES)]
+        x_scale = [held("x_scale%d" % o, [P, R], U8) for o in range(PASSES)]
+
+        def x_views(o, lo, hi):
+            dst = x_bf[o][:].rearrange("p (t m j) -> p m j t", t=PACK, j=PACK)[:, lo:hi]
+            src = x_raw[o][:].rearrange("p j (m t) -> p m j t", t=PACK)[:, lo:hi]
+            return dst, src
+
+        scores = [psum_scores.tile([P, N], F32, name="scores%d" % t) for t in range(PACK)]
+        for o in range(PASSES):
+            if o == 0:
+                nc.scalar.copy(*x_views(o, 0, P))
+            else:
+                nc.scalar.copy(*x_views(o, 0, CAST_SPLIT))
+                nc.vector.tensor_copy(*x_views(o, CAST_SPLIT, P))
+            nc.vector.quantize_mx(out=x_code[o][:].bitcast(E4M3), scales=x_scale[o][:], in_=x_bf[o][:])
+            for t in range(PACK):
+                nc.tensor.matmul_mx(
+                    out=scores[t][:],
+                    lhsT=x_code[o][:, t * P : (t + 1) * P].bitcast(E4M3),
+                    lhsT_scale=x_scale[o][:, t * P : (t + 1) * P],
+                    rhs=w_code[:, o * 2 * N : (o + 1) * 2 * N].bitcast(E2M1),
+                    rhs_scale=w_scale[:, o * N : (o + 1) * N],
+                    start=(o == 0),
+                    stop=(o == PASSES - 1),
+                )
+
+        wt_ts = held("wt_ts", [P, PACK, N], F32)
+        for t in range(PACK):
+            nc.scalar.activation(wt_ts[:, t, :], ts_sel[:], ACT.Copy, scale=wt_sb[:, t : t + 1])
+
+        neg_a = [held("neg_a%d" % t, [P, N], F32) for t in range(PACK)]
+        neg_max = [held("neg_max%d" % t, [P, 1], F32) for t in range(PACK)]
+        e = [held("e%d" % t, [P, N], F32) for t in range(PACK)]
+        total = [held("total%d" % t, [P, 1], F32) for t in range(PACK)]
+        inv = [held("inv%d" % t, [P, 1], F32) for t in range(PACK)]
+        g = held("g", [P, PACK, N], F32)
+
+        def scale_scores(t):
+            nc.vector.scalar_tensor_tensor(neg_a[t][:], scores[t][:], -1.0, ts_sel[:], ALU.mult, ALU.mult)
+
+        def exponentiate(t):
+            nc.vector.tensor_reduce(neg_max[t][:], neg_a[t][:], mybir.AxisListType.X, ALU.min)
+            nc.scalar.activation(e[t][:], neg_a[t][:], ACT.Exp, bias=neg_max[t][:], scale=-1.0, accum_out=total[t][:])
+
+        def invert(t):
+            nc.vector.reciprocal(inv[t][:], total[t][:])
+
+        def subtract_targets(t):
+            nc.vector.scalar_tensor_tensor(g[:, t, :], e[t][:], inv[t][:], y_sb[:, t, :], ALU.mult, ALU.subtract)
+
+        scale_scores(0)
+        for t in range(PACK):
+            if t + 1 < PACK:
+                scale_scores(t + 1)
+            exponentiate(t)
+        invert(0)
+        for t in range(PACK):
+            if t + 1 < PACK:
+                invert(t + 1)
+            subtract_targets(t)
+
+        h_bf = held("h_bf", [P, N, PACK], BF16)
+        h_code = held("h_code", [P, N], U32)
+        h_scale = held("h_scale", [P, N], U8)
+        halves = [slice(0, N // 2), slice(N // 2, N)]
+        for s in halves:
+            nc.vector.tensor_tensor(
+                h_bf[:, s, :],
+                g[:, :, s].rearrange("p t i -> p i t"),
+                wt_ts[:, :, s].rearrange("p t i -> p i t"),
+                ALU.mult,
+            )
+        for s in halves:
+            nc.vector.quantize_mx(
+                out=h_code[:, s].bitcast(E5M2), scales=h_scale[:, s], in_=h_bf[:, s, :].rearrange("p i t -> p (i t)")
+            )
+
+        xm_bf = [held("xm_bf%d" % c, [P, XM_COLS * PACK], BF16) for c in range(XM_PIECES)]
+        xm_code = [held("xm_code%d" % c, [P, XM_COLS], U32) for c in range(XM_PIECES)]
+        xm_scale = [held("xm_scale%d" % c, [P, XM_COLS], U8) for c in range(XM_PIECES)]
+
+        def quantise_xm(c):
+            for u in range(XM_COLS // P):
+                dst = xm_bf[c][:].rearrange("p (c i j) -> p c j i", i=4, j=PACK)[:, 32 * u : 32 * (u + 1)]
+                src = xm_raw[c][:].rearrange("p j (c i) -> p c j i", i=4)[:, 32 * u : 32 * (u + 1)]
+                nc.scalar.copy(dst, src)
+            nc.vector.quantize_mx(out=xm_code[c][:].bitcast(E4M3), scales=xm_scale[c][:], in_=xm_bf[c][:])
+
+        per_piece = XM_COLS // P
+        for m in range(BLOCKS):
+            c, u = divmod(m, per_piece)
+            if u == 0:
+                quantise_xm(c)
+            bank = psum_ring.tile([P, N], F32, name="bank")
+            nc.tensor.matmul_mx(
+                out=bank[:],
+                lhsT=xm_code[c][:, u * P : (u + 1) * P].bitcast(E4M3),
+                lhsT_scale=xm_scale[c][:, u * P : (u + 1) * P],
+                rhs=h_code[:].bitcast(E5M2),
+                rhs_scale=h_scale[:],
+                start=True,
+                stop=True,
+            )
+            dw = ring.tile([P, N], F32, name="dw")
+            nc.scalar.copy(dw[:], bank[:])
+            window = windows[m % WINDOWS]
+            nc.vector.tensor_copy(window[:].indirect(offsets[:]), dw[:])
+            nc.sync.dma_start(out[m * P : (m + 1) * P, :], window[:])

@@ -25,25 +25,27 @@ BLOCKS = D // P
 WINDOWS = 3
 XM_PIECES = 4
 XM_COLS = D // XM_PIECES
-CAST_SPLIT = 44
+CAST_SPLIT = 52
 
 
 def tile_attend_gkl_w_ts_kernel(tc, xT, w_words, w_scales, y, wt, ts, xm, offs, out):
     nc = tc.nc
     with ExitStack() as ctx:
         keep = ctx.enter_context(tc.tile_pool(name="keep", bufs=1))
+        placed = ctx.enter_context(tc.tile_pool(name="placed", bufs=1))
         ring = ctx.enter_context(tc.tile_pool(name="ring", bufs=3))
         psum_scores = ctx.enter_context(tc.psum_pool(name="psum_scores", bufs=1))
         psum_ring = ctx.enter_context(tc.psum_pool(name="psum_ring", bufs=4))
 
-        def held(name, shape, dtype):
-            return keep.tile(shape, dtype, name=name, align_bytes=64)
+        def held(name, shape, dtype, slot=None):
+            return keep.tile(shape, dtype, name=name, tag=slot or name, align_bytes=64)
 
         offsets = keep.tile([P, N // 16], U16, name="offsets")
         nc.sync.dma_start(offsets[:], offs)
 
-        scale_pool = held("scale_pool", [P, PASSES * T // 4], I32)
-        nc.vector.memset(scale_pool[:], 0)
+        scale_pool = placed.tile([P, PASSES * T // 4], I32, name="scale_pool", align_bytes=64, offset=0)
+        nc.gpsimd.memset(scale_pool[:, : T // 4], 0)
+        nc.vector.memset(scale_pool[:, T // 4 :], 0)
         warm = held("warm", [P, 1], F32)
         warm_out = held("warm_out", [P, 1], F32)
         nc.gpsimd.memset(warm[:], 0.0)
@@ -55,30 +57,20 @@ def tile_attend_gkl_w_ts_kernel(tc, xT, w_words, w_scales, y, wt, ts, xm, offs, 
         nc.sync.dma_start(ts_cols[:], ts[0:1, :].rearrange("o (p c) -> (o p) c", p=P))
         wt_sb = held("wt_sb", [P, PACK], F32)
         nc.sync.dma_start(wt_sb[:], wt[0].rearrange("(p t) o -> p (t o)", t=PACK))
+        word_pool = held("word_pool", [P, T], I32)
+        nc.sync.dma_start(word_pool[:], w_words[0].rearrange("p t b -> p (t b)").bitcast(I32))
+        x_rows = [xT[0, 512 * o : 512 * (o + 1), :].rearrange("(p j) r -> p j r", j=PACK) for o in range(PASSES)]
+        x_raw = [held("x_raw0", [P, PACK, R], F32)]
+        nc.sync.dma_start(x_raw[0][:], x_rows[0])
         scale_rows = w_scales.rearrange("o f t -> f o t").bitcast(I32)
         for q in range(4):
             nc.sync.dma_start(
                 scale_pool[32 * q : 32 * q + 4, :].rearrange("f (o t) -> f o t", o=PASSES),
                 scale_rows[4 * q : 4 * q + 4],
             )
-        x_raw = [held("x_raw%d" % o, [P, PACK, R], F32) for o in range(PASSES)]
-        word_pool = held("word_pool", [P, T], I32)
 
-        def load_x(o):
-            nc.sync.dma_start(x_raw[o][:], xT[0, 512 * o : 512 * (o + 1), :].rearrange("(p j) r -> p j r", j=PACK))
-
-        load_x(0)
-        nc.sync.dma_start(word_pool[:], w_words[0].rearrange("p t b -> p (t b)").bitcast(I32))
-        load_x(1)
-        y_sb = held("y_sb", [P, PACK, N], F32)
-        nc.sync.dma_start(y_sb[:], y[0].rearrange("(p t) i -> p t i", t=PACK))
-        xm_rows = xm[0].rearrange("(p j) d -> p j d", j=PACK)
-        xm_raw = [held("xm_raw%d" % c, [P, PACK, XM_COLS], F32) for c in range(XM_PIECES)]
-        for c in range(XM_PIECES):
-            nc.sync.dma_start(xm_raw[c][:], xm_rows[:, :, c * XM_COLS : (c + 1) * XM_COLS])
-
-        windows = [held("window%d" % k, [P, T], F32) for k in range(WINDOWS)]
-        for k in range(WINDOWS):
+        windows = [held("window%d" % k, [P, T], F32) for k in range(WINDOWS - 1)]
+        for k in range(WINDOWS - 1):
             nc.vector.memset(windows[k][:], 0.0)
 
         ts_pool = held("ts_pool", [P, T], F32)
@@ -88,14 +80,11 @@ def tile_attend_gkl_w_ts_kernel(tc, xT, w_words, w_scales, y, wt, ts, xm, offs, 
             for k in range(PACK):
                 c = PACK * b + k
                 nc.tensor.transpose(bank[:, k, :], ts_cols[:, c : c + 1].to_broadcast([P, P]), ident[:])
-            nc.scalar.activation(ts_view[:, :, PACK * b : PACK * (b + 1)], bank[:].rearrange("m k p -> m p k"), ACT.Copy)
+            dst, src = ts_view[:, :, PACK * b : PACK * (b + 1)], bank[:].rearrange("m k p -> m p k")
+            nc.scalar.activation(dst, src, ACT.Copy)
+        x_raw.append(held("x_raw1", [P, PACK, R], F32, slot="ts_cols"))
+        nc.sync.dma_start(x_raw[1][:], x_rows[1])
 
-        w_scale = held("w_scale", [P, PASSES * N], U8)
-        scale_bytes = scale_pool[:].bitcast(U8)
-        for o in range(PASSES):
-            nc.vector.tensor_copy(w_scale[:, o * N : (o + 1) * N], scale_bytes[:, o * T : (o + 1) * T].indirect(offsets[:]))
-        ts_sel = held("ts_sel", [P, N], F32)
-        nc.vector.tensor_copy(ts_sel[:], ts_pool[:].indirect(offsets[:]))
         w_pair = held("w_pair", [P, N], U32)
         nc.vector.tensor_copy(w_pair[:], word_pool[:].bitcast(U32).indirect(offsets[:]))
         w_code = held("w_code", [P, PASSES * 2 * N], U8)
@@ -103,9 +92,20 @@ def tile_attend_gkl_w_ts_kernel(tc, xT, w_words, w_scales, y, wt, ts, xm, offs, 
             w_code[:].bitcast(U16).rearrange("p (o i) -> p o i", o=PASSES),
             w_pair[:].bitcast(U16).rearrange("p (i o) -> p o i", o=PASSES),
         )
+        ts_sel = held("ts_sel", [P, N], F32, slot="w_pair")
+        nc.vector.tensor_copy(ts_sel[:], ts_pool[:].indirect(offsets[:]))
+        y_sb = held("y_sb", [P, PACK, N], F32, slot="ts_pool")
+        nc.sync.dma_start(y_sb[:], y[0].rearrange("(p t) i -> p t i", t=PACK))
+        w_scale = held("w_scale", [P, PASSES * N], U8)
+        scale_bytes = scale_pool[:].bitcast(U8)
+        for o in range(PASSES):
+            nc.vector.tensor_copy(w_scale[:, o * N : (o + 1) * N], scale_bytes[:, o * T : (o + 1) * T].indirect(offsets[:]))
 
-        x_bf = [held("x_bf%d" % o, [P, PACK * P * PACK], BF16) for o in range(PASSES)]
-        x_code = [held("x_code%d" % o, [P, R], U32) for o in range(PASSES)]
+        x_bf = [
+            held("x_bf0", [P, PACK * R], BF16, slot="ident"),
+            placed.tile([P, PACK * R], BF16, name="x_bf1", align_bytes=64, offset=4 * R),
+        ]
+        x_code = [placed.tile([P, R], U32, name="x_code0", align_bytes=64, offset=0), held("x_code1", [P, R], U32)]
         x_scale = [held("x_scale%d" % o, [P, R], U8) for o in range(PASSES)]
 
         def x_views(o, lo, hi):
@@ -132,7 +132,18 @@ def tile_attend_gkl_w_ts_kernel(tc, xT, w_words, w_scales, y, wt, ts, xm, offs, 
                     stop=(o == PASSES - 1),
                 )
 
-        wt_ts = held("wt_ts", [P, PACK, N], F32)
+        xm_rows = xm[0].rearrange("(p j) d -> p j d", j=PACK)
+        xm_first = held("xm_first", [P, 2, PACK, XM_COLS], F32, slot="x_raw0")
+        xm_raw = [
+            xm_first[:, 0],
+            xm_first[:, 1],
+            held("xm_raw2", [P, PACK, XM_COLS], F32, slot="ident")[:],
+            placed.tile([P, PACK, XM_COLS], F32, name="xm_raw3", align_bytes=64, offset=4 * R)[:],
+        ]
+        for c in range(XM_PIECES):
+            nc.sync.dma_start(xm_raw[c], xm_rows[:, :, c * XM_COLS : (c + 1) * XM_COLS])
+
+        wt_ts = held("wt_ts", [P, PACK, N], F32, slot="ts_cols")
         for t in range(PACK):
             nc.scalar.activation(wt_ts[:, t, :], ts_sel[:], ACT.Copy, scale=wt_sb[:, t : t + 1])
 
@@ -167,6 +178,27 @@ def tile_attend_gkl_w_ts_kernel(tc, xT, w_words, w_scales, y, wt, ts, xm, offs, 
                 invert(t + 1)
             subtract_targets(t)
 
+        xm_bf = [held("xm_bf%d" % m, [P, PACK * P], BF16, slot="neg_a%d" % m)[:] for m in range(PACK - 1)]
+        bf_rest = held("xm_bf_rest", [P, BLOCKS - PACK + 1, PACK * P], BF16, slot="neg_a3")
+        xm_bf.extend(bf_rest[:, k, :] for k in range(BLOCKS - PACK + 1))
+        xm_code = [held("xm_code0", [P, P], U32, slot="e1")[:]]
+        xm_scale = held("xm_scale", [P, D], U8)
+        for m in range(BLOCKS):
+            c, u = divmod(m, XM_COLS // P)
+            nc.scalar.copy(
+                xm_bf[m].rearrange("p (c i j) -> p c j i", i=4, j=PACK),
+                xm_raw[c][:, :, u * P : (u + 1) * P].rearrange("p j (c i) -> p c j i", i=4),
+            )
+
+        def quantise_xm(m):
+            nc.vector.quantize_mx(out=xm_code[m].bitcast(E4M3), scales=xm_scale[:, m * P : (m + 1) * P], in_=xm_bf[m])
+
+        quantise_xm(0)
+
+        last_window = held("last_window", [P, T], F32, slot="e0")
+        nc.gpsimd.memset(last_window[:], 0.0)
+        windows.append(last_window)
+
         h_bf = held("h_bf", [P, N, PACK], BF16)
         h_code = held("h_code", [P, N], U32)
         h_scale = held("h_scale", [P, N], U8)
@@ -183,27 +215,17 @@ def tile_attend_gkl_w_ts_kernel(tc, xT, w_words, w_scales, y, wt, ts, xm, offs, 
                 out=h_code[:, s].bitcast(E5M2), scales=h_scale[:, s], in_=h_bf[:, s, :].rearrange("p i t -> p (i t)")
             )
 
-        xm_bf = [held("xm_bf%d" % c, [P, XM_COLS * PACK], BF16) for c in range(XM_PIECES)]
-        xm_code = [held("xm_code%d" % c, [P, XM_COLS], U32) for c in range(XM_PIECES)]
-        xm_scale = [held("xm_scale%d" % c, [P, XM_COLS], U8) for c in range(XM_PIECES)]
+        code_rest = held("xm_code_rest", [P, D - P], U32, slot="h_bf")
+        xm_code.extend(code_rest[:, k * P : (k + 1) * P] for k in range(BLOCKS - 1))
+        for m in range(1, BLOCKS):
+            quantise_xm(m)
 
-        def quantise_xm(c):
-            for u in range(XM_COLS // P):
-                dst = xm_bf[c][:].rearrange("p (c i j) -> p c j i", i=4, j=PACK)[:, 32 * u : 32 * (u + 1)]
-                src = xm_raw[c][:].rearrange("p j (c i) -> p c j i", i=4)[:, 32 * u : 32 * (u + 1)]
-                nc.scalar.copy(dst, src)
-            nc.vector.quantize_mx(out=xm_code[c][:].bitcast(E4M3), scales=xm_scale[c][:], in_=xm_bf[c][:])
-
-        per_piece = XM_COLS // P
         for m in range(BLOCKS):
-            c, u = divmod(m, per_piece)
-            if u == 0:
-                quantise_xm(c)
             bank = psum_ring.tile([P, N], F32, name="bank")
             nc.tensor.matmul_mx(
                 out=bank[:],
-                lhsT=xm_code[c][:, u * P : (u + 1) * P].bitcast(E4M3),
-                lhsT_scale=xm_scale[c][:, u * P : (u + 1) * P],
+                lhsT=xm_code[m].bitcast(E4M3),
+                lhsT_scale=xm_scale[:, m * P : (m + 1) * P],
                 rhs=h_code[:].bitcast(E5M2),
                 rhs_scale=h_scale[:],
                 start=True,

@@ -26,6 +26,8 @@ WINDOWS = 3
 XM_PIECES = 4
 XM_COLS = D // XM_PIECES
 CAST_SPLIT = 52
+HALF = R // 2
+X1_AT = 8192
 
 
 def tile_attend_gkl_w_ts_kernel(tc, xT, w_words, w_scales, y, wt, ts, xm, offs, out):
@@ -40,10 +42,13 @@ def tile_attend_gkl_w_ts_kernel(tc, xT, w_words, w_scales, y, wt, ts, xm, offs, 
         def held(name, shape, dtype, slot=None):
             return keep.tile(shape, dtype, name=name, tag=slot or name, align_bytes=64)
 
+        def fixed(name, shape, dtype, at):
+            return placed.tile(shape, dtype, name=name, align_bytes=64, offset=at)
+
         offsets = keep.tile([P, N // 16], U16, name="offsets")
         nc.sync.dma_start(offsets[:], offs)
 
-        scale_pool = placed.tile([P, PASSES * T // 4], I32, name="scale_pool", align_bytes=64, offset=0)
+        scale_pool = fixed("scale_pool", [P, PASSES * T // 4], I32, 0)
         nc.gpsimd.memset(scale_pool[:, : T // 4], 0)
         nc.vector.memset(scale_pool[:, T // 4 :], 0)
         warm = held("warm", [P, 1], F32)
@@ -53,7 +58,7 @@ def tile_attend_gkl_w_ts_kernel(tc, xT, w_words, w_scales, y, wt, ts, xm, offs, 
         ident = held("ident", [P, P], F32)
         make_identity(nc, ident[:])
 
-        ts_cols = held("ts_cols", [P, T // P], F32)
+        ts_cols = fixed("ts_cols", [P, T // P], F32, X1_AT)
         nc.sync.dma_start(ts_cols[:], ts[0:1, :].rearrange("o (p c) -> (o p) c", p=P))
         wt_sb = held("wt_sb", [P, PACK], F32)
         nc.sync.dma_start(wt_sb[:], wt[0].rearrange("(p t) o -> p (t o)", t=PACK))
@@ -69,8 +74,8 @@ def tile_attend_gkl_w_ts_kernel(tc, xT, w_words, w_scales, y, wt, ts, xm, offs, 
                 scale_rows[4 * q : 4 * q + 4],
             )
 
-        windows = [held("window%d" % k, [P, T], F32) for k in range(WINDOWS - 1)]
-        for k in range(WINDOWS - 1):
+        windows = [held("window%d" % k, [P, T], F32) for k in range(WINDOWS)]
+        for k in range(WINDOWS):
             nc.vector.memset(windows[k][:], 0.0)
 
         ts_pool = held("ts_pool", [P, T], F32)
@@ -82,7 +87,7 @@ def tile_attend_gkl_w_ts_kernel(tc, xT, w_words, w_scales, y, wt, ts, xm, offs, 
                 nc.tensor.transpose(bank[:, k, :], ts_cols[:, c : c + 1].to_broadcast([P, P]), ident[:])
             dst, src = ts_view[:, :, PACK * b : PACK * (b + 1)], bank[:].rearrange("m k p -> m p k")
             nc.scalar.activation(dst, src, ACT.Copy)
-        x_raw.append(held("x_raw1", [P, PACK, R], F32, slot="ts_cols"))
+        x_raw.append(fixed("x_raw1", [P, PACK, R], F32, X1_AT))
         nc.sync.dma_start(x_raw[1][:], x_rows[1])
 
         w_pair = held("w_pair", [P, N], U32)
@@ -101,36 +106,50 @@ def tile_attend_gkl_w_ts_kernel(tc, xT, w_words, w_scales, y, wt, ts, xm, offs, 
         for o in range(PASSES):
             nc.vector.tensor_copy(w_scale[:, o * N : (o + 1) * N], scale_bytes[:, o * T : (o + 1) * T].indirect(offsets[:]))
 
-        x_bf = [
-            held("x_bf0", [P, PACK * R], BF16, slot="ident"),
-            placed.tile([P, PACK * R], BF16, name="x_bf1", align_bytes=64, offset=4 * R),
-        ]
-        x_code = [placed.tile([P, R], U32, name="x_code0", align_bytes=64, offset=0), held("x_code1", [P, R], U32)]
+        x_bf = [held("x_bf0", [P, PACK * R], BF16, slot="ident"), fixed("x_bf1", [P, PACK * R], BF16, 4 * R)]
+        x_code = {
+            (0, 0): fixed("x_code00", [P, HALF], U32, 0),
+            (0, 1): fixed("x_code01", [P, HALF], U32, X1_AT),
+            (1, 0): held("x_code10", [P, HALF], U32),
+            (1, 1): held("x_code11", [P, HALF], U32),
+        }
         x_scale = [held("x_scale%d" % o, [P, R], U8) for o in range(PASSES)]
 
         def x_views(o, lo, hi):
-            dst = x_bf[o][:].rearrange("p (t m j) -> p m j t", t=PACK, j=PACK)[:, lo:hi]
-            src = x_raw[o][:].rearrange("p j (m t) -> p m j t", t=PACK)[:, lo:hi]
+            dst = x_bf[o][:].rearrange("p (t m j) -> p m t j", t=PACK, j=PACK)[:, lo:hi]
+            src = x_raw[o][:].rearrange("p j (m t) -> p m t j", t=PACK)[:, lo:hi]
             return dst, src
 
+        def quantise_x(o, u):
+            nc.vector.quantize_mx(
+                out=x_code[o, u][:].bitcast(E4M3),
+                scales=x_scale[o][:, u * HALF : (u + 1) * HALF],
+                in_=x_bf[o][:, u * PACK * HALF : (u + 1) * PACK * HALF],
+            )
+
         scores = [psum_scores.tile([P, N], F32, name="scores%d" % t) for t in range(PACK)]
-        for o in range(PASSES):
-            if o == 0:
-                nc.scalar.copy(*x_views(o, 0, P))
-            else:
-                nc.scalar.copy(*x_views(o, 0, CAST_SPLIT))
-                nc.vector.tensor_copy(*x_views(o, CAST_SPLIT, P))
-            nc.vector.quantize_mx(out=x_code[o][:].bitcast(E4M3), scales=x_scale[o][:], in_=x_bf[o][:])
-            for t in range(PACK):
-                nc.tensor.matmul_mx(
-                    out=scores[t][:],
-                    lhsT=x_code[o][:, t * P : (t + 1) * P].bitcast(E4M3),
-                    lhsT_scale=x_scale[o][:, t * P : (t + 1) * P],
-                    rhs=w_code[:, o * 2 * N : (o + 1) * 2 * N].bitcast(E2M1),
-                    rhs_scale=w_scale[:, o * N : (o + 1) * N],
-                    start=(o == 0),
-                    stop=(o == PASSES - 1),
-                )
+
+        def score_pass(t, o):
+            u, k = divmod(t, 2)
+            nc.tensor.matmul_mx(
+                out=scores[t][:],
+                lhsT=x_code[o, u][:, k * P : (k + 1) * P].bitcast(E4M3),
+                lhsT_scale=x_scale[o][:, t * P : (t + 1) * P],
+                rhs=w_code[:, o * 2 * N : (o + 1) * 2 * N].bitcast(E2M1),
+                rhs_scale=w_scale[:, o * N : (o + 1) * N],
+                start=(o == 0),
+                stop=(o == PASSES - 1),
+            )
+
+        nc.scalar.copy(*x_views(0, 0, P))
+        quantise_x(0, 0)
+        nc.scalar.copy(*x_views(1, 0, CAST_SPLIT))
+        nc.vector.tensor_copy(*x_views(1, CAST_SPLIT, P))
+        quantise_x(1, 0)
+        quantise_x(0, 1)
+        quantise_x(1, 1)
+        for t, o in ((0, 0), (1, 0), (0, 1), (1, 1), (2, 0), (2, 1), (3, 0), (3, 1)):
+            score_pass(t, o)
 
         xm_rows = xm[0].rearrange("(p j) d -> p j d", j=PACK)
         xm_first = held("xm_first", [P, 2, PACK, XM_COLS], F32, slot="x_raw0")
@@ -138,12 +157,12 @@ def tile_attend_gkl_w_ts_kernel(tc, xT, w_words, w_scales, y, wt, ts, xm, offs, 
             xm_first[:, 0],
             xm_first[:, 1],
             held("xm_raw2", [P, PACK, XM_COLS], F32, slot="ident")[:],
-            placed.tile([P, PACK, XM_COLS], F32, name="xm_raw3", align_bytes=64, offset=4 * R)[:],
+            fixed("xm_raw3", [P, PACK, XM_COLS], F32, 4 * R)[:],
         ]
         for c in range(XM_PIECES):
             nc.sync.dma_start(xm_raw[c], xm_rows[:, :, c * XM_COLS : (c + 1) * XM_COLS])
 
-        wt_ts = held("wt_ts", [P, PACK, N], F32, slot="ts_cols")
+        wt_ts = fixed("wt_ts", [P, PACK, N], F32, X1_AT + 4 * HALF)
         for t in range(PACK):
             nc.scalar.activation(wt_ts[:, t, :], ts_sel[:], ACT.Copy, scale=wt_sb[:, t : t + 1])
 
@@ -195,19 +214,15 @@ def tile_attend_gkl_w_ts_kernel(tc, xT, w_words, w_scales, y, wt, ts, xm, offs, 
 
         quantise_xm(0)
 
-        last_window = held("last_window", [P, T], F32, slot="e0")
-        nc.gpsimd.memset(last_window[:], 0.0)
-        windows.append(last_window)
-
         h_bf = held("h_bf", [P, N, PACK], BF16)
         h_code = held("h_code", [P, N], U32)
         h_scale = held("h_scale", [P, N], U8)
         halves = [slice(0, N // 2), slice(N // 2, N)]
         for s in halves:
             nc.vector.tensor_tensor(
-                h_bf[:, s, :],
-                g[:, :, s].rearrange("p t i -> p i t"),
-                wt_ts[:, :, s].rearrange("p t i -> p i t"),
+                h_bf[:, s, :].rearrange("p (c i) t -> p c t i", i=2),
+                g[:, :, s].rearrange("p t (c i) -> p c t i", i=2),
+                wt_ts[:, :, s].rearrange("p t (c i) -> p c t i", i=2),
                 ALU.mult,
             )
         for s in halves:

@@ -1,7 +1,6 @@
 from contextlib import ExitStack
 
 import concourse.mybir as mybir
-from concourse.masks import make_identity
 
 N, T, D, R = 512, 2048, 1024, 512
 FLOPS = 2 * 2 * D * R * N
@@ -23,11 +22,8 @@ PACK = 4
 PASSES = D // (P * PACK)
 BLOCKS = D // P
 WINDOWS = 3
-XM_PIECES = 4
-XM_COLS = D // XM_PIECES
-CAST_SPLIT = 52
 HALF = R // 2
-X1_AT = 8192
+KIB = 1024
 
 
 def tile_attend_gkl_w_ts_kernel(tc, xT, w_words, w_scales, y, wt, ts, xm, offs, out):
@@ -47,36 +43,32 @@ def tile_attend_gkl_w_ts_kernel(tc, xT, w_words, w_scales, y, wt, ts, xm, offs, 
 
         offsets = keep.tile([P, N // 16], U16, name="offsets")
         nc.sync.dma_start(offsets[:], offs)
-
-        scale_pool = fixed("scale_pool", [P, PASSES * T // 4], I32, 0)
-        nc.gpsimd.memset(scale_pool[:, : T // 4], 0)
-        nc.vector.memset(scale_pool[:, T // 4 :], 0)
-        warm = held("warm", [P, 1], F32)
-        warm_out = held("warm_out", [P, 1], F32)
-        nc.gpsimd.memset(warm[:], 0.0)
-        nc.scalar.activation(warm_out[:], warm[:], ACT.Exp)
-        ident = held("ident", [P, P], F32)
-        make_identity(nc, ident[:])
-
-        ts_cols = fixed("ts_cols", [P, T // P], F32, X1_AT)
-        nc.sync.dma_start(ts_cols[:], ts[0:1, :].rearrange("o (p c) -> (o p) c", p=P))
+        ts_cols = placed.tile([P, T // P], F32, name="ts_cols", offset=20 * KIB - 32)
+        nc.scalar.dma_start(ts_cols[:], ts[0:1, :].rearrange("o (p c) -> (o p) c", p=P))
         wt_sb = held("wt_sb", [P, PACK], F32)
-        nc.sync.dma_start(wt_sb[:], wt[0].rearrange("(p t) o -> p (t o)", t=PACK))
+        nc.scalar.dma_start(wt_sb[:], wt[0].rearrange("(p t) o -> p (t o)", t=PACK))
+
         word_pool = held("word_pool", [P, T], I32)
         nc.sync.dma_start(word_pool[:], w_words[0].rearrange("p t b -> p (t b)").bitcast(I32))
-        x_rows = [xT[0, 512 * o : 512 * (o + 1), :].rearrange("(p j) r -> p j r", j=PACK) for o in range(PASSES)]
-        x_raw = [held("x_raw0", [P, PACK, R], F32)]
-        nc.sync.dma_start(x_raw[0][:], x_rows[0])
-        scale_rows = w_scales.rearrange("o f t -> f o t").bitcast(I32)
-        for q in range(4):
-            nc.sync.dma_start(
-                scale_pool[32 * q : 32 * q + 4, :].rearrange("f (o t) -> f o t", o=PASSES),
-                scale_rows[4 * q : 4 * q + 4],
-            )
 
-        windows = [held("window%d" % k, [P, T], F32) for k in range(WINDOWS)]
-        for k in range(WINDOWS):
-            nc.vector.memset(windows[k][:], 0.0)
+        scale_pool = held("scale_pool", [P, T // 4], I32)
+        nc.gpsimd.memset(scale_pool[:], 0)
+        scale_rows = w_scales.bitcast(I32)
+        for q in range(4):
+            nc.sync.dma_start(scale_pool[32 * q : 32 * q + 8, :], scale_rows[:, 4 * q : 4 * q + 4, :])
+
+        zeros = held("zeros", [P, P], F32, slot="x_first")
+        nc.gpsimd.memset(zeros[:], 0.0)
+        ident = held("ident", [P, P], F32)
+        nc.gpsimd.affine_select(
+            out=ident[:], in_=zeros[:], compare_op=ALU.not_equal, fill=1.0, base=0, pattern=[[-1, P]], channel_multiplier=1
+        )
+        x_rows = [xT[0, 512 * o : 512 * (o + 1), :].rearrange("(p j) r -> p j r", j=PACK) for o in range(PASSES)]
+        x_first = held("x_first", [P, PACK, R], F32)
+        nc.sync.dma_start(x_first[:], x_rows[0])
+
+        first_window = held("window0", [P, T], F32)
+        nc.vector.memset(first_window[:], 0.0)
 
         ts_pool = held("ts_pool", [P, T], F32)
         ts_view = ts_pool[:].rearrange("m (p c) -> m p c", p=P)
@@ -85,46 +77,52 @@ def tile_attend_gkl_w_ts_kernel(tc, xT, w_words, w_scales, y, wt, ts, xm, offs, 
             for k in range(PACK):
                 c = PACK * b + k
                 nc.tensor.transpose(bank[:, k, :], ts_cols[:, c : c + 1].to_broadcast([P, P]), ident[:])
-            dst, src = ts_view[:, :, PACK * b : PACK * (b + 1)], bank[:].rearrange("m k p -> m p k")
-            nc.scalar.activation(dst, src, ACT.Copy)
-        x_raw.append(fixed("x_raw1", [P, PACK, R], F32, X1_AT))
-        nc.sync.dma_start(x_raw[1][:], x_rows[1])
+            nc.scalar.copy(ts_view[:, :, PACK * b : PACK * (b + 1)], bank[:].rearrange("m k p -> m p k"))
+        x_second = [fixed("x_second0", [P, PACK, HALF], F32, 16 * KIB), fixed("x_second1", [P, PACK, HALF], F32, 20 * KIB)]
+        for h in range(2):
+            nc.sync.dma_start(x_second[h][:], x_rows[1][:, :, h * HALF : (h + 1) * HALF])
 
         w_pair = held("w_pair", [P, N], U32)
         nc.vector.tensor_copy(w_pair[:], word_pool[:].bitcast(U32).indirect(offsets[:]))
+        w_scale_both = held("w_scale_both", [P, N], U8)
+        nc.vector.tensor_copy(w_scale_both[:], scale_pool[:].bitcast(U8).indirect(offsets[:]))
+        w_scale_second = held("w_scale_second", [P, N // 4], I32, slot="ident")
+        nc.vector.memset(w_scale_second[:], 0)
+        for q in range(4):
+            nc.sync.dma_start(w_scale_second[32 * q : 32 * q + 4, :], w_scale_both[:].bitcast(I32)[32 * q + 4 : 32 * q + 8, :])
+        w_scale = [w_scale_both[:], w_scale_second[:].bitcast(U8)]
+
         w_code = held("w_code", [P, PASSES * 2 * N], U8)
         nc.vector.tensor_copy(
             w_code[:].bitcast(U16).rearrange("p (o i) -> p o i", o=PASSES),
             w_pair[:].bitcast(U16).rearrange("p (i o) -> p o i", o=PASSES),
         )
-        ts_sel = held("ts_sel", [P, N], F32, slot="w_pair")
-        nc.vector.tensor_copy(ts_sel[:], ts_pool[:].indirect(offsets[:]))
-        y_sb = held("y_sb", [P, PACK, N], F32, slot="ts_pool")
-        nc.sync.dma_start(y_sb[:], y[0].rearrange("(p t) i -> p t i", t=PACK))
-        w_scale = held("w_scale", [P, PASSES * N], U8)
-        scale_bytes = scale_pool[:].bitcast(U8)
-        for o in range(PASSES):
-            nc.vector.tensor_copy(w_scale[:, o * N : (o + 1) * N], scale_bytes[:, o * T : (o + 1) * T].indirect(offsets[:]))
 
-        x_bf = [held("x_bf0", [P, PACK * R], BF16, slot="ident"), fixed("x_bf1", [P, PACK * R], BF16, 4 * R)]
-        x_code = {
-            (0, 0): fixed("x_code00", [P, HALF], U32, 0),
-            (0, 1): fixed("x_code01", [P, HALF], U32, X1_AT),
-            (1, 0): held("x_code10", [P, HALF], U32),
-            (1, 1): held("x_code11", [P, HALF], U32),
+        xm_rows = xm[0].rearrange("(p j) d -> p j d", j=PACK)
+        xm_raw = [fixed("xm_raw0", [P, PACK, D // 2], F32, 12 * KIB), fixed("xm_raw1", [P, PACK, D // 2], F32, 20 * KIB)]
+
+        x_bf = {
+            (0, 0): held("x_bf00", [P, 2 * P * PACK], BF16),
+            (0, 1): held("x_bf01", [P, 2 * P * PACK], BF16),
+            (1, 0): held("x_bf10", [P, 2 * P * PACK], BF16),
+            (1, 1): fixed("x_bf11", [P, 2 * P * PACK], BF16, 39 * KIB),
         }
-        x_scale = [held("x_scale%d" % o, [P, R], U8) for o in range(PASSES)]
+        x_code = {key: held("x_code%d%d" % key, [P, 2 * P], U32) for key in x_bf}
+        x_scale = {key: held("x_scale%d%d" % key, [P, 2 * P], U8) for key in x_bf}
 
-        def x_views(o, lo, hi):
-            dst = x_bf[o][:].rearrange("p (t m j) -> p m t j", t=PACK, j=PACK)[:, lo:hi]
-            src = x_raw[o][:].rearrange("p j (m t) -> p m t j", t=PACK)[:, lo:hi]
-            return dst, src
+        def cast_x(o, u, raw, m0, on_vector):
+            src = raw[:].rearrange("p j (m t) -> p m t j", t=PACK)[:, :, 2 * u : 2 * u + 2, :]
+            dst = x_bf[o, u][:].rearrange("p (t m j) -> p m t j", t=2, j=PACK)[:, m0 : m0 + src.shape[1]]
+            if on_vector:
+                nc.vector.tensor_copy(dst, src)
+            else:
+                nc.scalar.copy(dst, src)
 
-        def quantise_x(o, u):
+        def quantise_x(o, u, lo, hi):
             nc.vector.quantize_mx(
-                out=x_code[o, u][:].bitcast(E4M3),
-                scales=x_scale[o][:, u * HALF : (u + 1) * HALF],
-                in_=x_bf[o][:, u * PACK * HALF : (u + 1) * PACK * HALF],
+                out=x_code[o, u][:, lo:hi].bitcast(E4M3),
+                scales=x_scale[o, u][:, lo:hi],
+                in_=x_bf[o, u][:, PACK * lo : PACK * hi],
             )
 
         scores = [psum_scores.tile([P, N], F32, name="scores%d" % t) for t in range(PACK)]
@@ -134,37 +132,36 @@ def tile_attend_gkl_w_ts_kernel(tc, xT, w_words, w_scales, y, wt, ts, xm, offs, 
             nc.tensor.matmul_mx(
                 out=scores[t][:],
                 lhsT=x_code[o, u][:, k * P : (k + 1) * P].bitcast(E4M3),
-                lhsT_scale=x_scale[o][:, t * P : (t + 1) * P],
+                lhsT_scale=x_scale[o, u][:, k * P : (k + 1) * P],
                 rhs=w_code[:, o * 2 * N : (o + 1) * 2 * N].bitcast(E2M1),
-                rhs_scale=w_scale[:, o * N : (o + 1) * N],
+                rhs_scale=w_scale[o],
                 start=(o == 0),
                 stop=(o == PASSES - 1),
             )
 
-        nc.scalar.copy(*x_views(0, 0, P))
-        quantise_x(0, 0)
-        nc.scalar.copy(*x_views(1, 0, CAST_SPLIT))
-        nc.vector.tensor_copy(*x_views(1, CAST_SPLIT, P))
-        quantise_x(1, 0)
-        quantise_x(0, 1)
-        quantise_x(1, 1)
+        for u in range(2):
+            cast_x(0, u, x_first, 0, u == 0)
+        y_sb = held("y_sb", [P, PACK, N], F32, slot="x_first")
+        nc.sync.dma_start(y_sb[:], y[0].rearrange("(p t) i -> p t i", t=PACK))
+        quantise_x(0, 0, 0, 2 * P)
+        for u in range(2):
+            cast_x(1, u, x_second[0], 0, False)
+        quantise_x(0, 1, 0, 2 * P)
+        for u in range(2):
+            cast_x(1, u, x_second[1], P // 2, u == 0)
+        for c in range(2):
+            nc.sync.dma_start(xm_raw[c][:], xm_rows[:, :, c * D // 2 : (c + 1) * D // 2])
+        quantise_x(1, 0, 0, P)
+        quantise_x(1, 0, P, 2 * P)
+        ts_sel = held("ts_sel", [P, N], F32, slot="x_bf10")
+        nc.vector.tensor_copy(ts_sel[:], ts_pool[:].indirect(offsets[:]))
+        quantise_x(1, 1, 0, 2 * P)
         for t, o in ((0, 0), (1, 0), (0, 1), (1, 1), (2, 0), (2, 1), (3, 0), (3, 1)):
             score_pass(t, o)
 
-        xm_rows = xm[0].rearrange("(p j) d -> p j d", j=PACK)
-        xm_first = held("xm_first", [P, 2, PACK, XM_COLS], F32, slot="x_raw0")
-        xm_raw = [
-            xm_first[:, 0],
-            xm_first[:, 1],
-            held("xm_raw2", [P, PACK, XM_COLS], F32, slot="ident")[:],
-            fixed("xm_raw3", [P, PACK, XM_COLS], F32, 4 * R)[:],
-        ]
-        for c in range(XM_PIECES):
-            nc.sync.dma_start(xm_raw[c], xm_rows[:, :, c * XM_COLS : (c + 1) * XM_COLS])
-
-        wt_ts = fixed("wt_ts", [P, PACK, N], F32, X1_AT + 4 * HALF)
-        for t in range(PACK):
-            nc.scalar.activation(wt_ts[:, t, :], ts_sel[:], ACT.Copy, scale=wt_sb[:, t : t + 1])
+        windows = [first_window, fixed("window1", [P, T], F32, 32 * KIB), fixed("window2", [P, T], F32, 40 * KIB)]
+        for window in windows[1:]:
+            nc.gpsimd.memset(window[:], 0.0)
 
         neg_a = [held("neg_a%d" % t, [P, N], F32) for t in range(PACK)]
         neg_max = [held("neg_max%d" % t, [P, 1], F32) for t in range(PACK)]
@@ -197,20 +194,22 @@ def tile_attend_gkl_w_ts_kernel(tc, xT, w_words, w_scales, y, wt, ts, xm, offs, 
                 invert(t + 1)
             subtract_targets(t)
 
-        xm_bf = [held("xm_bf%d" % m, [P, PACK * P], BF16, slot="neg_a%d" % m)[:] for m in range(PACK - 1)]
-        bf_rest = held("xm_bf_rest", [P, BLOCKS - PACK + 1, PACK * P], BF16, slot="neg_a3")
-        xm_bf.extend(bf_rest[:, k, :] for k in range(BLOCKS - PACK + 1))
+        wt_ts = held("wt_ts", [P, PACK, N], F32)
+        for t in range(PACK):
+            nc.scalar.activation(wt_ts[:, t, :], ts_sel[:], ACT.Copy, scale=wt_sb[:, t : t + 1])
+
+        xm_bf = [held("xm_bf%d" % m, [P, PACK * P], BF16) for m in range(BLOCKS)]
         xm_code = [held("xm_code0", [P, P], U32, slot="e1")[:]]
         xm_scale = held("xm_scale", [P, D], U8)
         for m in range(BLOCKS):
-            c, u = divmod(m, XM_COLS // P)
+            c, u = divmod(m, BLOCKS // 2)
             nc.scalar.copy(
-                xm_bf[m].rearrange("p (c i j) -> p c j i", i=4, j=PACK),
+                xm_bf[m][:].rearrange("p (c i j) -> p c j i", i=4, j=PACK),
                 xm_raw[c][:, :, u * P : (u + 1) * P].rearrange("p j (c i) -> p c j i", i=4),
             )
 
         def quantise_xm(m):
-            nc.vector.quantize_mx(out=xm_code[m].bitcast(E4M3), scales=xm_scale[:, m * P : (m + 1) * P], in_=xm_bf[m])
+            nc.vector.quantize_mx(out=xm_code[m].bitcast(E4M3), scales=xm_scale[:, m * P : (m + 1) * P], in_=xm_bf[m][:])
 
         quantise_xm(0)
 

@@ -43,32 +43,43 @@ def tile_attend_gkl_w_ts_kernel(tc, xT, w_words, w_scales, y, wt, ts, xm, offs, 
 
         offsets = keep.tile([P, N // 16], U16, name="offsets")
         nc.sync.dma_start(offsets[:], offs)
-        ts_cols = placed.tile([P, T // P], F32, name="ts_cols", offset=20 * KIB - 32)
-        nc.scalar.dma_start(ts_cols[:], ts[0:1, :].rearrange("o (p c) -> (o p) c", p=P))
-        wt_sb = held("wt_sb", [P, PACK], F32)
-        nc.scalar.dma_start(wt_sb[:], wt[0].rearrange("(p t) o -> p (t o)", t=PACK))
-
+        scale_pool = fixed("scale_pool", [P, T // 4], I32, 19 * KIB)
+        nc.sync.dma_start(scale_pool[0:32, :], w_scales.rearrange("o f t -> (o f) t").bitcast(I32))
+        nc.vector.memset(scale_pool[32:64, :], 0)
+        nc.vector.memset(scale_pool[64:128, :], 0)
+        ts_cols = held("ts_cols", [P, T // P], F32)
+        nc.sync.dma_start(ts_cols[:], ts[0:1, :].rearrange("o (p c) -> (o p) c", p=P))
         word_pool = held("word_pool", [P, T], I32)
         nc.sync.dma_start(word_pool[:], w_words[0].rearrange("p t b -> p (t b)").bitcast(I32))
-
-        scale_pool = held("scale_pool", [P, T // 4], I32)
-        nc.gpsimd.memset(scale_pool[:], 0)
-        scale_rows = w_scales.bitcast(I32)
-        for q in range(4):
-            nc.sync.dma_start(scale_pool[32 * q : 32 * q + 8, :], scale_rows[:, 4 * q : 4 * q + 4, :])
-
-        zeros = held("zeros", [P, P], F32, slot="x_first")
-        nc.gpsimd.memset(zeros[:], 0.0)
-        ident = held("ident", [P, P], F32)
-        nc.gpsimd.affine_select(
-            out=ident[:], in_=zeros[:], compare_op=ALU.not_equal, fill=1.0, base=0, pattern=[[-1, P]], channel_multiplier=1
-        )
         x_rows = [xT[0, 512 * o : 512 * (o + 1), :].rearrange("(p j) r -> p j r", j=PACK) for o in range(PASSES)]
         x_first = held("x_first", [P, PACK, R], F32)
         nc.sync.dma_start(x_first[:], x_rows[0])
 
-        first_window = held("window0", [P, T], F32)
-        nc.vector.memset(first_window[:], 0.0)
+        ident = held("ident", [P, P], F32)
+        zeros = fixed("zeros", [P, P], F32, 8 * KIB - 256)
+        nc.gpsimd.memset(zeros[:], 0.0)
+        nc.gpsimd.affine_select(
+            out=ident[:], in_=zeros[:], compare_op=ALU.not_equal, fill=1.0, base=0, pattern=[[-1, P]], channel_multiplier=1
+        )
+        plane_first = held("plane_first", [P, N // 4], I32)
+        nc.vector.memset(plane_first[:], 0)
+        first_window = fixed("window0", [P, T], F32, 0)
+        nc.gpsimd.memset(first_window[:], 0.0)
+        plane_second = fixed("plane_second", [P, N // 4], I32, 8 * KIB)
+        nc.gpsimd.memset(plane_second[:], 0)
+
+        scale_sel = held("scale_sel", [P, N], U8)
+        nc.vector.tensor_copy(scale_sel[:], scale_pool[:].bitcast(U8).indirect(offsets[:]))
+
+        def place_scales(plane, o):
+            for q in range(4):
+                row = 16 * o + 4 * q
+                nc.sync.dma_start(plane[32 * q : 32 * q + 4, :], scale_sel[:].bitcast(I32)[row : row + 4, :])
+
+        place_scales(plane_first, 0)
+        x_second = [fixed("x_second0", [P, PACK, HALF], F32, 16 * KIB), fixed("x_second1", [P, PACK, HALF], F32, 20 * KIB)]
+        for h in range(2):
+            nc.sync.dma_start(x_second[h][:], x_rows[1][:, :, h * HALF : (h + 1) * HALF])
 
         ts_pool = held("ts_pool", [P, T], F32)
         ts_view = ts_pool[:].rearrange("m (p c) -> m p c", p=P)
@@ -78,19 +89,13 @@ def tile_attend_gkl_w_ts_kernel(tc, xT, w_words, w_scales, y, wt, ts, xm, offs, 
                 c = PACK * b + k
                 nc.tensor.transpose(bank[:, k, :], ts_cols[:, c : c + 1].to_broadcast([P, P]), ident[:])
             nc.scalar.copy(ts_view[:, :, PACK * b : PACK * (b + 1)], bank[:].rearrange("m k p -> m p k"))
-        x_second = [fixed("x_second0", [P, PACK, HALF], F32, 16 * KIB), fixed("x_second1", [P, PACK, HALF], F32, 20 * KIB)]
-        for h in range(2):
-            nc.sync.dma_start(x_second[h][:], x_rows[1][:, :, h * HALF : (h + 1) * HALF])
 
         w_pair = held("w_pair", [P, N], U32)
         nc.vector.tensor_copy(w_pair[:], word_pool[:].bitcast(U32).indirect(offsets[:]))
-        w_scale_both = held("w_scale_both", [P, N], U8)
-        nc.vector.tensor_copy(w_scale_both[:], scale_pool[:].bitcast(U8).indirect(offsets[:]))
-        w_scale_second = held("w_scale_second", [P, N // 4], I32, slot="ident")
-        nc.vector.memset(w_scale_second[:], 0)
-        for q in range(4):
-            nc.sync.dma_start(w_scale_second[32 * q : 32 * q + 4, :], w_scale_both[:].bitcast(I32)[32 * q + 4 : 32 * q + 8, :])
-        w_scale = [w_scale_both[:], w_scale_second[:].bitcast(U8)]
+        place_scales(plane_second, 1)
+        w_scale = [plane_first[:].bitcast(U8), plane_second[:].bitcast(U8)]
+        wt_sb = held("wt_sb", [P, PACK], F32, slot="scale_sel")
+        nc.sync.dma_start(wt_sb[:], wt[0].rearrange("(p t) o -> p (t o)", t=PACK))
 
         w_code = held("w_code", [P, PASSES * 2 * N], U8)
         nc.vector.tensor_copy(
@@ -98,12 +103,15 @@ def tile_attend_gkl_w_ts_kernel(tc, xT, w_words, w_scales, y, wt, ts, xm, offs, 
             w_pair[:].bitcast(U16).rearrange("p (i o) -> p o i", o=PASSES),
         )
 
+        ts_sel = held("ts_sel", [P, N], F32)
+        nc.vector.tensor_copy(ts_sel[:], ts_pool[:].indirect(offsets[:]))
+
         xm_rows = xm[0].rearrange("(p j) d -> p j d", j=PACK)
         xm_raw = [fixed("xm_raw0", [P, PACK, D // 2], F32, 12 * KIB), fixed("xm_raw1", [P, PACK, D // 2], F32, 20 * KIB)]
 
         x_bf = {
             (0, 0): held("x_bf00", [P, 2 * P * PACK], BF16),
-            (0, 1): held("x_bf01", [P, 2 * P * PACK], BF16),
+            (0, 1): held("x_bf01", [P, 2 * P * PACK], BF16, slot="ts_cols"),
             (1, 0): held("x_bf10", [P, 2 * P * PACK], BF16),
             (1, 1): fixed("x_bf11", [P, 2 * P * PACK], BF16, 39 * KIB),
         }
@@ -153,8 +161,6 @@ def tile_attend_gkl_w_ts_kernel(tc, xT, w_words, w_scales, y, wt, ts, xm, offs, 
             nc.sync.dma_start(xm_raw[c][:], xm_rows[:, :, c * D // 2 : (c + 1) * D // 2])
         quantise_x(1, 0, 0, P)
         quantise_x(1, 0, P, 2 * P)
-        ts_sel = held("ts_sel", [P, N], F32, slot="x_bf10")
-        nc.vector.tensor_copy(ts_sel[:], ts_pool[:].indirect(offsets[:]))
         quantise_x(1, 1, 0, 2 * P)
         for t, o in ((0, 0), (1, 0), (0, 1), (1, 1), (2, 0), (2, 1), (3, 0), (3, 1)):
             score_pass(t, o)
@@ -166,8 +172,8 @@ def tile_attend_gkl_w_ts_kernel(tc, xT, w_words, w_scales, y, wt, ts, xm, offs, 
         neg_a = [held("neg_a%d" % t, [P, N], F32) for t in range(PACK)]
         neg_max = [held("neg_max%d" % t, [P, 1], F32) for t in range(PACK)]
         e = [held("e%d" % t, [P, N], F32) for t in range(PACK)]
-        total = [held("total%d" % t, [P, 1], F32) for t in range(PACK)]
-        inv = [held("inv%d" % t, [P, 1], F32) for t in range(PACK)]
+        total = held("total", [P, PACK], F32)
+        inv = held("inv", [P, PACK], F32)
         g = held("g", [P, PACK, N], F32)
 
         def scale_scores(t):
@@ -175,43 +181,50 @@ def tile_attend_gkl_w_ts_kernel(tc, xT, w_words, w_scales, y, wt, ts, xm, offs, 
 
         def exponentiate(t):
             nc.vector.tensor_reduce(neg_max[t][:], neg_a[t][:], mybir.AxisListType.X, ALU.min)
-            nc.scalar.activation(e[t][:], neg_a[t][:], ACT.Exp, bias=neg_max[t][:], scale=-1.0, accum_out=total[t][:])
+            nc.scalar.activation(e[t][:], neg_a[t][:], ACT.Exp, bias=neg_max[t][:], scale=-1.0, accum_out=total[:, t : t + 1])
 
-        def invert(t):
-            nc.vector.reciprocal(inv[t][:], total[t][:])
+        def invert(lo, hi):
+            nc.vector.reciprocal(inv[:, lo:hi], total[:, lo:hi])
 
         def subtract_targets(t):
-            nc.vector.scalar_tensor_tensor(g[:, t, :], e[t][:], inv[t][:], y_sb[:, t, :], ALU.mult, ALU.subtract)
+            nc.vector.scalar_tensor_tensor(g[:, t, :], e[t][:], inv[:, t : t + 1], y_sb[:, t, :], ALU.mult, ALU.subtract)
 
         scale_scores(0)
         for t in range(PACK):
             if t + 1 < PACK:
                 scale_scores(t + 1)
+            if t == PACK - 1:
+                invert(0, 2)
             exponentiate(t)
-        invert(0)
-        for t in range(PACK):
-            if t + 1 < PACK:
-                invert(t + 1)
-            subtract_targets(t)
+        subtract_targets(0)
+        subtract_targets(1)
+        invert(2, PACK)
+        subtract_targets(2)
+        subtract_targets(3)
 
         wt_ts = held("wt_ts", [P, PACK, N], F32)
         for t in range(PACK):
             nc.scalar.activation(wt_ts[:, t, :], ts_sel[:], ACT.Copy, scale=wt_sb[:, t : t + 1])
 
-        xm_bf = [held("xm_bf%d" % m, [P, PACK * P], BF16) for m in range(BLOCKS)]
-        xm_code = [held("xm_code0", [P, P], U32, slot="e1")[:]]
+        xm_bf = [held("xm_bf%d" % c, [P, PACK * D // 2], BF16) for c in range(2)]
+        code_first = held("xm_code0", [P, P], U32, slot="e1")
         xm_scale = held("xm_scale", [P, D], U8)
         for m in range(BLOCKS):
             c, u = divmod(m, BLOCKS // 2)
             nc.scalar.copy(
-                xm_bf[m][:].rearrange("p (c i j) -> p c j i", i=4, j=PACK),
+                xm_bf[c][:, u * PACK * P : (u + 1) * PACK * P].rearrange("p (c i j) -> p c j i", i=4, j=PACK),
                 xm_raw[c][:, :, u * P : (u + 1) * P].rearrange("p j (c i) -> p c j i", i=4),
             )
 
-        def quantise_xm(m):
-            nc.vector.quantize_mx(out=xm_code[m].bitcast(E4M3), scales=xm_scale[:, m * P : (m + 1) * P], in_=xm_bf[m][:])
+        def quantise_xm(code, lo, hi):
+            c, u = divmod(lo, BLOCKS // 2)
+            nc.vector.quantize_mx(
+                out=code.bitcast(E4M3),
+                scales=xm_scale[:, lo * P : hi * P],
+                in_=xm_bf[c][:, u * PACK * P : (u + hi - lo) * PACK * P],
+            )
 
-        quantise_xm(0)
+        quantise_xm(code_first[:], 0, 1)
 
         h_bf = held("h_bf", [P, N, PACK], BF16)
         h_code = held("h_code", [P, N], U32)
@@ -230,9 +243,9 @@ def tile_attend_gkl_w_ts_kernel(tc, xT, w_words, w_scales, y, wt, ts, xm, offs, 
             )
 
         code_rest = held("xm_code_rest", [P, D - P], U32, slot="h_bf")
-        xm_code.extend(code_rest[:, k * P : (k + 1) * P] for k in range(BLOCKS - 1))
-        for m in range(1, BLOCKS):
-            quantise_xm(m)
+        xm_code = [code_first[:]] + [code_rest[:, k * P : (k + 1) * P] for k in range(BLOCKS - 1)]
+        for lo, hi in ((1, 2), (2, 4), (4, 8)):
+            quantise_xm(code_rest[:, (lo - 1) * P : (hi - 1) * P], lo, hi)
 
         for m in range(BLOCKS):
             bank = psum_ring.tile([P, N], F32, name="bank")
@@ -246,7 +259,11 @@ def tile_attend_gkl_w_ts_kernel(tc, xT, w_words, w_scales, y, wt, ts, xm, offs, 
                 stop=True,
             )
             dw = ring.tile([P, N], F32, name="dw")
-            nc.scalar.copy(dw[:], bank[:])
             window = windows[m % WINDOWS]
-            nc.vector.tensor_copy(window[:].indirect(offsets[:]), dw[:])
+            pieces = 2 if m == 0 else 1
+            width = N // pieces
+            for k in range(pieces):
+                nc.scalar.copy(dw[:, k * width : (k + 1) * width], bank[:, k * width : (k + 1) * width])
+                listed = offsets[:, k * width // 16 : (k + 1) * width // 16]
+                nc.vector.tensor_copy(window[:].indirect(listed), dw[:, k * width : (k + 1) * width])
             nc.sync.dma_start(out[m * P : (m + 1) * P, :], window[:])

@@ -21,7 +21,7 @@ P = 128
 PACK = 4
 PASSES = D // (P * PACK)
 BLOCKS = D // P
-WINDOWS = 3
+WINDOWS = 4
 HALF = R // 2
 KIB = 1024
 
@@ -52,21 +52,21 @@ def tile_attend_gkl_w_ts_kernel(tc, xT, w_words, w_scales, y, wt, ts, xm, offs, 
         word_pool = held("word_pool", [P, T], I32)
         nc.sync.dma_start(word_pool[:], w_words[0].rearrange("p t b -> p (t b)").bitcast(I32))
         x_rows = [xT[0, 512 * o : 512 * (o + 1), :].rearrange("(p j) r -> p j r", j=PACK) for o in range(PASSES)]
-        x_first = held("x_first", [P, PACK, R], F32)
+        x_first = fixed("x_first", [P, PACK, R], F32, 68 * KIB)
         nc.sync.dma_start(x_first[:], x_rows[0])
+        wt_sb = held("wt_sb", [P, PACK], F32)
+        nc.sync.dma_start(wt_sb[:], wt[0].rearrange("(p t) o -> p (t o)", t=PACK))
 
         ident = held("ident", [P, P], F32)
-        zeros = fixed("zeros", [P, P], F32, 8 * KIB - 256)
+        zeros = held("zeros", [P, P], F32, slot="window0")
         nc.gpsimd.memset(zeros[:], 0.0)
         nc.gpsimd.affine_select(
             out=ident[:], in_=zeros[:], compare_op=ALU.not_equal, fill=1.0, base=0, pattern=[[-1, P]], channel_multiplier=1
         )
         plane_first = held("plane_first", [P, N // 4], I32)
         nc.vector.memset(plane_first[:], 0)
-        first_window = fixed("window0", [P, T], F32, 0)
+        first_window = held("window0", [P, T], F32)
         nc.gpsimd.memset(first_window[:], 0.0)
-        plane_second = fixed("plane_second", [P, N // 4], I32, 8 * KIB)
-        nc.gpsimd.memset(plane_second[:], 0)
 
         scale_sel = held("scale_sel", [P, N], U8)
         nc.vector.tensor_copy(scale_sel[:], scale_pool[:].bitcast(U8).indirect(offsets[:]))
@@ -92,10 +92,10 @@ def tile_attend_gkl_w_ts_kernel(tc, xT, w_words, w_scales, y, wt, ts, xm, offs, 
 
         w_pair = held("w_pair", [P, N], U32)
         nc.vector.tensor_copy(w_pair[:], word_pool[:].bitcast(U32).indirect(offsets[:]))
+        plane_second = held("plane_second", [P, N // 4], I32, slot="word_pool")
+        nc.vector.memset(plane_second[:], 0)
         place_scales(plane_second, 1)
         w_scale = [plane_first[:].bitcast(U8), plane_second[:].bitcast(U8)]
-        wt_sb = held("wt_sb", [P, PACK], F32, slot="scale_sel")
-        nc.sync.dma_start(wt_sb[:], wt[0].rearrange("(p t) o -> p (t o)", t=PACK))
 
         w_code = held("w_code", [P, PASSES * 2 * N], U8)
         nc.vector.tensor_copy(
@@ -107,7 +107,7 @@ def tile_attend_gkl_w_ts_kernel(tc, xT, w_words, w_scales, y, wt, ts, xm, offs, 
         nc.vector.tensor_copy(ts_sel[:], ts_pool[:].indirect(offsets[:]))
 
         xm_rows = xm[0].rearrange("(p j) d -> p j d", j=PACK)
-        xm_raw = [fixed("xm_raw0", [P, PACK, D // 2], F32, 12 * KIB), fixed("xm_raw1", [P, PACK, D // 2], F32, 20 * KIB)]
+        xm_raw = [fixed("xm_raw0", [P, PACK, D // 2], F32, 72 * KIB), fixed("xm_raw1", [P, PACK, D // 2], F32, 12 * KIB)]
 
         x_bf = {
             (0, 0): held("x_bf00", [P, 2 * P * PACK], BF16),
@@ -149,7 +149,8 @@ def tile_attend_gkl_w_ts_kernel(tc, xT, w_words, w_scales, y, wt, ts, xm, offs, 
 
         for u in range(2):
             cast_x(0, u, x_first, 0, u == 0)
-        y_sb = held("y_sb", [P, PACK, N], F32, slot="x_first")
+        y_sb = fixed("y_sb", [P, PACK, N], F32, 64 * KIB)
+        nc.sync.dma_start(xm_raw[0][:], xm_rows[:, :, : D // 2])
         nc.sync.dma_start(y_sb[:], y[0].rearrange("(p t) i -> p t i", t=PACK))
         quantise_x(0, 0, 0, 2 * P)
         for u in range(2):
@@ -157,19 +158,21 @@ def tile_attend_gkl_w_ts_kernel(tc, xT, w_words, w_scales, y, wt, ts, xm, offs, 
         quantise_x(0, 1, 0, 2 * P)
         for u in range(2):
             cast_x(1, u, x_second[1], P // 2, u == 0)
-        for c in range(2):
-            nc.sync.dma_start(xm_raw[c][:], xm_rows[:, :, c * D // 2 : (c + 1) * D // 2])
+        nc.sync.dma_start(xm_raw[1][:], xm_rows[:, :, D // 2 :])
         quantise_x(1, 0, 0, P)
         quantise_x(1, 0, P, 2 * P)
         quantise_x(1, 1, 0, 2 * P)
         for t, o in ((0, 0), (1, 0), (0, 1), (1, 1), (2, 0), (2, 1), (3, 0), (3, 1)):
             score_pass(t, o)
 
-        windows = [first_window, fixed("window1", [P, T], F32, 32 * KIB), fixed("window2", [P, T], F32, 40 * KIB)]
-        for window in windows[1:]:
-            nc.gpsimd.memset(window[:], 0.0)
+        second_window = fixed("window1", [P, T], F32, 40 * KIB)
+        nc.gpsimd.memset(second_window[:], 0.0)
 
-        neg_a = [held("neg_a%d" % t, [P, N], F32) for t in range(PACK)]
+        wt_ts = fixed("wt_ts", [P, PACK, N], F32, 20 * KIB)
+        for t in range(PACK):
+            nc.scalar.activation(wt_ts[:, t, :], ts_sel[:], ACT.Copy, scale=wt_sb[:, t : t + 1])
+
+        neg_a = [held("neg_a%d" % t, [P, N], F32) for t in range(PACK - 1)] + [fixed("neg_a3", [P, N], F32, 55 * KIB)]
         neg_max = [held("neg_max%d" % t, [P, 1], F32) for t in range(PACK)]
         e = [held("e%d" % t, [P, N], F32) for t in range(PACK)]
         total = held("total", [P, PACK], F32)
@@ -193,38 +196,37 @@ def tile_attend_gkl_w_ts_kernel(tc, xT, w_words, w_scales, y, wt, ts, xm, offs, 
         for t in range(PACK):
             if t + 1 < PACK:
                 scale_scores(t + 1)
-            if t == PACK - 1:
+            else:
                 invert(0, 2)
             exponentiate(t)
         subtract_targets(0)
         subtract_targets(1)
         invert(2, PACK)
-        subtract_targets(2)
-        subtract_targets(3)
 
-        wt_ts = held("wt_ts", [P, PACK, N], F32)
-        for t in range(PACK):
-            nc.scalar.activation(wt_ts[:, t, :], ts_sel[:], ACT.Copy, scale=wt_sb[:, t : t + 1])
-
-        xm_bf = [held("xm_bf%d" % c, [P, PACK * D // 2], BF16) for c in range(2)]
+        groups = ((0, 1), (1, 2), (2, 4), (4, 8))
+        xm_bf = [
+            held("xm_bf0", [P, PACK * P], BF16, slot="neg_a0"),
+            fixed("xm_bf1", [P, PACK * P], BF16, 54 * KIB + 512),
+            held("xm_bf2", [P, 2 * PACK * P], BF16, slot="neg_max3"),
+            fixed("xm_bf3", [P, PACK * PACK * P], BF16, 55 * KIB + 512),
+        ]
         code_first = held("xm_code0", [P, P], U32, slot="e1")
         xm_scale = held("xm_scale", [P, D], U8)
-        for m in range(BLOCKS):
-            c, u = divmod(m, BLOCKS // 2)
-            nc.scalar.copy(
-                xm_bf[c][:, u * PACK * P : (u + 1) * PACK * P].rearrange("p (c i j) -> p c j i", i=4, j=PACK),
-                xm_raw[c][:, :, u * P : (u + 1) * P].rearrange("p j (c i) -> p c j i", i=4),
-            )
+        for k, (lo, hi) in enumerate(groups):
+            for m in range(lo, hi):
+                c, u = divmod(m, BLOCKS // 2)
+                nc.scalar.copy(
+                    xm_bf[k][:, (m - lo) * PACK * P : (m - lo + 1) * PACK * P].rearrange("p (c i j) -> p c j i", i=4, j=PACK),
+                    xm_raw[c][:, :, u * P : (u + 1) * P].rearrange("p j (c i) -> p c j i", i=4),
+                )
 
-        def quantise_xm(code, lo, hi):
-            c, u = divmod(lo, BLOCKS // 2)
-            nc.vector.quantize_mx(
-                out=code.bitcast(E4M3),
-                scales=xm_scale[:, lo * P : hi * P],
-                in_=xm_bf[c][:, u * PACK * P : (u + hi - lo) * PACK * P],
-            )
+        def quantise_xm(code, k):
+            lo, hi = groups[k]
+            nc.vector.quantize_mx(out=code.bitcast(E4M3), scales=xm_scale[:, lo * P : hi * P], in_=xm_bf[k][:])
 
-        quantise_xm(code_first[:], 0, 1)
+        quantise_xm(code_first[:], 0)
+        subtract_targets(2)
+        subtract_targets(3)
 
         h_bf = held("h_bf", [P, N, PACK], BF16)
         h_code = held("h_code", [P, N], U32)
@@ -244,8 +246,12 @@ def tile_attend_gkl_w_ts_kernel(tc, xT, w_words, w_scales, y, wt, ts, xm, offs, 
 
         code_rest = held("xm_code_rest", [P, D - P], U32, slot="h_bf")
         xm_code = [code_first[:]] + [code_rest[:, k * P : (k + 1) * P] for k in range(BLOCKS - 1)]
-        for lo, hi in ((1, 2), (2, 4), (4, 8)):
-            quantise_xm(code_rest[:, (lo - 1) * P : (hi - 1) * P], lo, hi)
+        for k in range(1, len(groups)):
+            lo, hi = groups[k]
+            quantise_xm(code_rest[:, (lo - 1) * P : (hi - 1) * P], k)
+        windows = [first_window, second_window, fixed("window2", [P, T], F32, 48 * KIB), fixed("window3", [P, T], F32, 56 * KIB)]
+        for window in windows[2:]:
+            nc.gpsimd.memset(window[:], 0.0)
 
         for m in range(BLOCKS):
             bank = psum_ring.tile([P, N], F32, name="bank")

@@ -113,9 +113,9 @@ def tile_attend_gkl_w_ts_kernel(tc, xT, w_words, w_scales, y, wt, ts, xm, offs, 
             (0, 0): held("x_bf00", [P, 2 * P * PACK], BF16),
             (0, 1): held("x_bf01", [P, 2 * P * PACK], BF16, slot="ts_cols"),
             (1, 0): held("x_bf10", [P, 2 * P * PACK], BF16),
-            (1, 1): fixed("x_bf11", [P, 2 * P * PACK], BF16, 39 * KIB),
+            (1, 1): held("x_bf11", [P, 2 * P * PACK], BF16),
         }
-        x_code = {key: held("x_code%d%d" % key, [P, 2 * P], U32) for key in x_bf}
+        x_code = {key: held("x_code%d%d" % key, [P, 2 * P], U32, slot="window1" if key == (1, 1) else None) for key in x_bf}
         x_scale = {key: held("x_scale%d%d" % key, [P, 2 * P], U8) for key in x_bf}
 
         def cast_x(o, u, raw, m0, on_vector):
@@ -165,12 +165,14 @@ def tile_attend_gkl_w_ts_kernel(tc, xT, w_words, w_scales, y, wt, ts, xm, offs, 
         for t, o in ((0, 0), (1, 0), (0, 1), (1, 1), (2, 0), (2, 1), (3, 0), (3, 1)):
             score_pass(t, o)
 
-        second_window = fixed("window1", [P, T], F32, 40 * KIB)
+        second_window = held("window1", [P, T], F32)
         nc.gpsimd.memset(second_window[:], 0.0)
 
         wt_ts = fixed("wt_ts", [P, PACK, N], F32, 20 * KIB)
-        for t in range(PACK):
+        for t in range(2):
             nc.scalar.activation(wt_ts[:, t, :], ts_sel[:], ACT.Copy, scale=wt_sb[:, t : t + 1])
+        for t in range(2, PACK):
+            nc.vector.tensor_scalar(wt_ts[:, t, :], ts_sel[:], wt_sb[:, t : t + 1], None, ALU.mult)
 
         neg_a = [held("neg_a%d" % t, [P, N], F32) for t in range(PACK - 1)] + [fixed("neg_a3", [P, N], F32, 55 * KIB)]
         neg_max = [held("neg_max%d" % t, [P, 1], F32) for t in range(PACK)]
@@ -189,8 +191,8 @@ def tile_attend_gkl_w_ts_kernel(tc, xT, w_words, w_scales, y, wt, ts, xm, offs, 
         def invert(lo, hi):
             nc.vector.reciprocal(inv[:, lo:hi], total[:, lo:hi])
 
-        def subtract_targets(t):
-            nc.vector.scalar_tensor_tensor(g[:, t, :], e[t][:], inv[:, t : t + 1], y_sb[:, t, :], ALU.mult, ALU.subtract)
+        def subtract_targets(t, s=slice(0, N)):
+            nc.vector.scalar_tensor_tensor(g[:, t, s], e[t][:, s], inv[:, t : t + 1], y_sb[:, t, s], ALU.mult, ALU.subtract)
 
         scale_scores(0)
         for t in range(PACK):
@@ -200,15 +202,17 @@ def tile_attend_gkl_w_ts_kernel(tc, xT, w_words, w_scales, y, wt, ts, xm, offs, 
                 invert(0, 2)
             exponentiate(t)
         subtract_targets(0)
+        invert(2, 3)
         subtract_targets(1)
-        invert(2, PACK)
+        invert(3, PACK)
 
-        groups = ((0, 1), (1, 2), (2, 4), (4, 8))
+        groups = ((0, 1), (1, 2), (2, 3), (3, 4), (4, 8))
         xm_bf = [
-            held("xm_bf0", [P, PACK * P], BF16, slot="neg_a0"),
-            fixed("xm_bf1", [P, PACK * P], BF16, 54 * KIB + 512),
-            held("xm_bf2", [P, 2 * PACK * P], BF16, slot="neg_max3"),
-            fixed("xm_bf3", [P, PACK * PACK * P], BF16, 55 * KIB + 512),
+            held("xm_bf0", [P, PACK * P], BF16),
+            held("xm_bf1", [P, PACK * P], BF16),
+            held("xm_bf2", [P, PACK * P], BF16, slot="neg_a0"),
+            held("xm_bf3", [P, PACK * P], BF16, slot="neg_max3"),
+            fixed("xm_bf4", [P, PACK * PACK * P], BF16, 55 * KIB + 512),
         ]
         code_first = held("xm_code0", [P, P], U32, slot="e1")
         xm_scale = held("xm_scale", [P, D], U8)
@@ -224,14 +228,15 @@ def tile_attend_gkl_w_ts_kernel(tc, xT, w_words, w_scales, y, wt, ts, xm, offs, 
             lo, hi = groups[k]
             nc.vector.quantize_mx(out=code.bitcast(E4M3), scales=xm_scale[:, lo * P : hi * P], in_=xm_bf[k][:])
 
-        quantise_xm(code_first[:], 0)
+        halves = [slice(0, N // 2), slice(N // 2, N)]
         subtract_targets(2)
-        subtract_targets(3)
+        quantise_xm(code_first[:], 0)
+        for s in halves:
+            subtract_targets(3, s)
 
         h_bf = held("h_bf", [P, N, PACK], BF16)
         h_code = held("h_code", [P, N], U32)
         h_scale = held("h_scale", [P, N], U8)
-        halves = [slice(0, N // 2), slice(N // 2, N)]
         for s in halves:
             nc.vector.tensor_tensor(
                 h_bf[:, s, :].rearrange("p (c i) t -> p c t i", i=2),

@@ -24,6 +24,7 @@ BLOCKS = D // P
 WINDOWS = 4
 HALF = R // 2
 KIB = 1024
+ASIDE = 384
 
 
 def tile_attend_gkl_w_ts_kernel(tc, xT, w_words, w_scales, y, wt, ts, xm, offs, out):
@@ -115,12 +116,12 @@ def tile_attend_gkl_w_ts_kernel(tc, xT, w_words, w_scales, y, wt, ts, xm, offs, 
             (1, 0): held("x_bf10", [P, 2 * P * PACK], BF16),
             (1, 1): held("x_bf11", [P, 2 * P * PACK], BF16),
         }
-        x_code = {key: held("x_code%d%d" % key, [P, 2 * P], U32, slot="window1" if key == (1, 1) else None) for key in x_bf}
+        x_code = {key: held("x_code%d%d" % key, [P, 2 * P], U32) for key in x_bf}
         x_scale = {key: held("x_scale%d%d" % key, [P, 2 * P], U8) for key in x_bf}
 
         def cast_x(o, u, raw, m0, on_vector):
-            src = raw[:].rearrange("p j (m t) -> p m t j", t=PACK)[:, :, 2 * u : 2 * u + 2, :]
-            dst = x_bf[o, u][:].rearrange("p (t m j) -> p m t j", t=2, j=PACK)[:, m0 : m0 + src.shape[1]]
+            src = raw[:].rearrange("p j (m t) -> p m j t", t=PACK)[:, :, :, 2 * u : 2 * u + 2]
+            dst = x_bf[o, u][:].rearrange("p (t m j) -> p m j t", t=2, j=PACK)[:, m0 : m0 + src.shape[1]]
             if on_vector:
                 nc.vector.tensor_copy(dst, src)
             else:
@@ -165,14 +166,9 @@ def tile_attend_gkl_w_ts_kernel(tc, xT, w_words, w_scales, y, wt, ts, xm, offs, 
         for t, o in ((0, 0), (1, 0), (0, 1), (1, 1), (2, 0), (2, 1), (3, 0), (3, 1)):
             score_pass(t, o)
 
-        second_window = held("window1", [P, T], F32)
-        nc.gpsimd.memset(second_window[:], 0.0)
-
         wt_ts = fixed("wt_ts", [P, PACK, N], F32, 20 * KIB)
-        for t in range(2):
+        for t in range(PACK):
             nc.scalar.activation(wt_ts[:, t, :], ts_sel[:], ACT.Copy, scale=wt_sb[:, t : t + 1])
-        for t in range(2, PACK):
-            nc.vector.tensor_scalar(wt_ts[:, t, :], ts_sel[:], wt_sb[:, t : t + 1], None, ALU.mult)
 
         neg_a = [held("neg_a%d" % t, [P, N], F32) for t in range(PACK - 1)] + [fixed("neg_a3", [P, N], F32, 55 * KIB)]
         neg_max = [held("neg_max%d" % t, [P, 1], F32) for t in range(PACK)]
@@ -194,25 +190,33 @@ def tile_attend_gkl_w_ts_kernel(tc, xT, w_words, w_scales, y, wt, ts, xm, offs, 
         def subtract_targets(t, s=slice(0, N)):
             nc.vector.scalar_tensor_tensor(g[:, t, s], e[t][:, s], inv[:, t : t + 1], y_sb[:, t, s], ALU.mult, ALU.subtract)
 
+        minus_one = held("minus_one", [P, 1], F32)
+        nc.gpsimd.memset(minus_one[:], -1.0)
         scale_scores(0)
         for t in range(PACK):
             if t + 1 < PACK:
                 scale_scores(t + 1)
             else:
-                invert(0, 2)
+                invert(1, 2)
             exponentiate(t)
-        subtract_targets(0)
-        invert(2, 3)
+            if t == 0:
+                inv_first = held("inv_first", [P, 1], F32)
+                nc.gpsimd.tensor_tensor(inv_first[:], total[:, 0:1], minus_one[:], ALU.pow)
+                share = held("share", [P, ASIDE], F32, slot="window1")
+                nc.gpsimd.tensor_scalar(share[:], e[0][:, :ASIDE], inv_first[:], 0.0, ALU.mult, ALU.add)
+                nc.gpsimd.tensor_tensor(g[:, 0, :ASIDE], share[:], y_sb[:, 0, :ASIDE], ALU.subtract)
+                second_window = held("window1", [P, T], F32)
+                nc.gpsimd.memset(second_window[:], 0.0)
         subtract_targets(1)
-        invert(3, PACK)
+        invert(2, 3)
+        nc.vector.scalar_tensor_tensor(g[:, 0, ASIDE:], e[0][:, ASIDE:], inv_first[:], y_sb[:, 0, ASIDE:], ALU.mult, ALU.subtract)
 
-        groups = ((0, 1), (1, 2), (2, 3), (3, 4), (4, 8))
+        groups = ((0, 1), (1, 2), (2, 4), (4, 8))
         xm_bf = [
-            held("xm_bf0", [P, PACK * P], BF16),
-            held("xm_bf1", [P, PACK * P], BF16),
-            held("xm_bf2", [P, PACK * P], BF16, slot="neg_a0"),
-            held("xm_bf3", [P, PACK * P], BF16, slot="neg_max3"),
-            fixed("xm_bf4", [P, PACK * PACK * P], BF16, 55 * KIB + 512),
+            held("xm_bf0", [P, PACK * P], BF16, slot="neg_a0"),
+            fixed("xm_bf1", [P, PACK * P], BF16, 54 * KIB + 512),
+            held("xm_bf2", [P, 2 * PACK * P], BF16, slot="neg_max3"),
+            fixed("xm_bf3", [P, PACK * PACK * P], BF16, 55 * KIB + 512),
         ]
         code_first = held("xm_code0", [P, P], U32, slot="e1")
         xm_scale = held("xm_scale", [P, D], U8)
@@ -229,8 +233,10 @@ def tile_attend_gkl_w_ts_kernel(tc, xT, w_words, w_scales, y, wt, ts, xm, offs, 
             nc.vector.quantize_mx(out=code.bitcast(E4M3), scales=xm_scale[:, lo * P : hi * P], in_=xm_bf[k][:])
 
         halves = [slice(0, N // 2), slice(N // 2, N)]
-        subtract_targets(2)
         quantise_xm(code_first[:], 0)
+        subtract_targets(2, halves[0])
+        invert(3, PACK)
+        subtract_targets(2, halves[1])
         for s in halves:
             subtract_targets(3, s)
 

@@ -21,8 +21,8 @@ P = 128
 PACK = 4
 PASSES = D // (P * PACK)
 BLOCKS = D // P
-WINDOWS = 4
-HALF = R // 2
+WINDOWS = 3
+CAST_SPLIT = 96
 KIB = 1024
 ASIDE = 384
 
@@ -44,7 +44,7 @@ def tile_attend_gkl_w_ts_kernel(tc, xT, w_words, w_scales, y, wt, ts, xm, offs, 
 
         offsets = keep.tile([P, N // 16], U16, name="offsets")
         nc.sync.dma_start(offsets[:], offs)
-        scale_pool = fixed("scale_pool", [P, T // 4], I32, 19 * KIB)
+        scale_pool = fixed("scale_pool", [P, T // 4], I32, 23 * KIB)
         nc.sync.dma_start(scale_pool[0:32, :], w_scales.rearrange("o f t -> (o f) t").bitcast(I32))
         nc.vector.memset(scale_pool[32:64, :], 0)
         nc.vector.memset(scale_pool[64:128, :], 0)
@@ -55,8 +55,6 @@ def tile_attend_gkl_w_ts_kernel(tc, xT, w_words, w_scales, y, wt, ts, xm, offs, 
         x_rows = [xT[0, 512 * o : 512 * (o + 1), :].rearrange("(p j) r -> p j r", j=PACK) for o in range(PASSES)]
         x_first = fixed("x_first", [P, PACK, R], F32, 68 * KIB)
         nc.sync.dma_start(x_first[:], x_rows[0])
-        wt_sb = held("wt_sb", [P, PACK], F32)
-        nc.sync.dma_start(wt_sb[:], wt[0].rearrange("(p t) o -> p (t o)", t=PACK))
 
         ident = held("ident", [P, P], F32)
         zeros = held("zeros", [P, P], F32, slot="window0")
@@ -78,9 +76,10 @@ def tile_attend_gkl_w_ts_kernel(tc, xT, w_words, w_scales, y, wt, ts, xm, offs, 
                 nc.sync.dma_start(plane[32 * q : 32 * q + 4, :], scale_sel[:].bitcast(I32)[row : row + 4, :])
 
         place_scales(plane_first, 0)
-        x_second = [fixed("x_second0", [P, PACK, HALF], F32, 16 * KIB), fixed("x_second1", [P, PACK, HALF], F32, 20 * KIB)]
-        for h in range(2):
-            nc.sync.dma_start(x_second[h][:], x_rows[1][:, :, h * HALF : (h + 1) * HALF])
+        x_second = fixed("x_second", [P, PACK, R], F32, 16 * KIB)
+        nc.sync.dma_start(x_second[:], x_rows[1])
+        wt_sb = fixed("wt_sb", [P, PACK], F32, 24 * KIB)
+        nc.sync.dma_start(wt_sb[:], wt[0].rearrange("(p t) o -> p (t o)", t=PACK))
 
         ts_pool = held("ts_pool", [P, T], F32)
         ts_view = ts_pool[:].rearrange("m (p c) -> m p c", p=P)
@@ -114,14 +113,14 @@ def tile_attend_gkl_w_ts_kernel(tc, xT, w_words, w_scales, y, wt, ts, xm, offs, 
             (0, 0): held("x_bf00", [P, 2 * P * PACK], BF16),
             (0, 1): held("x_bf01", [P, 2 * P * PACK], BF16, slot="ts_cols"),
             (1, 0): held("x_bf10", [P, 2 * P * PACK], BF16),
-            (1, 1): held("x_bf11", [P, 2 * P * PACK], BF16),
+            (1, 1): fixed("x_bf11", [P, 2 * P * PACK], BF16, 30 * KIB),
         }
         x_code = {key: held("x_code%d%d" % key, [P, 2 * P], U32) for key in x_bf}
         x_scale = {key: held("x_scale%d%d" % key, [P, 2 * P], U8) for key in x_bf}
 
-        def cast_x(o, u, raw, m0, on_vector):
-            src = raw[:].rearrange("p j (m t) -> p m j t", t=PACK)[:, :, :, 2 * u : 2 * u + 2]
-            dst = x_bf[o, u][:].rearrange("p (t m j) -> p m j t", t=2, j=PACK)[:, m0 : m0 + src.shape[1]]
+        def cast_x(o, u, raw, lo, hi, on_vector):
+            src = raw[:].rearrange("p j (m t) -> p m j t", t=PACK)[:, lo:hi, :, 2 * u : 2 * u + 2]
+            dst = x_bf[o, u][:].rearrange("p (t m j) -> p m j t", t=2, j=PACK)[:, lo:hi]
             if on_vector:
                 nc.vector.tensor_copy(dst, src)
             else:
@@ -149,16 +148,15 @@ def tile_attend_gkl_w_ts_kernel(tc, xT, w_words, w_scales, y, wt, ts, xm, offs, 
             )
 
         for u in range(2):
-            cast_x(0, u, x_first, 0, u == 0)
+            cast_x(0, u, x_first, 0, P, u == 0)
         y_sb = fixed("y_sb", [P, PACK, N], F32, 64 * KIB)
         nc.sync.dma_start(xm_raw[0][:], xm_rows[:, :, : D // 2])
         nc.sync.dma_start(y_sb[:], y[0].rearrange("(p t) i -> p t i", t=PACK))
         quantise_x(0, 0, 0, 2 * P)
-        for u in range(2):
-            cast_x(1, u, x_second[0], 0, False)
         quantise_x(0, 1, 0, 2 * P)
-        for u in range(2):
-            cast_x(1, u, x_second[1], P // 2, u == 0)
+        cast_x(1, 0, x_second, 0, CAST_SPLIT, True)
+        cast_x(1, 0, x_second, CAST_SPLIT, P, False)
+        cast_x(1, 1, x_second, 0, P, False)
         nc.sync.dma_start(xm_raw[1][:], xm_rows[:, :, D // 2 :])
         quantise_x(1, 0, 0, P)
         quantise_x(1, 0, P, 2 * P)
@@ -166,9 +164,11 @@ def tile_attend_gkl_w_ts_kernel(tc, xT, w_words, w_scales, y, wt, ts, xm, offs, 
         for t, o in ((0, 0), (1, 0), (0, 1), (1, 1), (2, 0), (2, 1), (3, 0), (3, 1)):
             score_pass(t, o)
 
-        wt_ts = fixed("wt_ts", [P, PACK, N], F32, 20 * KIB)
-        for t in range(PACK):
+        wt_ts = fixed("wt_ts", [P, PACK, N], F32, 30 * KIB)
+        for t in range(2):
             nc.scalar.activation(wt_ts[:, t, :], ts_sel[:], ACT.Copy, scale=wt_sb[:, t : t + 1])
+        for t in range(2, PACK):
+            nc.gpsimd.tensor_scalar(wt_ts[:, t, :], ts_sel[:], wt_sb[:, t : t + 1], 0.0, ALU.mult, ALU.add)
 
         neg_a = [held("neg_a%d" % t, [P, N], F32) for t in range(PACK - 1)] + [fixed("neg_a3", [P, N], F32, 55 * KIB)]
         neg_max = [held("neg_max%d" % t, [P, 1], F32) for t in range(PACK)]
@@ -202,11 +202,9 @@ def tile_attend_gkl_w_ts_kernel(tc, xT, w_words, w_scales, y, wt, ts, xm, offs, 
             if t == 0:
                 inv_first = held("inv_first", [P, 1], F32)
                 nc.gpsimd.tensor_tensor(inv_first[:], total[:, 0:1], minus_one[:], ALU.pow)
-                share = held("share", [P, ASIDE], F32, slot="window1")
+                share = held("share", [P, ASIDE], F32)
                 nc.gpsimd.tensor_scalar(share[:], e[0][:, :ASIDE], inv_first[:], 0.0, ALU.mult, ALU.add)
                 nc.gpsimd.tensor_tensor(g[:, 0, :ASIDE], share[:], y_sb[:, 0, :ASIDE], ALU.subtract)
-                second_window = held("window1", [P, T], F32)
-                nc.gpsimd.memset(second_window[:], 0.0)
         subtract_targets(1)
         invert(2, 3)
         nc.vector.scalar_tensor_tensor(g[:, 0, ASIDE:], e[0][:, ASIDE:], inv_first[:], y_sb[:, 0, ASIDE:], ALU.mult, ALU.subtract)
@@ -260,8 +258,8 @@ def tile_attend_gkl_w_ts_kernel(tc, xT, w_words, w_scales, y, wt, ts, xm, offs, 
         for k in range(1, len(groups)):
             lo, hi = groups[k]
             quantise_xm(code_rest[:, (lo - 1) * P : (hi - 1) * P], k)
-        windows = [first_window, second_window, fixed("window2", [P, T], F32, 48 * KIB), fixed("window3", [P, T], F32, 56 * KIB)]
-        for window in windows[2:]:
+        windows = [first_window, fixed("window1", [P, T], F32, 48 * KIB), fixed("window2", [P, T], F32, 56 * KIB)]
+        for window in windows[1:]:
             nc.gpsimd.memset(window[:], 0.0)
 
         for m in range(BLOCKS):

@@ -22,9 +22,10 @@ PACK = 4
 PASSES = D // (P * PACK)
 BLOCKS = D // P
 WINDOWS = 3
+HALF = N // 2
+EARLY = 2
 CAST_SPLIT = 96
 KIB = 1024
-ASIDE = 384
 
 
 def tile_attend_gkl_w_ts_kernel(tc, xT, w_words, w_scales, y, wt, ts, xm, offs, out):
@@ -33,8 +34,10 @@ def tile_attend_gkl_w_ts_kernel(tc, xT, w_words, w_scales, y, wt, ts, xm, offs, 
         keep = ctx.enter_context(tc.tile_pool(name="keep", bufs=1))
         placed = ctx.enter_context(tc.tile_pool(name="placed", bufs=1))
         ring = ctx.enter_context(tc.tile_pool(name="ring", bufs=3))
-        psum_scores = ctx.enter_context(tc.psum_pool(name="psum_scores", bufs=1))
-        psum_ring = ctx.enter_context(tc.psum_pool(name="psum_ring", bufs=4))
+        psum = ctx.enter_context(tc.psum_pool(name="psum", bufs=1))
+
+        def in_bank(name, k, shape):
+            return psum.tile(shape, F32, name=name, tag="bank%d" % k)
 
         def held(name, shape, dtype, slot=None):
             return keep.tile(shape, dtype, name=name, tag=slot or name, align_bytes=64)
@@ -84,12 +87,16 @@ def tile_attend_gkl_w_ts_kernel(tc, xT, w_words, w_scales, y, wt, ts, xm, offs, 
         ts_pool = held("ts_pool", [P, T], F32)
         ts_view = ts_pool[:].rearrange("m (p c) -> m p c", p=P)
         for b in range(4):
-            bank = psum_ring.tile([P, PACK, P], F32, name="bank")
+            bank = in_bank("ts_spread%d" % b, PACK + b, [P, PACK, P])
             for k in range(PACK):
                 c = PACK * b + k
                 nc.tensor.transpose(bank[:, k, :], ts_cols[:, c : c + 1].to_broadcast([P, P]), ident[:])
             nc.scalar.copy(ts_view[:, :, PACK * b : PACK * (b + 1)], bank[:].rearrange("m k p -> m p k"))
 
+        h_code = held("h_code", [P, N], U32)
+        h_scale = held("h_scale", [P, N], U8)
+        nc.vector.memset(h_code[:, HALF:], 0)
+        nc.vector.memset(h_scale[:, HALF:].bitcast(I32), 0)
         w_pair = held("w_pair", [P, N], U32)
         nc.vector.tensor_copy(w_pair[:], word_pool[:].bitcast(U32).indirect(offsets[:]))
         plane_second = held("plane_second", [P, N // 4], I32, slot="word_pool")
@@ -107,13 +114,23 @@ def tile_attend_gkl_w_ts_kernel(tc, xT, w_words, w_scales, y, wt, ts, xm, offs, 
         nc.vector.tensor_copy(ts_sel[:], ts_pool[:].indirect(offsets[:]))
 
         xm_rows = xm[0].rearrange("(p j) d -> p j d", j=PACK)
-        xm_raw = [fixed("xm_raw0", [P, PACK, D // 2], F32, 72 * KIB), fixed("xm_raw1", [P, PACK, D // 2], F32, 12 * KIB)]
+        xm_spans = ((0, 2), (2, 4), (4, 8))
+        xm_raw = [
+            fixed("xm_raw0", [P, PACK, 2 * P], F32, 72 * KIB),
+            fixed("xm_raw1", [P, PACK, 2 * P], F32, 20 * KIB),
+            fixed("xm_raw2", [P, PACK, 4 * P], F32, 12 * KIB),
+        ]
+
+        def load_xm(c):
+            lo, hi = xm_spans[c]
+            nc.sync.dma_start(xm_raw[c][:], xm_rows[:, :, lo * P : hi * P])
+
 
         x_bf = {
             (0, 0): held("x_bf00", [P, 2 * P * PACK], BF16),
             (0, 1): held("x_bf01", [P, 2 * P * PACK], BF16, slot="ts_cols"),
             (1, 0): held("x_bf10", [P, 2 * P * PACK], BF16),
-            (1, 1): fixed("x_bf11", [P, 2 * P * PACK], BF16, 30 * KIB),
+            (1, 1): fixed("x_bf11", [P, 2 * P * PACK], BF16, 40 * KIB),
         }
         x_code = {key: held("x_code%d%d" % key, [P, 2 * P], U32) for key in x_bf}
         x_scale = {key: held("x_scale%d%d" % key, [P, 2 * P], U8) for key in x_bf}
@@ -133,7 +150,7 @@ def tile_attend_gkl_w_ts_kernel(tc, xT, w_words, w_scales, y, wt, ts, xm, offs, 
                 in_=x_bf[o, u][:, PACK * lo : PACK * hi],
             )
 
-        scores = [psum_scores.tile([P, N], F32, name="scores%d" % t) for t in range(PACK)]
+        scores = [in_bank("scores%d" % t, t, [P, N]) for t in range(PACK)]
 
         def score_pass(t, o):
             u, k = divmod(t, 2)
@@ -150,32 +167,53 @@ def tile_attend_gkl_w_ts_kernel(tc, xT, w_words, w_scales, y, wt, ts, xm, offs, 
         for u in range(2):
             cast_x(0, u, x_first, 0, P, u == 0)
         y_sb = fixed("y_sb", [P, PACK, N], F32, 64 * KIB)
-        nc.sync.dma_start(xm_raw[0][:], xm_rows[:, :, : D // 2])
+        load_xm(0)
         nc.sync.dma_start(y_sb[:], y[0].rearrange("(p t) i -> p t i", t=PACK))
         quantise_x(0, 0, 0, 2 * P)
         quantise_x(0, 1, 0, 2 * P)
         cast_x(1, 0, x_second, 0, CAST_SPLIT, True)
         cast_x(1, 0, x_second, CAST_SPLIT, P, False)
         cast_x(1, 1, x_second, 0, P, False)
-        nc.sync.dma_start(xm_raw[1][:], xm_rows[:, :, D // 2 :])
+        load_xm(1)
+        load_xm(2)
         quantise_x(1, 0, 0, P)
         quantise_x(1, 0, P, 2 * P)
         quantise_x(1, 1, 0, 2 * P)
         for t, o in ((0, 0), (1, 0), (0, 1), (1, 1), (2, 0), (2, 1), (3, 0), (3, 1)):
             score_pass(t, o)
 
-        wt_ts = fixed("wt_ts", [P, PACK, N], F32, 30 * KIB)
-        for t in range(2):
-            nc.scalar.activation(wt_ts[:, t, :], ts_sel[:], ACT.Copy, scale=wt_sb[:, t : t + 1])
-        for t in range(2, PACK):
-            nc.gpsimd.tensor_scalar(wt_ts[:, t, :], ts_sel[:], wt_sb[:, t : t + 1], 0.0, ALU.mult, ALU.add)
+        halves = [slice(0, HALF), slice(HALF, N)]
+        turns = HALF // P
+
+        ts_bank = in_bank("ts_bank", 4, [P, turns, P])
+        for b in range(turns):
+            nc.tensor.transpose(ts_bank[:, b, :], ts_sel[:, HALF + b * P : HALF + (b + 1) * P], ident[:])
+        ts_late = held("ts_late", [P, turns], F32)
+        wt_ts = fixed("wt_ts", [P, PACK, HALF], F32, 37 * KIB)
+        for t in range(PACK):
+            nc.gpsimd.tensor_scalar(wt_ts[:, t, :], ts_sel[:, halves[0]], wt_sb[:, t : t + 1], 0.0, ALU.mult, ALU.add)
+        neg_wt = held("neg_wt", [P, PACK], F32)
+        nc.gpsimd.tensor_scalar(neg_wt[:], wt_sb[:], -1.0, 0.0, ALU.mult, ALU.add)
+        neg_target = held("neg_target", [P, PACK, HALF], F32)
+        for t in range(PACK):
+            nc.gpsimd.tensor_scalar(neg_target[:, t, :], y_sb[:, t, halves[1]], neg_wt[:, t : t + 1], 0.0, ALU.mult, ALU.add)
+
+        second_window = held("window1", [P, T], F32, slot="neg_wt")
+        nc.gpsimd.memset(second_window[:], 0.0)
+
+        turned = [in_bank("turned%d" % b, 5 + b, [P, PACK, P]) for b in range(turns)]
+        for b in range(turns):
+            for t in range(PACK):
+                nc.tensor.matmul(
+                    turned[b][:, t, :], neg_target[:, t, b * P : (b + 1) * P], ident[:], start=(t == 0), stop=False, is_transpose=True
+                )
 
         neg_a = [held("neg_a%d" % t, [P, N], F32) for t in range(PACK - 1)] + [fixed("neg_a3", [P, N], F32, 55 * KIB)]
         neg_max = [held("neg_max%d" % t, [P, 1], F32) for t in range(PACK)]
         e = [held("e%d" % t, [P, N], F32) for t in range(PACK)]
         total = held("total", [P, PACK], F32)
         inv = held("inv", [P, PACK], F32)
-        g = held("g", [P, PACK, N], F32)
+        g = held("g", [P, PACK, HALF], F32)
 
         def scale_scores(t):
             nc.vector.scalar_tensor_tensor(neg_a[t][:], scores[t][:], -1.0, ts_sel[:], ALU.mult, ALU.mult)
@@ -187,98 +225,142 @@ def tile_attend_gkl_w_ts_kernel(tc, xT, w_words, w_scales, y, wt, ts, xm, offs, 
         def invert(lo, hi):
             nc.vector.reciprocal(inv[:, lo:hi], total[:, lo:hi])
 
-        def subtract_targets(t, s=slice(0, N)):
-            nc.vector.scalar_tensor_tensor(g[:, t, s], e[t][:, s], inv[:, t : t + 1], y_sb[:, t, s], ALU.mult, ALU.subtract)
-
-        minus_one = held("minus_one", [P, 1], F32)
-        nc.gpsimd.memset(minus_one[:], -1.0)
         scale_scores(0)
         for t in range(PACK):
             if t + 1 < PACK:
                 scale_scores(t + 1)
             else:
-                invert(1, 2)
+                invert(0, 2)
             exponentiate(t)
-            if t == 0:
-                inv_first = held("inv_first", [P, 1], F32)
-                nc.gpsimd.tensor_tensor(inv_first[:], total[:, 0:1], minus_one[:], ALU.pow)
-                share = held("share", [P, ASIDE], F32)
-                nc.gpsimd.tensor_scalar(share[:], e[0][:, :ASIDE], inv_first[:], 0.0, ALU.mult, ALU.add)
-                nc.gpsimd.tensor_tensor(g[:, 0, :ASIDE], share[:], y_sb[:, 0, :ASIDE], ALU.subtract)
-        subtract_targets(1)
+
+        nc.scalar.copy(ts_late[:], ts_bank[:, :, 0])
+
+        def subtract_targets(t):
+            nc.vector.scalar_tensor_tensor(
+                g[:, t, :], e[t][:, halves[0]], inv[:, t : t + 1], y_sb[:, t, halves[0]], ALU.mult, ALU.subtract
+            )
+
+        subtract_targets(0)
         invert(2, 3)
-        nc.vector.scalar_tensor_tensor(g[:, 0, ASIDE:], e[0][:, ASIDE:], inv_first[:], y_sb[:, 0, ASIDE:], ALU.mult, ALU.subtract)
+        subtract_targets(1)
+        invert(3, PACK)
 
         groups = ((0, 1), (1, 2), (2, 4), (4, 8))
         xm_bf = [
-            held("xm_bf0", [P, PACK * P], BF16, slot="neg_a0"),
-            fixed("xm_bf1", [P, PACK * P], BF16, 54 * KIB + 512),
-            held("xm_bf2", [P, 2 * PACK * P], BF16, slot="neg_max3"),
-            fixed("xm_bf3", [P, PACK * PACK * P], BF16, 55 * KIB + 512),
+            fixed("xm_bf0", [P, PACK * P], BF16, 41 * KIB),
+            held("xm_bf1", [P, PACK * P], BF16, slot="x_bf10"),
+            fixed("xm_bf2", [P, 2 * PACK * P], BF16, 49 * KIB + 512),
+            fixed("xm_bf3", [P, PACK * PACK * P], BF16, 46 * KIB),
         ]
-        code_first = held("xm_code0", [P, P], U32, slot="e1")
         xm_scale = held("xm_scale", [P, D], U8)
-        for k, (lo, hi) in enumerate(groups):
+        xm_code = held("xm_code", [P, D], U32)
+
+        def cast_xm(k):
+            lo, hi = groups[k]
             for m in range(lo, hi):
-                c, u = divmod(m, BLOCKS // 2)
+                c = max(0, k - 1)
+                u = m - xm_spans[c][0]
                 nc.scalar.copy(
                     xm_bf[k][:, (m - lo) * PACK * P : (m - lo + 1) * PACK * P].rearrange("p (c i j) -> p c j i", i=4, j=PACK),
                     xm_raw[c][:, :, u * P : (u + 1) * P].rearrange("p j (c i) -> p c j i", i=4),
                 )
 
-        def quantise_xm(code, k):
+        def quantise_xm(k):
             lo, hi = groups[k]
-            nc.vector.quantize_mx(out=code.bitcast(E4M3), scales=xm_scale[:, lo * P : hi * P], in_=xm_bf[k][:])
-
-        halves = [slice(0, N // 2), slice(N // 2, N)]
-        quantise_xm(code_first[:], 0)
-        subtract_targets(2, halves[0])
-        invert(3, PACK)
-        subtract_targets(2, halves[1])
-        for s in halves:
-            subtract_targets(3, s)
-
-        h_bf = held("h_bf", [P, N, PACK], BF16)
-        h_code = held("h_code", [P, N], U32)
-        h_scale = held("h_scale", [P, N], U8)
-        for s in halves:
-            nc.vector.tensor_tensor(
-                h_bf[:, s, :].rearrange("p (c i) t -> p c t i", i=2),
-                g[:, :, s].rearrange("p t (c i) -> p c t i", i=2),
-                wt_ts[:, :, s].rearrange("p t (c i) -> p c t i", i=2),
-                ALU.mult,
-            )
-        for s in halves:
             nc.vector.quantize_mx(
-                out=h_code[:, s].bitcast(E5M2), scales=h_scale[:, s], in_=h_bf[:, s, :].rearrange("p i t -> p (i t)")
+                out=xm_code[:, lo * P : hi * P].bitcast(E4M3), scales=xm_scale[:, lo * P : hi * P], in_=xm_bf[k][:]
             )
 
-        code_rest = held("xm_code_rest", [P, D - P], U32, slot="h_bf")
-        xm_code = [code_first[:]] + [code_rest[:, k * P : (k + 1) * P] for k in range(BLOCKS - 1)]
-        for k in range(1, len(groups)):
-            lo, hi = groups[k]
-            quantise_xm(code_rest[:, (lo - 1) * P : (hi - 1) * P], k)
-        windows = [first_window, fixed("window1", [P, T], F32, 48 * KIB), fixed("window2", [P, T], F32, 56 * KIB)]
-        for window in windows[1:]:
-            nc.gpsimd.memset(window[:], 0.0)
+        cast_xm(0)
+        cast_xm(1)
+        subtract_targets(2)
+        weight = held("weight", [P, PACK], F32)
+        nc.vector.tensor_tensor(weight[:], inv[:], wt_sb[:], ALU.mult)
+        subtract_targets(3)
+        quantise_xm(0)
 
-        for m in range(BLOCKS):
-            bank = psum_ring.tile([P, N], F32, name="bank")
+        h_bf = [held("h_bf%d" % k, [P, HALF, PACK], BF16) for k in range(2)]
+
+        def quantise_h(k):
+            nc.vector.quantize_mx(
+                out=h_code[:, halves[k]].bitcast(E5M2),
+                scales=h_scale[:, halves[k]],
+                in_=h_bf[k][:].rearrange("p i t -> p (i t)"),
+            )
+
+        nc.vector.tensor_tensor(
+            h_bf[0][:].rearrange("p (c i) t -> p c t i", i=2),
+            g[:].rearrange("p t (c i) -> p c t i", i=2),
+            wt_ts[:].rearrange("p t (c i) -> p c t i", i=2),
+            ALU.mult,
+        )
+        quantise_h(0)
+        quantise_xm(1)
+
+        def multiply(m, s, bank):
             nc.tensor.matmul_mx(
                 out=bank[:],
-                lhsT=xm_code[m].bitcast(E4M3),
+                lhsT=xm_code[:, m * P : (m + 1) * P].bitcast(E4M3),
                 lhsT_scale=xm_scale[:, m * P : (m + 1) * P],
                 rhs=h_code[:].bitcast(E5M2),
                 rhs_scale=h_scale[:],
                 start=True,
                 stop=True,
             )
-            dw = ring.tile([P, N], F32, name="dw")
-            window = windows[m % WINDOWS]
-            pieces = 2 if m == 0 else 1
-            width = N // pieces
-            for k in range(pieces):
-                nc.scalar.copy(dw[:, k * width : (k + 1) * width], bank[:, k * width : (k + 1) * width])
-                listed = offsets[:, k * width // 16 : (k + 1) * width // 16]
-                nc.vector.tensor_copy(window[:].indirect(listed), dw[:, k * width : (k + 1) * width])
-            nc.sync.dma_start(out[m * P : (m + 1) * P, :], window[:])
+            return bank[:, s]
+
+        windows = [first_window, second_window]
+
+        def scatter(m, s, dw):
+            nc.vector.tensor_copy(windows[m % WINDOWS][:].indirect(offsets[:, s.start // 16 : s.stop // 16]), dw)
+
+        dw_early = [held("dw_early0", [P, HALF], F32), fixed("dw_early1", [P, HALF], F32, 47 * KIB + 512)]
+        first_bank = in_bank("first_bank", 7, [P, N])
+        nc.vector.tensor_copy(dw_early[0][:], multiply(0, halves[0], first_bank))
+        scatter(0, halves[0], dw_early[0][:])
+
+        share = held("share", [P, PACK, HALF], F32)
+        for t in range(PACK):
+            nc.scalar.activation(share[:, t, :], e[t][:, halves[1]], ACT.Copy, scale=weight[:, t : t + 1])
+            for b in range(turns):
+                nc.tensor.matmul(
+                    turned[b][:, t, :], share[:, t, b * P : (b + 1) * P], ident[:], start=False, stop=(t == PACK - 1), is_transpose=True
+                )
+        h_turned = fixed("h_turned", [P, turns, 2, P, 2], BF16, 48 * KIB)
+        back = in_bank("back", 0, [P, turns, 2, P])
+        for b in range(turns):
+            nc.scalar.activation(
+                h_turned[:, b], turned[b][:].rearrange("s (u e) p -> s u p e", e=2), ACT.Copy, scale=ts_late[:, b : b + 1]
+            )
+            for u in range(2):
+                nc.tensor.transpose(back[:, b, u, :], h_turned[:, b, u].rearrange("s p e -> s (p e)").bitcast(F32), ident[:])
+        nc.scalar.copy(
+            h_bf[1][:].rearrange("p i t -> p (i t)").bitcast(F32).rearrange("p (b s u) -> p b s u", b=turns, u=2),
+            back[:].rearrange("p b u s -> p b s u"),
+        )
+
+        second_bank = in_bank("second_bank", 6, [P, N])
+        second_product = multiply(1, halves[0], second_bank)
+        quantise_h(1)
+        nc.scalar.copy(dw_early[1][:], second_product)
+        scatter(1, halves[0], dw_early[1][:])
+        cast_xm(2)
+        quantise_xm(2)
+        third_window = fixed("window2", [P, T], F32, 51 * KIB)
+        nc.gpsimd.memset(third_window[:], 0.0)
+        windows.append(third_window)
+
+        placed_dw = {0: 20 * KIB, EARLY: 12 * KIB}
+        for m in range(BLOCKS):
+            if m == EARLY:
+                cast_xm(3)
+                quantise_xm(3)
+            s = halves[1] if m < EARLY else slice(0, N)
+            bank = multiply(m, s, in_bank("product%d" % m, (m + 1) % BLOCKS, [P, N]))
+            if m in placed_dw:
+                dw = fixed("dw_placed%d" % m, [P, N], F32, placed_dw[m])
+            else:
+                dw = ring.tile([P, N], F32, name="dw")
+            nc.scalar.copy(dw[:, s], bank)
+            scatter(m, s, dw[:, s])
+            nc.sync.dma_start(out[m * P : (m + 1) * P, :], windows[m % WINDOWS][:])

@@ -60,15 +60,21 @@ def tile_attend_gkl_w_ts_kernel(tc, xT, w_words, w_scales, y, wt, ts, xm, offs, 
         nc.sync.dma_start(x_first[:], x_rows[0])
 
         ident = held("ident", [P, P], F32)
-        zeros = held("zeros", [P, P], F32, slot="window0")
-        nc.gpsimd.memset(zeros[:], 0.0)
+        plane_first = held("plane_first", [P, N // 4], I32)
+        nc.vector.memset(plane_first[:], 0)
+        h_code = held("h_code", [P, N], U32)
+        h_scale = held("h_scale", [P, N], U8)
+        nc.vector.memset(h_code[:, HALF:], 0)
+        nc.vector.memset(h_scale[:, HALF:].bitcast(I32), 0)
+        first_window = held("window0", [P, T], F32)
+        nc.vector.memset(first_window[:], 0.0)
+        zeros = held("zeros", [P, P], F32, slot="window1")
+        nc.vector.memset(zeros[:], 0.0)
         nc.gpsimd.affine_select(
             out=ident[:], in_=zeros[:], compare_op=ALU.not_equal, fill=1.0, base=0, pattern=[[-1, P]], channel_multiplier=1
         )
-        plane_first = held("plane_first", [P, N // 4], I32)
-        nc.vector.memset(plane_first[:], 0)
-        first_window = held("window0", [P, T], F32)
-        nc.gpsimd.memset(first_window[:], 0.0)
+        second_window = held("window1", [P, T], F32)
+        nc.gpsimd.memset(second_window[:], 0.0)
 
         scale_sel = held("scale_sel", [P, N], U8)
         nc.vector.tensor_copy(scale_sel[:], scale_pool[:].bitcast(U8).indirect(offsets[:]))
@@ -93,11 +99,7 @@ def tile_attend_gkl_w_ts_kernel(tc, xT, w_words, w_scales, y, wt, ts, xm, offs, 
                 nc.tensor.transpose(bank[:, k, :], ts_cols[:, c : c + 1].to_broadcast([P, P]), ident[:])
             nc.scalar.copy(ts_view[:, :, PACK * b : PACK * (b + 1)], bank[:].rearrange("m k p -> m p k"))
 
-        h_code = held("h_code", [P, N], U32)
-        h_scale = held("h_scale", [P, N], U8)
-        nc.vector.memset(h_code[:, HALF:], 0)
-        nc.vector.memset(h_scale[:, HALF:].bitcast(I32), 0)
-        w_pair = held("w_pair", [P, N], U32)
+        w_pair = fixed("w_pair", [P, N], U32, 84 * KIB)
         nc.vector.tensor_copy(w_pair[:], word_pool[:].bitcast(U32).indirect(offsets[:]))
         plane_second = held("plane_second", [P, N // 4], I32, slot="word_pool")
         nc.vector.memset(plane_second[:], 0)
@@ -116,7 +118,7 @@ def tile_attend_gkl_w_ts_kernel(tc, xT, w_words, w_scales, y, wt, ts, xm, offs, 
         xm_rows = xm[0].rearrange("(p j) d -> p j d", j=PACK)
         xm_spans = ((0, 2), (2, 4), (4, 8))
         xm_raw = [
-            fixed("xm_raw0", [P, PACK, 2 * P], F32, 72 * KIB),
+            fixed("xm_raw0", [P, PACK, 2 * P], F32, 80 * KIB + 512),
             fixed("xm_raw1", [P, PACK, 2 * P], F32, 20 * KIB),
             fixed("xm_raw2", [P, PACK, 4 * P], F32, 12 * KIB),
         ]
@@ -166,7 +168,7 @@ def tile_attend_gkl_w_ts_kernel(tc, xT, w_words, w_scales, y, wt, ts, xm, offs, 
 
         for u in range(2):
             cast_x(0, u, x_first, 0, P, u == 0)
-        y_sb = fixed("y_sb", [P, PACK, N], F32, 64 * KIB)
+        y_sb = fixed("y_sb", [P, PACK, N], F32, 85 * KIB + 512)
         load_xm(0)
         nc.sync.dma_start(y_sb[:], y[0].rearrange("(p t) i -> p t i", t=PACK))
         quantise_x(0, 0, 0, 2 * P)
@@ -179,8 +181,14 @@ def tile_attend_gkl_w_ts_kernel(tc, xT, w_words, w_scales, y, wt, ts, xm, offs, 
         quantise_x(1, 0, 0, P)
         quantise_x(1, 0, P, 2 * P)
         quantise_x(1, 1, 0, 2 * P)
-        for t, o in ((0, 0), (1, 0), (0, 1), (1, 1), (2, 0), (2, 1), (3, 0), (3, 1)):
-            score_pass(t, o)
+        for o in range(PASSES):
+            for t in range(PACK):
+                score_pass(t, o)
+
+        neg_a = [held("neg_a%d" % t, [P, N], F32) for t in range(PACK)]
+        neg_raw = held("neg_raw", [P, N], F32)
+        nc.scalar.activation(neg_raw[:], scores[0][:], ACT.Copy, scale=-1.0)
+        nc.gpsimd.tensor_tensor(neg_a[0][:], neg_raw[:], ts_sel[:], ALU.mult)
 
         halves = [slice(0, HALF), slice(HALF, N)]
         turns = HALF // P
@@ -198,8 +206,6 @@ def tile_attend_gkl_w_ts_kernel(tc, xT, w_words, w_scales, y, wt, ts, xm, offs, 
         for t in range(PACK):
             nc.gpsimd.tensor_scalar(neg_target[:, t, :], y_sb[:, t, halves[1]], neg_wt[:, t : t + 1], 0.0, ALU.mult, ALU.add)
 
-        second_window = held("window1", [P, T], F32, slot="neg_wt")
-        nc.gpsimd.memset(second_window[:], 0.0)
 
         turned = [in_bank("turned%d" % b, 5 + b, [P, PACK, P]) for b in range(turns)]
         for b in range(turns):
@@ -208,7 +214,6 @@ def tile_attend_gkl_w_ts_kernel(tc, xT, w_words, w_scales, y, wt, ts, xm, offs, 
                     turned[b][:, t, :], neg_target[:, t, b * P : (b + 1) * P], ident[:], start=(t == 0), stop=False, is_transpose=True
                 )
 
-        neg_a = [held("neg_a%d" % t, [P, N], F32) for t in range(PACK - 1)] + [fixed("neg_a3", [P, N], F32, 55 * KIB)]
         neg_max = [held("neg_max%d" % t, [P, 1], F32) for t in range(PACK)]
         e = [held("e%d" % t, [P, N], F32) for t in range(PACK)]
         total = held("total", [P, PACK], F32)
@@ -222,16 +227,17 @@ def tile_attend_gkl_w_ts_kernel(tc, xT, w_words, w_scales, y, wt, ts, xm, offs, 
             nc.vector.tensor_reduce(neg_max[t][:], neg_a[t][:], mybir.AxisListType.X, ALU.min)
             nc.scalar.activation(e[t][:], neg_a[t][:], ACT.Exp, bias=neg_max[t][:], scale=-1.0, accum_out=total[:, t : t + 1])
 
-        def invert(lo, hi):
-            nc.vector.reciprocal(inv[:, lo:hi], total[:, lo:hi])
+        def invert(cols):
+            nc.vector.reciprocal(inv[:, cols], total[:, cols])
 
-        scale_scores(0)
-        for t in range(PACK):
-            if t + 1 < PACK:
-                scale_scores(t + 1)
-            else:
-                invert(0, 2)
-            exponentiate(t)
+        scale_scores(1)
+        scale_scores(2)
+        exponentiate(1)
+        scale_scores(3)
+        exponentiate(2)
+        exponentiate(0)
+        exponentiate(3)
+        invert(slice(1, 3))
 
         nc.scalar.copy(ts_late[:], ts_bank[:, :, 0])
 
@@ -240,44 +246,44 @@ def tile_attend_gkl_w_ts_kernel(tc, xT, w_words, w_scales, y, wt, ts, xm, offs, 
                 g[:, t, :], e[t][:, halves[0]], inv[:, t : t + 1], y_sb[:, t, halves[0]], ALU.mult, ALU.subtract
             )
 
-        subtract_targets(0)
-        invert(2, 3)
         subtract_targets(1)
-        invert(3, PACK)
+        subtract_targets(2)
+        invert(slice(0, PACK, 3))
 
-        groups = ((0, 1), (1, 2), (2, 4), (4, 8))
+        groups = ((0, 1), (1, 2), (2, 3), (3, 4), (4, 8))
         xm_bf = [
             fixed("xm_bf0", [P, PACK * P], BF16, 41 * KIB),
             held("xm_bf1", [P, PACK * P], BF16, slot="x_bf10"),
-            fixed("xm_bf2", [P, 2 * PACK * P], BF16, 49 * KIB + 512),
-            fixed("xm_bf3", [P, PACK * PACK * P], BF16, 46 * KIB),
+            held("xm_bf2", [P, PACK * P], BF16, slot="neg_a3"),
+            held("xm_bf3", [P, PACK * P], BF16, slot="ts_late"),
+            fixed("xm_bf4", [P, PACK * PACK * P], BF16, 48 * KIB + 512),
         ]
         xm_scale = held("xm_scale", [P, D], U8)
-        xm_code = held("xm_code", [P, D], U32)
+        code_early = held("xm_code_early", [P, D // 2], U32)
+        xm_code = [code_early[:, m * P : (m + 1) * P] for m in range(BLOCKS // 2)]
 
         def cast_xm(k):
             lo, hi = groups[k]
             for m in range(lo, hi):
-                c = max(0, k - 1)
+                c = min(m // 2, 2)
                 u = m - xm_spans[c][0]
                 nc.scalar.copy(
                     xm_bf[k][:, (m - lo) * PACK * P : (m - lo + 1) * PACK * P].rearrange("p (c i j) -> p c j i", i=4, j=PACK),
                     xm_raw[c][:, :, u * P : (u + 1) * P].rearrange("p j (c i) -> p c j i", i=4),
                 )
 
-        def quantise_xm(k):
+        def quantise_xm(k, code):
             lo, hi = groups[k]
-            nc.vector.quantize_mx(
-                out=xm_code[:, lo * P : hi * P].bitcast(E4M3), scales=xm_scale[:, lo * P : hi * P], in_=xm_bf[k][:]
-            )
+            nc.vector.quantize_mx(out=code.bitcast(E4M3), scales=xm_scale[:, lo * P : hi * P], in_=xm_bf[k][:])
 
         cast_xm(0)
         cast_xm(1)
-        subtract_targets(2)
+        cast_xm(2)
+        quantise_xm(0, xm_code[0])
         weight = held("weight", [P, PACK], F32)
         nc.vector.tensor_tensor(weight[:], inv[:], wt_sb[:], ALU.mult)
+        subtract_targets(0)
         subtract_targets(3)
-        quantise_xm(0)
 
         h_bf = [held("h_bf%d" % k, [P, HALF, PACK], BF16) for k in range(2)]
 
@@ -295,12 +301,13 @@ def tile_attend_gkl_w_ts_kernel(tc, xT, w_words, w_scales, y, wt, ts, xm, offs, 
             ALU.mult,
         )
         quantise_h(0)
-        quantise_xm(1)
+        quantise_xm(1, xm_code[1])
+        quantise_xm(2, xm_code[2])
 
         def multiply(m, s, bank):
             nc.tensor.matmul_mx(
                 out=bank[:],
-                lhsT=xm_code[:, m * P : (m + 1) * P].bitcast(E4M3),
+                lhsT=xm_code[m].bitcast(E4M3),
                 lhsT_scale=xm_scale[:, m * P : (m + 1) * P],
                 rhs=h_code[:].bitcast(E5M2),
                 rhs_scale=h_scale[:],
@@ -327,13 +334,15 @@ def tile_attend_gkl_w_ts_kernel(tc, xT, w_words, w_scales, y, wt, ts, xm, offs, 
                     turned[b][:, t, :], share[:, t, b * P : (b + 1) * P], ident[:], start=False, stop=(t == PACK - 1), is_transpose=True
                 )
         h_turned = fixed("h_turned", [P, turns, 2, P, 2], BF16, 48 * KIB)
-        back = in_bank("back", 0, [P, turns, 2, P])
+        back = in_bank("back", 7, [P, turns, 2, P])
         for b in range(turns):
             nc.scalar.activation(
                 h_turned[:, b], turned[b][:].rearrange("s (u e) p -> s u p e", e=2), ACT.Copy, scale=ts_late[:, b : b + 1]
             )
             for u in range(2):
                 nc.tensor.transpose(back[:, b, u, :], h_turned[:, b, u].rearrange("s p e -> s (p e)").bitcast(F32), ident[:])
+        cast_xm(3)
+        quantise_xm(3, xm_code[3])
         nc.scalar.copy(
             h_bf[1][:].rearrange("p i t -> p (i t)").bitcast(F32).rearrange("p (b s u) -> p b s u", b=turns, u=2),
             back[:].rearrange("p b u s -> p b s u"),
@@ -344,21 +353,22 @@ def tile_attend_gkl_w_ts_kernel(tc, xT, w_words, w_scales, y, wt, ts, xm, offs, 
         quantise_h(1)
         nc.scalar.copy(dw_early[1][:], second_product)
         scatter(1, halves[0], dw_early[1][:])
-        cast_xm(2)
-        quantise_xm(2)
-        third_window = fixed("window2", [P, T], F32, 51 * KIB)
+        third_window = held("window2", [P, T], F32, slot="h_bf1")
         nc.gpsimd.memset(third_window[:], 0.0)
         windows.append(third_window)
 
-        placed_dw = {0: 20 * KIB, EARLY: 12 * KIB}
         for m in range(BLOCKS):
             if m == EARLY:
-                cast_xm(3)
-                quantise_xm(3)
+                cast_xm(4)
+                code_late = held("xm_code_late", [P, D // 2], U32, slot="dw_first")
+                quantise_xm(4, code_late[:])
+                xm_code.extend([code_late[:, k * P : (k + 1) * P] for k in range(BLOCKS // 2)])
             s = halves[1] if m < EARLY else slice(0, N)
             bank = multiply(m, s, in_bank("product%d" % m, (m + 1) % BLOCKS, [P, N]))
-            if m in placed_dw:
-                dw = fixed("dw_placed%d" % m, [P, N], F32, placed_dw[m])
+            if m == 0:
+                dw = held("dw_first", [P, N], F32)
+            elif m == EARLY:
+                dw = fixed("dw_placed", [P, N], F32, 12 * KIB)
             else:
                 dw = ring.tile([P, N], F32, name="dw")
             nc.scalar.copy(dw[:, s], bank)

@@ -186,9 +186,6 @@ def tile_attend_gkl_w_ts_kernel(tc, xT, w_words, w_scales, y, wt, ts, xm, offs, 
                 score_pass(t, o)
 
         neg_a = [held("neg_a%d" % t, [P, N], F32) for t in range(PACK)]
-        neg_raw = held("neg_raw", [P, N], F32)
-        nc.scalar.activation(neg_raw[:], scores[0][:], ACT.Copy, scale=-1.0)
-        nc.gpsimd.tensor_tensor(neg_a[0][:], neg_raw[:], ts_sel[:], ALU.mult)
 
         halves = [slice(0, HALF), slice(HALF, N)]
         turns = HALF // P
@@ -198,8 +195,10 @@ def tile_attend_gkl_w_ts_kernel(tc, xT, w_words, w_scales, y, wt, ts, xm, offs, 
             nc.tensor.transpose(ts_bank[:, b, :], ts_sel[:, HALF + b * P : HALF + (b + 1) * P], ident[:])
         ts_late = held("ts_late", [P, turns], F32)
         wt_ts = fixed("wt_ts", [P, PACK, HALF], F32, 37 * KIB)
-        for t in range(PACK):
+        for t in range(2):
             nc.gpsimd.tensor_scalar(wt_ts[:, t, :], ts_sel[:, halves[0]], wt_sb[:, t : t + 1], 0.0, ALU.mult, ALU.add)
+        for t in range(2, PACK):
+            nc.scalar.activation(wt_ts[:, t, :], ts_sel[:, halves[0]], ACT.Copy, scale=wt_sb[:, t : t + 1])
         neg_wt = held("neg_wt", [P, PACK], F32)
         nc.gpsimd.tensor_scalar(neg_wt[:], wt_sb[:], -1.0, 0.0, ALU.mult, ALU.add)
         neg_target = held("neg_target", [P, PACK, HALF], F32)
@@ -230,14 +229,13 @@ def tile_attend_gkl_w_ts_kernel(tc, xT, w_words, w_scales, y, wt, ts, xm, offs, 
         def invert(cols):
             nc.vector.reciprocal(inv[:, cols], total[:, cols])
 
-        scale_scores(1)
-        scale_scores(2)
-        exponentiate(1)
-        scale_scores(3)
-        exponentiate(2)
-        exponentiate(0)
-        exponentiate(3)
-        invert(slice(1, 3))
+        scale_scores(0)
+        for t in range(PACK):
+            if t + 1 < PACK:
+                scale_scores(t + 1)
+            else:
+                invert(slice(0, 2))
+            exponentiate(t)
 
         nc.scalar.copy(ts_late[:], ts_bank[:, :, 0])
 
@@ -246,21 +244,21 @@ def tile_attend_gkl_w_ts_kernel(tc, xT, w_words, w_scales, y, wt, ts, xm, offs, 
                 g[:, t, :], e[t][:, halves[0]], inv[:, t : t + 1], y_sb[:, t, halves[0]], ALU.mult, ALU.subtract
             )
 
+        subtract_targets(0)
         subtract_targets(1)
-        subtract_targets(2)
-        invert(slice(0, PACK, 3))
+        invert(slice(2, PACK))
 
         groups = ((0, 1), (1, 2), (2, 3), (3, 4), (4, 8))
         xm_bf = [
             fixed("xm_bf0", [P, PACK * P], BF16, 41 * KIB),
             held("xm_bf1", [P, PACK * P], BF16, slot="x_bf10"),
             held("xm_bf2", [P, PACK * P], BF16, slot="neg_a3"),
-            held("xm_bf3", [P, PACK * P], BF16, slot="ts_late"),
+            held("xm_bf3", [P, PACK * P], BF16, slot="weight"),
             fixed("xm_bf4", [P, PACK * PACK * P], BF16, 48 * KIB + 512),
         ]
         xm_scale = held("xm_scale", [P, D], U8)
-        code_early = held("xm_code_early", [P, D // 2], U32)
-        xm_code = [code_early[:, m * P : (m + 1) * P] for m in range(BLOCKS // 2)]
+        code_first = held("xm_code_first", [P, P], U32)
+        xm_code = [code_first[:]]
 
         def cast_xm(k):
             lo, hi = groups[k]
@@ -282,7 +280,7 @@ def tile_attend_gkl_w_ts_kernel(tc, xT, w_words, w_scales, y, wt, ts, xm, offs, 
         quantise_xm(0, xm_code[0])
         weight = held("weight", [P, PACK], F32)
         nc.vector.tensor_tensor(weight[:], inv[:], wt_sb[:], ALU.mult)
-        subtract_targets(0)
+        subtract_targets(2)
         subtract_targets(3)
 
         h_bf = [held("h_bf%d" % k, [P, HALF, PACK], BF16) for k in range(2)]
@@ -301,6 +299,8 @@ def tile_attend_gkl_w_ts_kernel(tc, xT, w_words, w_scales, y, wt, ts, xm, offs, 
             ALU.mult,
         )
         quantise_h(0)
+        code_early = held("xm_code_early", [P, 3 * P], U32, slot="h_bf0")
+        xm_code.extend([code_early[:, k * P : (k + 1) * P] for k in range(3)])
         quantise_xm(1, xm_code[1])
         quantise_xm(2, xm_code[2])
 
@@ -323,8 +323,7 @@ def tile_attend_gkl_w_ts_kernel(tc, xT, w_words, w_scales, y, wt, ts, xm, offs, 
 
         dw_early = [held("dw_early0", [P, HALF], F32), fixed("dw_early1", [P, HALF], F32, 47 * KIB + 512)]
         first_bank = in_bank("first_bank", 7, [P, N])
-        nc.vector.tensor_copy(dw_early[0][:], multiply(0, halves[0], first_bank))
-        scatter(0, halves[0], dw_early[0][:])
+        first_product = multiply(0, halves[0], first_bank)
 
         share = held("share", [P, PACK, HALF], F32)
         for t in range(PACK):
@@ -333,22 +332,25 @@ def tile_attend_gkl_w_ts_kernel(tc, xT, w_words, w_scales, y, wt, ts, xm, offs, 
                 nc.tensor.matmul(
                     turned[b][:, t, :], share[:, t, b * P : (b + 1) * P], ident[:], start=False, stop=(t == PACK - 1), is_transpose=True
                 )
+        cast_xm(3)
+        quantise_xm(3, xm_code[3])
+        nc.scalar.copy(dw_early[0][:], first_product)
+        scatter(0, halves[0], dw_early[0][:])
         h_turned = fixed("h_turned", [P, turns, 2, P, 2], BF16, 48 * KIB)
-        back = in_bank("back", 7, [P, turns, 2, P])
+        back = in_bank("back", 6, [P, turns, 2, P])
         for b in range(turns):
             nc.scalar.activation(
                 h_turned[:, b], turned[b][:].rearrange("s (u e) p -> s u p e", e=2), ACT.Copy, scale=ts_late[:, b : b + 1]
             )
+        for b in range(turns):
             for u in range(2):
                 nc.tensor.transpose(back[:, b, u, :], h_turned[:, b, u].rearrange("s p e -> s (p e)").bitcast(F32), ident[:])
-        cast_xm(3)
-        quantise_xm(3, xm_code[3])
         nc.scalar.copy(
             h_bf[1][:].rearrange("p i t -> p (i t)").bitcast(F32).rearrange("p (b s u) -> p b s u", b=turns, u=2),
             back[:].rearrange("p b u s -> p b s u"),
         )
 
-        second_bank = in_bank("second_bank", 6, [P, N])
+        second_bank = in_bank("second_bank", 7, [P, N])
         second_product = multiply(1, halves[0], second_bank)
         quantise_h(1)
         nc.scalar.copy(dw_early[1][:], second_product)

@@ -21,7 +21,7 @@ P = 128
 PACK = 4
 PASSES = D // (P * PACK)
 BLOCKS = D // P
-WINDOWS = 3
+WINDOWS = 5
 HALF = N // 2
 EARLY = 2
 CAST_SPLIT = 96
@@ -33,7 +33,7 @@ def tile_attend_gkl_w_ts_kernel(tc, xT, w_words, w_scales, y, wt, ts, xm, offs, 
     with ExitStack() as ctx:
         keep = ctx.enter_context(tc.tile_pool(name="keep", bufs=1))
         placed = ctx.enter_context(tc.tile_pool(name="placed", bufs=1))
-        ring = ctx.enter_context(tc.tile_pool(name="ring", bufs=3))
+        ring = ctx.enter_context(tc.tile_pool(name="ring", bufs=1))
         psum = ctx.enter_context(tc.psum_pool(name="psum", bufs=1))
 
         def in_bank(name, k, shape):
@@ -64,8 +64,6 @@ def tile_attend_gkl_w_ts_kernel(tc, xT, w_words, w_scales, y, wt, ts, xm, offs, 
         nc.vector.memset(plane_first[:], 0)
         h_code = held("h_code", [P, N], U32)
         h_scale = held("h_scale", [P, N], U8)
-        nc.vector.memset(h_code[:, HALF:], 0)
-        nc.vector.memset(h_scale[:, HALF:].bitcast(I32), 0)
         first_window = held("window0", [P, T], F32)
         nc.vector.memset(first_window[:], 0.0)
         zeros = held("zeros", [P, P], F32, slot="window1")
@@ -206,6 +204,10 @@ def tile_attend_gkl_w_ts_kernel(tc, xT, w_words, w_scales, y, wt, ts, xm, offs, 
             nc.gpsimd.tensor_scalar(neg_target[:, t, :], y_sb[:, t, halves[1]], neg_wt[:, t : t + 1], 0.0, ALU.mult, ALU.add)
 
 
+        third_window = held("window2", [P, T], F32, slot="neg_wt")
+        for q in range(4):
+            nc.gpsimd.memset(third_window[:, q * N : (q + 1) * N], 0.0)
+
         turned = [in_bank("turned%d" % b, 5 + b, [P, PACK, P]) for b in range(turns)]
         for b in range(turns):
             for t in range(PACK):
@@ -248,13 +250,12 @@ def tile_attend_gkl_w_ts_kernel(tc, xT, w_words, w_scales, y, wt, ts, xm, offs, 
         subtract_targets(1)
         invert(slice(2, PACK))
 
-        groups = ((0, 1), (1, 2), (2, 3), (3, 4), (4, 8))
+        groups = ((0, 1), (1, 2), (2, 3), (3, 4))
         xm_bf = [
             fixed("xm_bf0", [P, PACK * P], BF16, 41 * KIB),
             held("xm_bf1", [P, PACK * P], BF16, slot="x_bf10"),
             held("xm_bf2", [P, PACK * P], BF16, slot="neg_a3"),
             held("xm_bf3", [P, PACK * P], BF16, slot="weight"),
-            fixed("xm_bf4", [P, PACK * PACK * P], BF16, 48 * KIB + 512),
         ]
         xm_scale = held("xm_scale", [P, D], U8)
         code_first = held("xm_code_first", [P, P], U32)
@@ -283,7 +284,7 @@ def tile_attend_gkl_w_ts_kernel(tc, xT, w_words, w_scales, y, wt, ts, xm, offs, 
         subtract_targets(2)
         subtract_targets(3)
 
-        h_bf = [held("h_bf%d" % k, [P, HALF, PACK], BF16) for k in range(2)]
+        h_bf = [held("h_bf0", [P, HALF, PACK], BF16), fixed("h_bf1", [P, HALF, PACK], BF16, 60 * KIB)]
 
         def quantise_h(k):
             nc.vector.quantize_mx(
@@ -309,20 +310,29 @@ def tile_attend_gkl_w_ts_kernel(tc, xT, w_words, w_scales, y, wt, ts, xm, offs, 
                 out=bank[:],
                 lhsT=xm_code[m].bitcast(E4M3),
                 lhsT_scale=xm_scale[:, m * P : (m + 1) * P],
-                rhs=h_code[:].bitcast(E5M2),
-                rhs_scale=h_scale[:],
+                rhs=h_code[:, s].bitcast(E5M2),
+                rhs_scale=h_scale[:, s],
                 start=True,
                 stop=True,
             )
-            return bank[:, s]
+            return bank[:]
 
-        windows = [first_window, second_window]
+        windows = [first_window, second_window, third_window]
 
         def scatter(m, s, dw):
-            nc.vector.tensor_copy(windows[m % WINDOWS][:].indirect(offsets[:, s.start // 16 : s.stop // 16]), dw)
+            window = windows[m % WINDOWS]
+            if m % 2 == 0:
+                nc.vector.tensor_copy(window[:].indirect(offsets[:, s.start // 16 : s.stop // 16]), dw)
+            else:
+                for lo in range(s.start, s.stop, HALF):
+                    nc.scalar.activation(
+                        window[:].indirect(offsets[:, lo // 16 : (lo + HALF) // 16]),
+                        dw[:, lo - s.start : lo - s.start + HALF],
+                        ACT.Copy,
+                    )
 
         dw_early = [held("dw_early0", [P, HALF], F32), fixed("dw_early1", [P, HALF], F32, 47 * KIB + 512)]
-        first_bank = in_bank("first_bank", 7, [P, N])
+        first_bank = in_bank("first_bank", 7, [P, HALF])
         first_product = multiply(0, halves[0], first_bank)
 
         share = held("share", [P, PACK, HALF], F32)
@@ -350,29 +360,55 @@ def tile_attend_gkl_w_ts_kernel(tc, xT, w_words, w_scales, y, wt, ts, xm, offs, 
             back[:].rearrange("p b u s -> p b s u"),
         )
 
-        second_bank = in_bank("second_bank", 7, [P, N])
+        second_bank = in_bank("second_bank", 7, [P, HALF])
         second_product = multiply(1, halves[0], second_bank)
         quantise_h(1)
         nc.scalar.copy(dw_early[1][:], second_product)
         scatter(1, halves[0], dw_early[1][:])
-        third_window = held("window2", [P, T], F32, slot="h_bf1")
-        nc.gpsimd.memset(third_window[:], 0.0)
-        windows.append(third_window)
+
+        windows.append(fixed("window3", [P, T], F32, 52 * KIB + 512))
+        nc.gpsimd.memset(windows[3][:], 0.0)
+
+        def cast_late(pair, staged):
+            for k in range(2):
+                u = 2 * pair + k
+                nc.gpsimd.tensor_scalar(
+                    staged[:, k * PACK * P : (k + 1) * PACK * P].rearrange("p (c j) -> p c j", j=PACK),
+                    xm_raw[2][:, :, u * P : (u + 1) * P].rearrange("p j c -> p c j"),
+                    1.0,
+                    0.0,
+                    ALU.mult,
+                    ALU.add,
+                )
+
+        def quantise_late(pair, staged):
+            code = held("xm_code_late%d" % pair, [P, 2 * P], U32)
+            lo = (4 + 2 * pair) * P
+            nc.vector.quantize_mx(out=code[:].bitcast(E4M3), scales=xm_scale[:, lo : lo + 2 * P], in_=staged[:])
+            xm_code.extend([code[:, k * P : (k + 1) * P] for k in range(2)])
+
+        staged_first = fixed("xm_late0", [P, 2 * PACK * P], BF16, 61 * KIB)
+        cast_late(0, staged_first)
 
         for m in range(BLOCKS):
-            if m == EARLY:
-                cast_xm(4)
-                code_late = held("xm_code_late", [P, D // 2], U32, slot="dw_first")
-                quantise_xm(4, code_late[:])
-                xm_code.extend([code_late[:, k * P : (k + 1) * P] for k in range(BLOCKS // 2)])
+            if m == 2:
+                windows.append(held("window4", [P, T], F32, slot="dw_first"))
+                nc.gpsimd.memset(windows[4][:], 0.0)
+            if m == 4:
+                quantise_late(0, staged_first)
+                staged_second = fixed("xm_late1", [P, 2 * PACK * P], BF16, 61 * KIB)
+                cast_late(1, staged_second)
+            if m == 6:
+                quantise_late(1, staged_second)
             s = halves[1] if m < EARLY else slice(0, N)
-            bank = multiply(m, s, in_bank("product%d" % m, (m + 1) % BLOCKS, [P, N]))
+            bank = multiply(m, s, in_bank("product%d" % m, (m + 1) % BLOCKS, [P, s.stop - s.start]))
             if m == 0:
-                dw = held("dw_first", [P, N], F32)
-            elif m == EARLY:
-                dw = fixed("dw_placed", [P, N], F32, 12 * KIB)
+                dw = held("dw_first", [P, HALF], F32)
             else:
-                dw = ring.tile([P, N], F32, name="dw")
-            nc.scalar.copy(dw[:, s], bank)
-            scatter(m, s, dw[:, s])
+                dw = ring.tile([P, s.stop - s.start], F32, name="dw%d" % m, tag="dw%d" % (m % 2))
+            if m % 2 == 0:
+                nc.vector.tensor_copy(dw[:], bank)
+            else:
+                nc.scalar.copy(dw[:], bank)
+            scatter(m, s, dw[:])
             nc.sync.dma_start(out[m * P : (m + 1) * P, :], windows[m % WINDOWS][:])

@@ -21,10 +21,8 @@ P = 128
 PACK = 4
 PASSES = D // (P * PACK)
 BLOCKS = D // P
-WINDOWS = 5
+WINDOWS = 4
 HALF = N // 2
-EARLY = 2
-CAST_SPLIT = 96
 KIB = 1024
 
 
@@ -33,7 +31,6 @@ def tile_attend_gkl_w_ts_kernel(tc, xT, w_words, w_scales, y, wt, ts, xm, offs, 
     with ExitStack() as ctx:
         keep = ctx.enter_context(tc.tile_pool(name="keep", bufs=1))
         placed = ctx.enter_context(tc.tile_pool(name="placed", bufs=1))
-        ring = ctx.enter_context(tc.tile_pool(name="ring", bufs=1))
         psum = ctx.enter_context(tc.psum_pool(name="psum", bufs=1))
 
         def in_bank(name, k, shape):
@@ -88,7 +85,7 @@ def tile_attend_gkl_w_ts_kernel(tc, xT, w_words, w_scales, y, wt, ts, xm, offs, 
         wt_sb = fixed("wt_sb", [P, PACK], F32, 24 * KIB)
         nc.sync.dma_start(wt_sb[:], wt[0].rearrange("(p t) o -> p (t o)", t=PACK))
 
-        ts_pool = held("ts_pool", [P, T], F32)
+        ts_pool = fixed("ts_pool", [P, T], F32, 33 * KIB)
         ts_view = ts_pool[:].rearrange("m (p c) -> m p c", p=P)
         for b in range(4):
             bank = in_bank("ts_spread%d" % b, PACK + b, [P, PACK, P])
@@ -111,7 +108,7 @@ def tile_attend_gkl_w_ts_kernel(tc, xT, w_words, w_scales, y, wt, ts, xm, offs, 
         )
 
         ts_sel = held("ts_sel", [P, N], F32)
-        nc.vector.tensor_copy(ts_sel[:], ts_pool[:].indirect(offsets[:]))
+        nc.scalar.activation(ts_sel[:], ts_pool[:].indirect(offsets[:]), ACT.Copy)
 
         xm_rows = xm[0].rearrange("(p j) d -> p j d", j=PACK)
         xm_spans = ((0, 2), (2, 4), (4, 8))
@@ -128,8 +125,8 @@ def tile_attend_gkl_w_ts_kernel(tc, xT, w_words, w_scales, y, wt, ts, xm, offs, 
 
         x_bf = {
             (0, 0): held("x_bf00", [P, 2 * P * PACK], BF16),
-            (0, 1): held("x_bf01", [P, 2 * P * PACK], BF16, slot="ts_cols"),
-            (1, 0): held("x_bf10", [P, 2 * P * PACK], BF16),
+            (0, 1): held("x_bf01", [P, 2 * P * PACK], BF16),
+            (1, 0): held("x_bf10", [P, 2 * P * PACK], BF16, slot="x_bf01"),
             (1, 1): fixed("x_bf11", [P, 2 * P * PACK], BF16, 40 * KIB),
         }
         x_code = {key: held("x_code%d%d" % key, [P, 2 * P], U32) for key in x_bf}
@@ -165,14 +162,13 @@ def tile_attend_gkl_w_ts_kernel(tc, xT, w_words, w_scales, y, wt, ts, xm, offs, 
             )
 
         for u in range(2):
-            cast_x(0, u, x_first, 0, P, u == 0)
+            cast_x(0, u, x_first, 0, P, True)
         y_sb = fixed("y_sb", [P, PACK, N], F32, 85 * KIB + 512)
         load_xm(0)
         nc.sync.dma_start(y_sb[:], y[0].rearrange("(p t) i -> p t i", t=PACK))
         quantise_x(0, 0, 0, 2 * P)
         quantise_x(0, 1, 0, 2 * P)
-        cast_x(1, 0, x_second, 0, CAST_SPLIT, True)
-        cast_x(1, 0, x_second, CAST_SPLIT, P, False)
+        cast_x(1, 0, x_second, 0, P, True)
         cast_x(1, 1, x_second, 0, P, False)
         load_xm(1)
         load_xm(2)
@@ -183,8 +179,6 @@ def tile_attend_gkl_w_ts_kernel(tc, xT, w_words, w_scales, y, wt, ts, xm, offs, 
             for t in range(PACK):
                 score_pass(t, o)
 
-        neg_a = [held("neg_a%d" % t, [P, N], F32) for t in range(PACK)]
-
         halves = [slice(0, HALF), slice(HALF, N)]
         turns = HALF // P
 
@@ -192,7 +186,9 @@ def tile_attend_gkl_w_ts_kernel(tc, xT, w_words, w_scales, y, wt, ts, xm, offs, 
         for b in range(turns):
             nc.tensor.transpose(ts_bank[:, b, :], ts_sel[:, HALF + b * P : HALF + (b + 1) * P], ident[:])
         ts_late = held("ts_late", [P, turns], F32)
-        wt_ts = fixed("wt_ts", [P, PACK, HALF], F32, 37 * KIB)
+        nc.scalar.copy(ts_late[:], ts_bank[:, :, 0])
+
+        wt_ts = fixed("wt_ts", [P, PACK, HALF], F32, 36 * KIB + 512)
         for t in range(2):
             nc.gpsimd.tensor_scalar(wt_ts[:, t, :], ts_sel[:, halves[0]], wt_sb[:, t : t + 1], 0.0, ALU.mult, ALU.add)
         for t in range(2, PACK):
@@ -203,23 +199,30 @@ def tile_attend_gkl_w_ts_kernel(tc, xT, w_words, w_scales, y, wt, ts, xm, offs, 
         for t in range(PACK):
             nc.gpsimd.tensor_scalar(neg_target[:, t, :], y_sb[:, t, halves[1]], neg_wt[:, t : t + 1], 0.0, ALU.mult, ALU.add)
 
-
         third_window = held("window2", [P, T], F32, slot="neg_wt")
-        for q in range(4):
+        for q in range(T // N):
             nc.gpsimd.memset(third_window[:, q * N : (q + 1) * N], 0.0)
 
-        turned = [in_bank("turned%d" % b, 5 + b, [P, PACK, P]) for b in range(turns)]
-        for b in range(turns):
-            for t in range(PACK):
+        turned = [in_bank("turned%d" % u, 5 + u, [P, turns, 2, P]) for u in range(2)]
+        for t in range(PACK):
+            for b in range(turns):
                 nc.tensor.matmul(
-                    turned[b][:, t, :], neg_target[:, t, b * P : (b + 1) * P], ident[:], start=(t == 0), stop=False, is_transpose=True
+                    turned[t // 2][:, b, t % 2, :],
+                    neg_target[:, t, b * P : (b + 1) * P],
+                    ident[:],
+                    start=(t % 2 == 0 and b == 0),
+                    stop=False,
+                    is_transpose=True,
                 )
 
+        neg_a = [held("neg_a%d" % t, [P, N], F32) for t in range(PACK)]
         neg_max = [held("neg_max%d" % t, [P, 1], F32) for t in range(PACK)]
-        e = [held("e%d" % t, [P, N], F32) for t in range(PACK)]
+        e = [held("e%d" % t, [P, N], F32, slot="weight0" if t == 2 else None) for t in range(PACK)]
         total = held("total", [P, PACK], F32)
-        inv = held("inv", [P, PACK], F32)
+        inv = [held("inv%d" % t, [P, 1], F32) for t in range(PACK)]
+        weight = [held("weight%d" % t, [P, 1], F32) for t in range(PACK)]
         g = held("g", [P, PACK, HALF], F32)
+        share = held("share", [P, PACK, HALF], F32)
 
         def scale_scores(t):
             nc.vector.scalar_tensor_tensor(neg_a[t][:], scores[t][:], -1.0, ts_sel[:], ALU.mult, ALU.mult)
@@ -228,61 +231,76 @@ def tile_attend_gkl_w_ts_kernel(tc, xT, w_words, w_scales, y, wt, ts, xm, offs, 
             nc.vector.tensor_reduce(neg_max[t][:], neg_a[t][:], mybir.AxisListType.X, ALU.min)
             nc.scalar.activation(e[t][:], neg_a[t][:], ACT.Exp, bias=neg_max[t][:], scale=-1.0, accum_out=total[:, t : t + 1])
 
-        def invert(cols):
-            nc.vector.reciprocal(inv[:, cols], total[:, cols])
+        def invert(t):
+            nc.vector.reciprocal(inv[t][:], total[:, t : t + 1])
 
-        scale_scores(0)
-        for t in range(PACK):
-            if t + 1 < PACK:
-                scale_scores(t + 1)
-            else:
-                invert(slice(0, 2))
-            exponentiate(t)
-
-        nc.scalar.copy(ts_late[:], ts_bank[:, :, 0])
+        def weigh(t):
+            nc.vector.tensor_tensor(weight[t][:], inv[t][:], wt_sb[:, t : t + 1], ALU.mult)
 
         def subtract_targets(t):
             nc.vector.scalar_tensor_tensor(
-                g[:, t, :], e[t][:, halves[0]], inv[:, t : t + 1], y_sb[:, t, halves[0]], ALU.mult, ALU.subtract
+                g[:, t, :], e[t][:, halves[0]], inv[t][:], y_sb[:, t, halves[0]], ALU.mult, ALU.subtract
             )
 
-        subtract_targets(0)
-        subtract_targets(1)
-        invert(slice(2, PACK))
-
-        groups = ((0, 1), (1, 2), (2, 3), (3, 4))
-        xm_bf = [
-            fixed("xm_bf0", [P, PACK * P], BF16, 41 * KIB),
-            held("xm_bf1", [P, PACK * P], BF16, slot="x_bf10"),
-            held("xm_bf2", [P, PACK * P], BF16, slot="neg_a3"),
-            held("xm_bf3", [P, PACK * P], BF16, slot="weight"),
-        ]
-        xm_scale = held("xm_scale", [P, D], U8)
-        code_first = held("xm_code_first", [P, P], U32)
-        xm_code = [code_first[:]]
-
-        def cast_xm(k):
-            lo, hi = groups[k]
-            for m in range(lo, hi):
-                c = min(m // 2, 2)
-                u = m - xm_spans[c][0]
-                nc.scalar.copy(
-                    xm_bf[k][:, (m - lo) * PACK * P : (m - lo + 1) * PACK * P].rearrange("p (c i j) -> p c j i", i=4, j=PACK),
-                    xm_raw[c][:, :, u * P : (u + 1) * P].rearrange("p j (c i) -> p c j i", i=4),
+        def add_share(t):
+            nc.scalar.activation(share[:, t, :], e[t][:, halves[1]], ACT.Copy, scale=weight[t][:])
+            for b in range(turns):
+                nc.tensor.matmul(
+                    turned[t // 2][:, b, t % 2, :],
+                    share[:, t, b * P : (b + 1) * P],
+                    ident[:],
+                    start=False,
+                    stop=(t % 2 == 1 and b == turns - 1),
+                    is_transpose=True,
                 )
 
-        def quantise_xm(k, code):
-            lo, hi = groups[k]
-            nc.vector.quantize_mx(out=code.bitcast(E4M3), scales=xm_scale[:, lo * P : hi * P], in_=xm_bf[k][:])
+        scale_scores(0)
+        scale_scores(1)
+        exponentiate(0)
+        scale_scores(2)
+        exponentiate(1)
+        invert(0)
+        scale_scores(3)
+        weigh(0)
+        add_share(0)
+        exponentiate(2)
+        invert(1)
+        exponentiate(3)
+        weigh(1)
+        invert(2)
+        subtract_targets(0)
+        weigh(2)
 
-        cast_xm(0)
-        cast_xm(1)
-        cast_xm(2)
-        quantise_xm(0, xm_code[0])
-        weight = held("weight", [P, PACK], F32)
-        nc.vector.tensor_tensor(weight[:], inv[:], wt_sb[:], ALU.mult)
+        xm_scale = held("xm_scale", [P, D], U8)
+        xm_code = []
+
+        def cast_xm(m, staged):
+            c, u = divmod(m, 2)
+            copy = nc.scalar.copy if c == 0 else nc.vector.tensor_copy
+            copy(
+                staged.rearrange("p (c i j) -> p c j i", i=4, j=PACK),
+                xm_raw[c][:, :, u * P : (u + 1) * P].rearrange("p j (c i) -> p c j i", i=4),
+            )
+
+        def quantise_xm(lo, hi, staged, slot=None, at=None):
+            if at is None:
+                code = held("xm_code%d" % lo, [P, (hi - lo) * P], U32, slot=slot)
+            else:
+                code = fixed("xm_code%d" % lo, [P, (hi - lo) * P], U32, at)
+            nc.vector.quantize_mx(out=code[:].bitcast(E4M3), scales=xm_scale[:, lo * P : hi * P], in_=staged[:])
+            xm_code.extend([code[:, k * P : (k + 1) * P] for k in range(hi - lo)])
+
+        xm_first = [fixed("xm_first%d" % m, [P, PACK * P], BF16, 40 * KIB + 512 + KIB * m) for m in range(2)]
+        for m in range(2):
+            cast_xm(m, xm_first[m][:])
+        quantise_xm(0, 1, xm_first[0], slot="inv0")
+        invert(3)
+        subtract_targets(1)
+        weigh(3)
         subtract_targets(2)
         subtract_targets(3)
+        for t in range(1, PACK):
+            add_share(t)
 
         h_bf = [held("h_bf0", [P, HALF, PACK], BF16), fixed("h_bf1", [P, HALF, PACK], BF16, 60 * KIB)]
 
@@ -299,15 +317,24 @@ def tile_attend_gkl_w_ts_kernel(tc, xT, w_words, w_scales, y, wt, ts, xm, offs, 
             wt_ts[:].rearrange("p t (c i) -> p c t i", i=2),
             ALU.mult,
         )
+        quantise_xm(1, 2, xm_first[1], slot="inv3")
         quantise_h(0)
-        code_early = held("xm_code_early", [P, 3 * P], U32, slot="h_bf0")
-        xm_code.extend([code_early[:, k * P : (k + 1) * P] for k in range(3)])
-        quantise_xm(1, xm_code[1])
-        quantise_xm(2, xm_code[2])
 
-        def multiply(m, s, bank):
+        h_turned = [held("h_turned%d" % b, [P, 2, P, 2], BF16) for b in range(turns)]
+        back = [in_bank("back%d" % b, b, [P, 2, P]) for b in range(turns)]
+        for u in range(2):
+            for b in range(turns):
+                nc.scalar.activation(
+                    h_turned[b][:, u], turned[u][:, b].rearrange("s e p -> s p e"), ACT.Copy, scale=ts_late[:, b : b + 1]
+                )
+                nc.tensor.transpose(back[b][:, u, :], h_turned[b][:, u].rearrange("s p e -> s (p e)").bitcast(F32), ident[:])
+        h_words = h_bf[1][:].rearrange("p i t -> p (i t)").bitcast(F32).rearrange("p (b s u) -> p b s u", b=turns, u=2)
+        for b in range(turns):
+            nc.scalar.copy(h_words[:, b], back[b][:].rearrange("p u s -> p s u"))
+
+        def multiply(m, s, product):
             nc.tensor.matmul_mx(
-                out=bank[:],
+                out=product,
                 lhsT=xm_code[m].bitcast(E4M3),
                 lhsT_scale=xm_scale[:, m * P : (m + 1) * P],
                 rhs=h_code[:, s].bitcast(E5M2),
@@ -315,13 +342,12 @@ def tile_attend_gkl_w_ts_kernel(tc, xT, w_words, w_scales, y, wt, ts, xm, offs, 
                 start=True,
                 stop=True,
             )
-            return bank[:]
 
         windows = [first_window, second_window, third_window]
 
         def scatter(m, s, dw):
             window = windows[m % WINDOWS]
-            if m % 2 == 0:
+            if m % 2 == 1:
                 nc.vector.tensor_copy(window[:].indirect(offsets[:, s.start // 16 : s.stop // 16]), dw)
             else:
                 for lo in range(s.start, s.stop, HALF):
@@ -331,43 +357,13 @@ def tile_attend_gkl_w_ts_kernel(tc, xT, w_words, w_scales, y, wt, ts, xm, offs, 
                         ACT.Copy,
                     )
 
-        dw_early = [held("dw_early0", [P, HALF], F32), fixed("dw_early1", [P, HALF], F32, 47 * KIB + 512)]
-        first_bank = in_bank("first_bank", 7, [P, HALF])
-        first_product = multiply(0, halves[0], first_bank)
+        def store(m):
+            nc.sync.dma_start(out[m * P : (m + 1) * P, :], windows[m % WINDOWS][:])
 
-        share = held("share", [P, PACK, HALF], F32)
-        for t in range(PACK):
-            nc.scalar.activation(share[:, t, :], e[t][:, halves[1]], ACT.Copy, scale=weight[:, t : t + 1])
-            for b in range(turns):
-                nc.tensor.matmul(
-                    turned[b][:, t, :], share[:, t, b * P : (b + 1) * P], ident[:], start=False, stop=(t == PACK - 1), is_transpose=True
-                )
-        cast_xm(3)
-        quantise_xm(3, xm_code[3])
-        nc.scalar.copy(dw_early[0][:], first_product)
-        scatter(0, halves[0], dw_early[0][:])
-        h_turned = fixed("h_turned", [P, turns, 2, P, 2], BF16, 48 * KIB)
-        back = in_bank("back", 6, [P, turns, 2, P])
-        for b in range(turns):
-            nc.scalar.activation(
-                h_turned[:, b], turned[b][:].rearrange("s (u e) p -> s u p e", e=2), ACT.Copy, scale=ts_late[:, b : b + 1]
-            )
-        for b in range(turns):
-            for u in range(2):
-                nc.tensor.transpose(back[:, b, u, :], h_turned[:, b, u].rearrange("s p e -> s (p e)").bitcast(F32), ident[:])
-        nc.scalar.copy(
-            h_bf[1][:].rearrange("p i t -> p (i t)").bitcast(F32).rearrange("p (b s u) -> p b s u", b=turns, u=2),
-            back[:].rearrange("p b u s -> p b s u"),
-        )
-
-        second_bank = in_bank("second_bank", 7, [P, HALF])
-        second_product = multiply(1, halves[0], second_bank)
-        quantise_h(1)
-        nc.scalar.copy(dw_early[1][:], second_product)
-        scatter(1, halves[0], dw_early[1][:])
-
-        windows.append(fixed("window3", [P, T], F32, 52 * KIB + 512))
-        nc.gpsimd.memset(windows[3][:], 0.0)
+        def zero(window):
+            for q in range(T // N):
+                nc.gpsimd.memset(window[:, q * N : (q + 1) * N], 0.0)
+            windows.append(window)
 
         def cast_late(pair, staged):
             for k in range(2):
@@ -381,34 +377,47 @@ def tile_attend_gkl_w_ts_kernel(tc, xT, w_words, w_scales, y, wt, ts, xm, offs, 
                     ALU.add,
                 )
 
-        def quantise_late(pair, staged):
-            code = held("xm_code_late%d" % pair, [P, 2 * P], U32)
-            lo = (4 + 2 * pair) * P
-            nc.vector.quantize_mx(out=code[:].bitcast(E4M3), scales=xm_scale[:, lo : lo + 2 * P], in_=staged[:])
-            xm_code.extend([code[:, k * P : (k + 1) * P] for k in range(2)])
+        first_bank = in_bank("first_bank", 2, [P, HALF])
+        multiply(0, halves[0], first_bank[:])
+        dw_first = held("dw_first", [P, HALF], F32, slot="h_turned1")
+        nc.vector.tensor_copy(dw_first[:], first_bank[:])
+        scatter(0, halves[0], dw_first[:])
+        xm_third = held("xm_third", [P, PACK * P], BF16, slot="h_bf0")
+        cast_xm(2, xm_third[:])
+        quantise_h(1)
 
-        staged_first = fixed("xm_late0", [P, 2 * PACK * P], BF16, 61 * KIB)
-        cast_late(0, staged_first)
+        pair_bank = in_bank("pair_bank", 3, [P, N])
+        multiply(0, halves[1], pair_bank[:, halves[0]])
+        multiply(1, halves[0], pair_bank[:, halves[1]])
+        dw_pair = [held("dw_pair%d" % m, [P, HALF], F32, slot="dw%d" % m) for m in range(2)]
+        for m in range(2):
+            nc.vector.tensor_copy(dw_pair[m][:], pair_bank[:, halves[m]])
+        scatter(0, halves[1], dw_pair[0][:])
+        store(0)
+        quantise_xm(2, 3, xm_third, at=60 * KIB)
+        xm_fourth = fixed("xm_fourth", [P, PACK * P], BF16, 61 * KIB)
+        cast_xm(3, xm_fourth[:])
+        quantise_xm(3, 4, xm_fourth)
+        scatter(1, halves[0], dw_pair[1][:])
 
-        for m in range(BLOCKS):
-            if m == 2:
-                windows.append(held("window4", [P, T], F32, slot="dw_first"))
-                nc.gpsimd.memset(windows[4][:], 0.0)
+        staged = fixed("xm_late0", [P, 2 * PACK * P], BF16, 61 * KIB)
+        cast_late(0, staged)
+        zero(held("window3", [P, T], F32, slot="h_turned1"))
+
+        for m in range(1, BLOCKS):
             if m == 4:
-                quantise_late(0, staged_first)
-                staged_second = fixed("xm_late1", [P, 2 * PACK * P], BF16, 61 * KIB)
-                cast_late(1, staged_second)
+                quantise_xm(4, 6, staged)
+                staged = fixed("xm_late1", [P, 2 * PACK * P], BF16, 61 * KIB)
+                cast_late(1, staged)
             if m == 6:
-                quantise_late(1, staged_second)
-            s = halves[1] if m < EARLY else slice(0, N)
-            bank = multiply(m, s, in_bank("product%d" % m, (m + 1) % BLOCKS, [P, s.stop - s.start]))
-            if m == 0:
-                dw = held("dw_first", [P, HALF], F32)
+                quantise_xm(6, 8, staged)
+            s = halves[1] if m == 1 else slice(0, N)
+            bank = in_bank("product%d" % m, (4, 7, 5, 6, 0, 1, 2)[m - 1], [P, s.stop - s.start])
+            multiply(m, s, bank[:])
+            dw = held("dw_block%d" % m, [P, s.stop - s.start], F32, slot="dw%d" % (m % 2))
+            if m % 2 == 1:
+                nc.vector.tensor_copy(dw[:], bank[:])
             else:
-                dw = ring.tile([P, s.stop - s.start], F32, name="dw%d" % m, tag="dw%d" % (m % 2))
-            if m % 2 == 0:
-                nc.vector.tensor_copy(dw[:], bank)
-            else:
-                nc.scalar.copy(dw[:], bank)
+                nc.scalar.copy(dw[:], bank[:])
             scatter(m, s, dw[:])
-            nc.sync.dma_start(out[m * P : (m + 1) * P, :], windows[m % WINDOWS][:])
+            store(m)

@@ -111,11 +111,12 @@ def tile_attend_gkl_w_ts_kernel(tc, xT, w_words, w_scales, y, wt, ts, xm, offs, 
         nc.scalar.activation(ts_sel[:], ts_pool[:].indirect(offsets[:]), ACT.Copy)
 
         xm_rows = xm[0].rearrange("(p j) d -> p j d", j=PACK)
-        xm_spans = ((0, 2), (2, 4), (4, 8))
+        xm_spans = ((0, 2), (2, 4), (4, 6), (6, 8))
         xm_raw = [
             fixed("xm_raw0", [P, PACK, 2 * P], F32, 80 * KIB + 512),
             fixed("xm_raw1", [P, PACK, 2 * P], F32, 20 * KIB),
-            fixed("xm_raw2", [P, PACK, 4 * P], F32, 12 * KIB),
+            fixed("xm_raw2", [P, PACK, 2 * P], F32, 16 * KIB),
+            fixed("xm_raw3", [P, PACK, 2 * P], F32, 68 * KIB),
         ]
 
         def load_xm(c):
@@ -147,7 +148,7 @@ def tile_attend_gkl_w_ts_kernel(tc, xT, w_words, w_scales, y, wt, ts, xm, offs, 
                 in_=x_bf[o, u][:, PACK * lo : PACK * hi],
             )
 
-        scores = [in_bank("scores%d" % t, t, [P, N]) for t in range(PACK)]
+        scores = [in_bank("scores%d" % t, t, [P, N]) for t in range(PACK - 1)]
 
         def score_pass(t, o):
             u, k = divmod(t, 2)
@@ -172,34 +173,54 @@ def tile_attend_gkl_w_ts_kernel(tc, xT, w_words, w_scales, y, wt, ts, xm, offs, 
         cast_x(1, 1, x_second, 0, P, False)
         load_xm(1)
         load_xm(2)
+        load_xm(3)
         quantise_x(1, 0, 0, P)
         quantise_x(1, 0, P, 2 * P)
         quantise_x(1, 1, 0, 2 * P)
         for o in range(PASSES):
-            for t in range(PACK):
+            for t in range(PACK - 1):
                 score_pass(t, o)
+        by_slot = [in_bank("by_slot%d" % h, 5 + h, [P, 2, P]) for h in range(2)]
+        for c in range(PACK):
+            for o in range(PASSES):
+                nc.tensor.matmul_mx(
+                    out=by_slot[c // 2][:, c % 2, :],
+                    lhsT=w_code[:, o * 2 * N + 2 * c * P : o * 2 * N + 2 * (c + 1) * P].bitcast(E2M1),
+                    lhsT_scale=w_scale[o][:, c * P : (c + 1) * P],
+                    rhs=x_code[o, 1][:, P:].bitcast(E4M3),
+                    rhs_scale=x_scale[o, 1][:, P:],
+                    start=(o == 0),
+                    stop=(o == PASSES - 1),
+                )
 
         halves = [slice(0, HALF), slice(HALF, N)]
-        turns = HALF // P
+        turns = 1
+        direct = slice(0, N - P)
+        third = slice(HALF, N - P)
+        aside = slice(N - P, N)
 
-        ts_bank = in_bank("ts_bank", 4, [P, turns, P])
-        for b in range(turns):
-            nc.tensor.transpose(ts_bank[:, b, :], ts_sel[:, HALF + b * P : HALF + (b + 1) * P], ident[:])
-        ts_late = held("ts_late", [P, turns], F32)
-        nc.scalar.copy(ts_late[:], ts_bank[:, :, 0])
+        ts_bank = in_bank("ts_bank", 4, [P, PACK, P])
+        for c in range(PACK):
+            nc.tensor.transpose(ts_bank[:, c, :], ts_sel[:, c * P : (c + 1) * P], ident[:])
+        ts_slot = fixed("ts_slot", [P, 32], F32, 10 * KIB)
+        nc.scalar.copy(ts_slot[:, 0:PACK], ts_bank[:, :, 0])
 
-        wt_ts = fixed("wt_ts", [P, PACK, HALF], F32, 36 * KIB + 512)
-        for t in range(2):
-            nc.gpsimd.tensor_scalar(wt_ts[:, t, :], ts_sel[:, halves[0]], wt_sb[:, t : t + 1], 0.0, ALU.mult, ALU.add)
-        for t in range(2, PACK):
-            nc.scalar.activation(wt_ts[:, t, :], ts_sel[:, halves[0]], ACT.Copy, scale=wt_sb[:, t : t + 1])
+        last_by_slot = held("last_by_slot", [P, PACK, P], F32)
+        last_scores = in_bank("last_scores", 7, [P, N])
+        for c in range(PACK):
+            nc.scalar.activation(last_by_slot[:, c, :], by_slot[c // 2][:, c % 2, :], ACT.Copy, scale=ts_slot[:, c : c + 1])
+        for c in range(PACK):
+            nc.tensor.transpose(last_scores[:, c * P : (c + 1) * P], last_by_slot[:, c, :], ident[:])
+
+        wt_ts = fixed("wt_ts", [P, PACK, N - P], F32, 34 * KIB + 512)
+        for t in range(PACK):
+            nc.gpsimd.tensor_scalar(wt_ts[:, t, :], ts_sel[:, direct], wt_sb[:, t : t + 1], 0.0, ALU.mult, ALU.add)
+        third_window = fixed("window2", [P, T], F32, 41 * KIB)
         neg_wt = held("neg_wt", [P, PACK], F32)
         nc.gpsimd.tensor_scalar(neg_wt[:], wt_sb[:], -1.0, 0.0, ALU.mult, ALU.add)
-        neg_target = held("neg_target", [P, PACK, HALF], F32)
+        neg_target = held("neg_target", [P, PACK, P], F32)
         for t in range(PACK):
-            nc.gpsimd.tensor_scalar(neg_target[:, t, :], y_sb[:, t, halves[1]], neg_wt[:, t : t + 1], 0.0, ALU.mult, ALU.add)
-
-        third_window = held("window2", [P, T], F32, slot="neg_wt")
+            nc.gpsimd.tensor_scalar(neg_target[:, t, :], y_sb[:, t, aside], neg_wt[:, t : t + 1], 0.0, ALU.mult, ALU.add)
         for q in range(T // N):
             nc.gpsimd.memset(third_window[:, q * N : (q + 1) * N], 0.0)
 
@@ -215,27 +236,33 @@ def tile_attend_gkl_w_ts_kernel(tc, xT, w_words, w_scales, y, wt, ts, xm, offs, 
                     is_transpose=True,
                 )
 
-        neg_a = [held("neg_a%d" % t, [P, N], F32) for t in range(PACK)]
+        neg_a = [held("neg_a%d" % t, [P, N], F32) for t in range(PACK - 1)]
         neg_max = [held("neg_max%d" % t, [P, 1], F32) for t in range(PACK)]
-        e = [held("e%d" % t, [P, N], F32, slot="weight0" if t == 2 else None) for t in range(PACK)]
+        e = [held("e%d" % t, [P, N], F32) if t != 1 else fixed("e1", [P, N], F32, 81 * KIB) for t in range(PACK)]
         total = held("total", [P, PACK], F32)
-        inv = [held("inv%d" % t, [P, 1], F32) for t in range(PACK)]
-        weight = [held("weight%d" % t, [P, 1], F32) for t in range(PACK)]
+        inv_first = held("inv0", [P, 2], F32)
+        inv = [inv_first[:, 0:1], inv_first[:, 1:2], held("inv2", [P, 1], F32), held("inv3", [P, 1], F32)]
+        weight = held("weight", [P, PACK], F32)
         g = held("g", [P, PACK, HALF], F32)
-        share = held("share", [P, PACK, HALF], F32)
+        g_third = held("g_third", [P, PACK, P], F32)
+        share = held("share", [P, PACK, P], F32)
 
         def scale_scores(t):
             nc.vector.scalar_tensor_tensor(neg_a[t][:], scores[t][:], -1.0, ts_sel[:], ALU.mult, ALU.mult)
 
         def exponentiate(t):
-            nc.vector.tensor_reduce(neg_max[t][:], neg_a[t][:], mybir.AxisListType.X, ALU.min)
-            nc.scalar.activation(e[t][:], neg_a[t][:], ACT.Exp, bias=neg_max[t][:], scale=-1.0, accum_out=total[:, t : t + 1])
+            if t < PACK - 1:
+                nc.vector.tensor_reduce(neg_max[t][:], neg_a[t][:], mybir.AxisListType.X, ALU.min)
+                nc.scalar.activation(e[t][:], neg_a[t][:], ACT.Exp, bias=neg_max[t][:], scale=-1.0, accum_out=total[:, t : t + 1])
+            else:
+                nc.vector.tensor_reduce(neg_max[t][:], last_scores[:], mybir.AxisListType.X, ALU.max, negate=True)
+                nc.scalar.activation(e[t][:], last_scores[:], ACT.Exp, bias=neg_max[t][:], accum_out=total[:, t : t + 1])
 
         def invert(t):
             nc.vector.reciprocal(inv[t][:], total[:, t : t + 1])
 
         def weigh(t):
-            nc.vector.tensor_tensor(weight[t][:], inv[t][:], wt_sb[:, t : t + 1], ALU.mult)
+            nc.vector.tensor_tensor(weight[:, t : t + 1], inv[t][:], wt_sb[:, t : t + 1], ALU.mult)
 
         def subtract_targets(t):
             nc.vector.scalar_tensor_tensor(
@@ -243,7 +270,7 @@ def tile_attend_gkl_w_ts_kernel(tc, xT, w_words, w_scales, y, wt, ts, xm, offs, 
             )
 
         def add_share(t):
-            nc.scalar.activation(share[:, t, :], e[t][:, halves[1]], ACT.Copy, scale=weight[t][:])
+            nc.scalar.activation(share[:, t, :], e[t][:, aside], ACT.Copy, scale=weight[:, t : t + 1])
             for b in range(turns):
                 nc.tensor.matmul(
                     turned[t // 2][:, b, t % 2, :],
@@ -254,29 +281,12 @@ def tile_attend_gkl_w_ts_kernel(tc, xT, w_words, w_scales, y, wt, ts, xm, offs, 
                     is_transpose=True,
                 )
 
-        scale_scores(0)
-        scale_scores(1)
-        exponentiate(0)
-        scale_scores(2)
-        exponentiate(1)
-        invert(0)
-        scale_scores(3)
-        weigh(0)
-        add_share(0)
-        exponentiate(2)
-        invert(1)
-        exponentiate(3)
-        weigh(1)
-        invert(2)
-        subtract_targets(0)
-        weigh(2)
-
         xm_scale = held("xm_scale", [P, D], U8)
         xm_code = []
 
         def cast_xm(m, staged):
             c, u = divmod(m, 2)
-            copy = nc.scalar.copy if c == 0 else nc.vector.tensor_copy
+            copy = nc.scalar.copy if m < 3 else nc.vector.tensor_copy
             copy(
                 staged.rearrange("p (c i j) -> p c j i", i=4, j=PACK),
                 xm_raw[c][:, :, u * P : (u + 1) * P].rearrange("p j (c i) -> p c j i", i=4),
@@ -290,19 +300,34 @@ def tile_attend_gkl_w_ts_kernel(tc, xT, w_words, w_scales, y, wt, ts, xm, offs, 
             nc.vector.quantize_mx(out=code[:].bitcast(E4M3), scales=xm_scale[:, lo * P : hi * P], in_=staged[:])
             xm_code.extend([code[:, k * P : (k + 1) * P] for k in range(hi - lo)])
 
-        xm_first = [fixed("xm_first%d" % m, [P, PACK * P], BF16, 40 * KIB + 512 + KIB * m) for m in range(2)]
+        xm_pair = held("xm_pair", [P, 2 * PACK * P], BF16, slot="x_bf01")
+        xm_first = [xm_pair[:, m * PACK * P : (m + 1) * PACK * P] for m in range(2)]
         for m in range(2):
             cast_xm(m, xm_first[m][:])
-        quantise_xm(0, 1, xm_first[0], slot="inv0")
+
+        scale_scores(0)
+        scale_scores(1)
+        exponentiate(0)
+        scale_scores(2)
+        exponentiate(1)
+        exponentiate(2)
+        nc.vector.reciprocal(inv_first[:], total[:, 0:2])
+        exponentiate(3)
+        nc.vector.tensor_tensor(weight[:, 0:2], inv_first[:], wt_sb[:, 0:2], ALU.mult)
+        invert(2)
+        subtract_targets(0)
+        weigh(2)
+
         invert(3)
+        quantise_xm(0, 1, xm_first[0], slot="neg_max3")
         subtract_targets(1)
         weigh(3)
         subtract_targets(2)
         subtract_targets(3)
-        for t in range(1, PACK):
+        for t in range(PACK):
             add_share(t)
 
-        h_bf = [held("h_bf0", [P, HALF, PACK], BF16), fixed("h_bf1", [P, HALF, PACK], BF16, 60 * KIB)]
+        h_bf = [fixed("h_bf0", [P, HALF, PACK], BF16, 59 * KIB), fixed("h_bf1", [P, HALF, PACK], BF16, 60 * KIB)]
 
         def quantise_h(k):
             nc.vector.quantize_mx(
@@ -314,23 +339,34 @@ def tile_attend_gkl_w_ts_kernel(tc, xT, w_words, w_scales, y, wt, ts, xm, offs, 
         nc.vector.tensor_tensor(
             h_bf[0][:].rearrange("p (c i) t -> p c t i", i=2),
             g[:].rearrange("p t (c i) -> p c t i", i=2),
-            wt_ts[:].rearrange("p t (c i) -> p c t i", i=2),
+            wt_ts[:, :, halves[0]].rearrange("p t (c i) -> p c t i", i=2),
             ALU.mult,
         )
-        quantise_xm(1, 2, xm_first[1], slot="inv3")
+        quantise_xm(1, 2, xm_first[1], slot="total")
         quantise_h(0)
 
-        h_turned = [held("h_turned%d" % b, [P, 2, P, 2], BF16) for b in range(turns)]
+        for t in range(PACK):
+            nc.vector.scalar_tensor_tensor(
+                g_third[:, t, :], e[t][:, third], inv[t][:], y_sb[:, t, third], ALU.mult, ALU.subtract
+            )
+        nc.vector.tensor_tensor(
+            h_bf[1][:, 0:P, :].rearrange("p (c i) t -> p c t i", i=2),
+            g_third[:].rearrange("p t (c i) -> p c t i", i=2),
+            wt_ts[:, :, third].rearrange("p t (c i) -> p c t i", i=2),
+            ALU.mult,
+        )
+
+        h_turned = [held("h_turned%d" % b, [P, 2, P, 2], BF16, slot="weight") for b in range(turns)]
         back = [in_bank("back%d" % b, b, [P, 2, P]) for b in range(turns)]
         for u in range(2):
             for b in range(turns):
                 nc.scalar.activation(
-                    h_turned[b][:, u], turned[u][:, b].rearrange("s e p -> s p e"), ACT.Copy, scale=ts_late[:, b : b + 1]
+                    h_turned[b][:, u], turned[u][:, b].rearrange("s e p -> s p e"), ACT.Copy, scale=ts_slot[:, PACK - 1 : PACK]
                 )
                 nc.tensor.transpose(back[b][:, u, :], h_turned[b][:, u].rearrange("s p e -> s (p e)").bitcast(F32), ident[:])
-        h_words = h_bf[1][:].rearrange("p i t -> p (i t)").bitcast(F32).rearrange("p (b s u) -> p b s u", b=turns, u=2)
+        h_words = h_bf[1][:, P:, :].rearrange("p i t -> p (i t)").bitcast(F32).rearrange("p (b s u) -> p b s u", b=turns, u=2)
         for b in range(turns):
-            nc.scalar.copy(h_words[:, b], back[b][:].rearrange("p u s -> p s u"))
+            nc.vector.tensor_copy(h_words[:, b], back[b][:].rearrange("p u s -> p s u"))
 
         def multiply(m, s, product):
             nc.tensor.matmul_mx(
@@ -345,17 +381,12 @@ def tile_attend_gkl_w_ts_kernel(tc, xT, w_words, w_scales, y, wt, ts, xm, offs, 
 
         windows = [first_window, second_window, third_window]
 
-        def scatter(m, s, dw):
-            window = windows[m % WINDOWS]
-            if m % 2 == 1:
-                nc.vector.tensor_copy(window[:].indirect(offsets[:, s.start // 16 : s.stop // 16]), dw)
+        def scatter(m, s, dw, on_scalar):
+            window = windows[m % WINDOWS][:].indirect(offsets[:, s.start // 16 : s.stop // 16])
+            if on_scalar:
+                nc.scalar.activation(window, dw, ACT.Copy)
             else:
-                for lo in range(s.start, s.stop, HALF):
-                    nc.scalar.activation(
-                        window[:].indirect(offsets[:, lo // 16 : (lo + HALF) // 16]),
-                        dw[:, lo - s.start : lo - s.start + HALF],
-                        ACT.Copy,
-                    )
+                nc.vector.tensor_copy(window, dw)
 
         def store(m):
             nc.sync.dma_start(out[m * P : (m + 1) * P, :], windows[m % WINDOWS][:])
@@ -367,57 +398,79 @@ def tile_attend_gkl_w_ts_kernel(tc, xT, w_words, w_scales, y, wt, ts, xm, offs, 
 
         def cast_late(pair, staged):
             for k in range(2):
-                u = 2 * pair + k
                 nc.gpsimd.tensor_scalar(
                     staged[:, k * PACK * P : (k + 1) * PACK * P].rearrange("p (c j) -> p c j", j=PACK),
-                    xm_raw[2][:, :, u * P : (u + 1) * P].rearrange("p j c -> p c j"),
+                    xm_raw[2 + pair][:, :, k * P : (k + 1) * P].rearrange("p j c -> p c j"),
                     1.0,
                     0.0,
                     ALU.mult,
                     ALU.add,
                 )
 
-        first_bank = in_bank("first_bank", 2, [P, HALF])
-        multiply(0, halves[0], first_bank[:])
-        dw_first = held("dw_first", [P, HALF], F32, slot="h_turned1")
-        nc.vector.tensor_copy(dw_first[:], first_bank[:])
-        scatter(0, halves[0], dw_first[:])
-        xm_third = held("xm_third", [P, PACK * P], BF16, slot="h_bf0")
-        cast_xm(2, xm_third[:])
-        quantise_h(1)
+        def copy_halves(k, banks, places, copy):
+            tiles = [fixed("dw_pair%d%d" % (m, k), [P, HALF], F32, places[m]) for m in range(2)]
+            for m in range(2):
+                bank = in_bank("half_product%d%d" % (m, k), banks[m], [P, HALF])
+                multiply(m, halves[k], bank[:])
+                copy(tiles[m][:], bank[:])
+            return tiles
 
-        pair_bank = in_bank("pair_bank", 3, [P, N])
-        multiply(0, halves[1], pair_bank[:, halves[0]])
-        multiply(1, halves[0], pair_bank[:, halves[1]])
-        dw_pair = [held("dw_pair%d" % m, [P, HALF], F32, slot="dw%d" % m) for m in range(2)]
-        for m in range(2):
-            nc.vector.tensor_copy(dw_pair[m][:], pair_bank[:, halves[m]])
-        scatter(0, halves[1], dw_pair[0][:])
-        store(0)
-        quantise_xm(2, 3, xm_third, at=60 * KIB)
-        xm_fourth = fixed("xm_fourth", [P, PACK * P], BF16, 61 * KIB)
-        cast_xm(3, xm_fourth[:])
-        quantise_xm(3, 4, xm_fourth)
-        scatter(1, halves[0], dw_pair[1][:])
-
-        staged = fixed("xm_late0", [P, 2 * PACK * P], BF16, 61 * KIB)
-        cast_late(0, staged)
-        zero(held("window3", [P, T], F32, slot="h_turned1"))
-
-        for m in range(1, BLOCKS):
-            if m == 4:
-                quantise_xm(4, 6, staged)
-                staged = fixed("xm_late1", [P, 2 * PACK * P], BF16, 61 * KIB)
-                cast_late(1, staged)
-            if m == 6:
-                quantise_xm(6, 8, staged)
-            s = halves[1] if m == 1 else slice(0, N)
-            bank = in_bank("product%d" % m, (4, 7, 5, 6, 0, 1, 2)[m - 1], [P, s.stop - s.start])
-            multiply(m, s, bank[:])
-            dw = held("dw_block%d" % m, [P, s.stop - s.start], F32, slot="dw%d" % (m % 2))
+        def copy_block(m, bank_index, at):
+            bank = in_bank("product%d" % m, bank_index, [P, N])
+            multiply(m, whole, bank[:])
+            dw = fixed("dw_block%d" % m, [P, N], F32, at)
             if m % 2 == 1:
                 nc.vector.tensor_copy(dw[:], bank[:])
             else:
                 nc.scalar.copy(dw[:], bank[:])
-            scatter(m, s, dw[:])
-            store(m)
+            return dw
+
+        whole = slice(0, N)
+        xm_third = held("xm_third", [P, PACK * P], BF16, slot="share")
+        cast_xm(2, xm_third[:])
+        early = copy_halves(0, (2, 1), (10 * KIB - 960, 10 * KIB + 64), nc.scalar.copy)
+        for m in range(2):
+            scatter(m, halves[0], early[m][:], True)
+        quantise_h(1)
+
+        late = copy_halves(1, (3, 4), (50 * KIB, 52 * KIB), nc.vector.tensor_copy)
+        quantise_xm(2, 3, xm_third, at=60 * KIB)
+        xm_fourth = fixed("xm_fourth", [P, PACK * P], BF16, 61 * KIB)
+        cast_xm(3, xm_fourth[:])
+        quantise_xm(3, 4, xm_fourth)
+        scatter(0, halves[1], late[0][:], False)
+        store(0)
+
+        staged = fixed("xm_late0", [P, 2 * PACK * P], BF16, 61 * KIB)
+        cast_late(0, staged)
+        zero(fixed("window3", [P, T], F32, 11 * KIB + 512))
+
+        dw = {2: copy_block(2, 7, 54 * KIB), 3: copy_block(3, 5, 50 * KIB)}
+        scatter(1, halves[1], late[1][:], False)
+        store(1)
+
+        scatter(2, halves[0], dw[2][:, halves[0]], True)
+        quantise_xm(4, 6, staged)
+        staged = fixed("xm_late1", [P, 2 * PACK * P], BF16, 61 * KIB)
+        cast_late(1, staged)
+        scatter(2, halves[1], dw[2][:, halves[1]], True)
+        store(2)
+        dw[4] = copy_block(4, 6, 54 * KIB)
+        scatter(3, whole, dw[3][:], False)
+        store(3)
+        dw[5] = copy_block(5, 0, 50 * KIB)
+
+        scatter(4, halves[0], dw[4][:, halves[0]], True)
+        quantise_xm(6, 8, staged)
+        scatter(4, halves[1], dw[4][:, halves[1]], True)
+        store(4)
+        dw[6] = copy_block(6, 1, 54 * KIB)
+        dw[7] = copy_block(7, 2, 52 * KIB)
+        scatter(5, whole, dw[5][:], False)
+        store(5)
+
+        for k in range(2):
+            scatter(6, halves[k], dw[6][:, halves[k]], True)
+        store(6)
+        scatter(7, whole, dw[7][:], False)
+        store(7)

@@ -29,8 +29,9 @@ KIB = 1024
 def tile_attend_gkl_w_ts_kernel(tc, xT, w_words, w_scales, y, wt, ts, xm, offs, out):
     nc = tc.nc
     with ExitStack() as ctx:
-        keep = ctx.enter_context(tc.tile_pool(name="keep", bufs=1))
         placed = ctx.enter_context(tc.tile_pool(name="placed", bufs=1))
+        keep = ctx.enter_context(tc.tile_pool(name="keep", bufs=1))
+        far = ctx.enter_context(tc.tile_pool(name="far", bufs=1))
         psum = ctx.enter_context(tc.psum_pool(name="psum", bufs=1))
 
         def in_bank(name, k, shape):
@@ -61,14 +62,14 @@ def tile_attend_gkl_w_ts_kernel(tc, xT, w_words, w_scales, y, wt, ts, xm, offs, 
         nc.vector.memset(plane_first[:], 0)
         h_code = held("h_code", [P, N], U32)
         h_scale = held("h_scale", [P, N], U8)
-        first_window = held("window0", [P, T], F32)
+        first_window = far.tile([P, T], F32, name="window0", align_bytes=64, offset=60 * KIB)
         nc.vector.memset(first_window[:], 0.0)
-        zeros = held("zeros", [P, P], F32, slot="window1")
+        zeros = fixed("zeros", [P, P], F32, 0)
         nc.vector.memset(zeros[:], 0.0)
         nc.gpsimd.affine_select(
             out=ident[:], in_=zeros[:], compare_op=ALU.not_equal, fill=1.0, base=0, pattern=[[-1, P]], channel_multiplier=1
         )
-        second_window = held("window1", [P, T], F32)
+        second_window = fixed("window1", [P, T], F32, 0)
         nc.gpsimd.memset(second_window[:], 0.0)
 
         scale_sel = held("scale_sel", [P, N], U8)
@@ -148,7 +149,7 @@ def tile_attend_gkl_w_ts_kernel(tc, xT, w_words, w_scales, y, wt, ts, xm, offs, 
                 in_=x_bf[o, u][:, PACK * lo : PACK * hi],
             )
 
-        scores = [in_bank("scores%d" % t, t, [P, N]) for t in range(PACK - 1)]
+        scores = [in_bank("scores%d" % t, t, [P, N]) for t in range(PACK)]
 
         def score_pass(t, o):
             u, k = divmod(t, 2)
@@ -165,8 +166,8 @@ def tile_attend_gkl_w_ts_kernel(tc, xT, w_words, w_scales, y, wt, ts, xm, offs, 
         for u in range(2):
             cast_x(0, u, x_first, 0, P, True)
         y_sb = fixed("y_sb", [P, PACK, N], F32, 85 * KIB + 512)
-        load_xm(0)
         nc.sync.dma_start(y_sb[:], y[0].rearrange("(p t) i -> p t i", t=PACK))
+        load_xm(0)
         quantise_x(0, 0, 0, 2 * P)
         quantise_x(0, 1, 0, 2 * P)
         cast_x(1, 0, x_second, 0, P, True)
@@ -178,20 +179,8 @@ def tile_attend_gkl_w_ts_kernel(tc, xT, w_words, w_scales, y, wt, ts, xm, offs, 
         quantise_x(1, 0, P, 2 * P)
         quantise_x(1, 1, 0, 2 * P)
         for o in range(PASSES):
-            for t in range(PACK - 1):
+            for t in range(PACK):
                 score_pass(t, o)
-        by_slot = [in_bank("by_slot%d" % h, 5 + h, [P, 2, P]) for h in range(2)]
-        for c in range(PACK):
-            for o in range(PASSES):
-                nc.tensor.matmul_mx(
-                    out=by_slot[c // 2][:, c % 2, :],
-                    lhsT=w_code[:, o * 2 * N + 2 * c * P : o * 2 * N + 2 * (c + 1) * P].bitcast(E2M1),
-                    lhsT_scale=w_scale[o][:, c * P : (c + 1) * P],
-                    rhs=x_code[o, 1][:, P:].bitcast(E4M3),
-                    rhs_scale=x_scale[o, 1][:, P:],
-                    start=(o == 0),
-                    stop=(o == PASSES - 1),
-                )
 
         halves = [slice(0, HALF), slice(HALF, N)]
         turns = 1
@@ -199,24 +188,16 @@ def tile_attend_gkl_w_ts_kernel(tc, xT, w_words, w_scales, y, wt, ts, xm, offs, 
         third = slice(HALF, N - P)
         aside = slice(N - P, N)
 
-        ts_bank = in_bank("ts_bank", 4, [P, PACK, P])
-        for c in range(PACK):
-            nc.tensor.transpose(ts_bank[:, c, :], ts_sel[:, c * P : (c + 1) * P], ident[:])
+        ts_bank = in_bank("ts_bank", 4, [P, P])
+        nc.tensor.transpose(ts_bank[:], ts_sel[:, aside], ident[:])
         ts_slot = fixed("ts_slot", [P, 32], F32, 10 * KIB)
-        nc.scalar.copy(ts_slot[:, 0:PACK], ts_bank[:, :, 0])
-
-        last_by_slot = held("last_by_slot", [P, PACK, P], F32)
-        last_scores = in_bank("last_scores", 7, [P, N])
-        for c in range(PACK):
-            nc.scalar.activation(last_by_slot[:, c, :], by_slot[c // 2][:, c % 2, :], ACT.Copy, scale=ts_slot[:, c : c + 1])
-        for c in range(PACK):
-            nc.tensor.transpose(last_scores[:, c * P : (c + 1) * P], last_by_slot[:, c, :], ident[:])
+        nc.scalar.copy(ts_slot[:, 0:1], ts_bank[:, 0:1])
 
         wt_ts = fixed("wt_ts", [P, PACK, N - P], F32, 34 * KIB + 512)
         for t in range(PACK):
-            nc.gpsimd.tensor_scalar(wt_ts[:, t, :], ts_sel[:, direct], wt_sb[:, t : t + 1], 0.0, ALU.mult, ALU.add)
-        third_window = fixed("window2", [P, T], F32, 41 * KIB)
-        neg_wt = held("neg_wt", [P, PACK], F32)
+            nc.scalar.activation(wt_ts[:, t, :], ts_sel[:, direct], ACT.Copy, scale=wt_sb[:, t : t + 1])
+        third_window = far.tile([P, T], F32, name="window2", align_bytes=64, offset=68 * KIB)
+        neg_wt = far.tile([P, PACK], F32, name="neg_wt", align_bytes=64, offset=68 * KIB)
         nc.gpsimd.tensor_scalar(neg_wt[:], wt_sb[:], -1.0, 0.0, ALU.mult, ALU.add)
         neg_target = held("neg_target", [P, PACK, P], F32)
         for t in range(PACK):
@@ -236,9 +217,9 @@ def tile_attend_gkl_w_ts_kernel(tc, xT, w_words, w_scales, y, wt, ts, xm, offs, 
                     is_transpose=True,
                 )
 
-        neg_a = [held("neg_a%d" % t, [P, N], F32) for t in range(PACK - 1)]
+        neg_a = [held("neg_a%d" % t, [P, N], F32) for t in range(PACK)]
         neg_max = [held("neg_max%d" % t, [P, 1], F32) for t in range(PACK)]
-        e = [held("e%d" % t, [P, N], F32) if t != 1 else fixed("e1", [P, N], F32, 81 * KIB) for t in range(PACK)]
+        e = [held("e%d" % t, [P, N], F32) for t in range(PACK)]
         total = held("total", [P, PACK], F32)
         inv_first = held("inv0", [P, 2], F32)
         inv = [inv_first[:, 0:1], inv_first[:, 1:2], held("inv2", [P, 1], F32), held("inv3", [P, 1], F32)]
@@ -251,12 +232,8 @@ def tile_attend_gkl_w_ts_kernel(tc, xT, w_words, w_scales, y, wt, ts, xm, offs, 
             nc.vector.scalar_tensor_tensor(neg_a[t][:], scores[t][:], -1.0, ts_sel[:], ALU.mult, ALU.mult)
 
         def exponentiate(t):
-            if t < PACK - 1:
-                nc.vector.tensor_reduce(neg_max[t][:], neg_a[t][:], mybir.AxisListType.X, ALU.min)
-                nc.scalar.activation(e[t][:], neg_a[t][:], ACT.Exp, bias=neg_max[t][:], scale=-1.0, accum_out=total[:, t : t + 1])
-            else:
-                nc.vector.tensor_reduce(neg_max[t][:], last_scores[:], mybir.AxisListType.X, ALU.max, negate=True)
-                nc.scalar.activation(e[t][:], last_scores[:], ACT.Exp, bias=neg_max[t][:], accum_out=total[:, t : t + 1])
+            nc.vector.tensor_reduce(neg_max[t][:], neg_a[t][:], mybir.AxisListType.X, ALU.min)
+            nc.scalar.activation(e[t][:], neg_a[t][:], ACT.Exp, bias=neg_max[t][:], scale=-1.0, accum_out=total[:, t : t + 1])
 
         def invert(t):
             nc.vector.reciprocal(inv[t][:], total[:, t : t + 1])
@@ -300,16 +277,19 @@ def tile_attend_gkl_w_ts_kernel(tc, xT, w_words, w_scales, y, wt, ts, xm, offs, 
             nc.vector.quantize_mx(out=code[:].bitcast(E4M3), scales=xm_scale[:, lo * P : hi * P], in_=staged[:])
             xm_code.extend([code[:, k * P : (k + 1) * P] for k in range(hi - lo)])
 
-        xm_pair = held("xm_pair", [P, 2 * PACK * P], BF16, slot="x_bf01")
-        xm_first = [xm_pair[:, m * PACK * P : (m + 1) * PACK * P] for m in range(2)]
-        for m in range(2):
-            cast_xm(m, xm_first[m][:])
+        def stage_xm(m):
+            staged = held("xm_first%d" % m, [P, PACK * P], BF16, slot="neg_max%d" % m)
+            cast_xm(m, staged[:])
+            return staged
 
         scale_scores(0)
         scale_scores(1)
         exponentiate(0)
+        xm_first = [stage_xm(0)]
         scale_scores(2)
         exponentiate(1)
+        xm_first.append(stage_xm(1))
+        scale_scores(3)
         exponentiate(2)
         nc.vector.reciprocal(inv_first[:], total[:, 0:2])
         exponentiate(3)
@@ -361,7 +341,7 @@ def tile_attend_gkl_w_ts_kernel(tc, xT, w_words, w_scales, y, wt, ts, xm, offs, 
         for u in range(2):
             for b in range(turns):
                 nc.scalar.activation(
-                    h_turned[b][:, u], turned[u][:, b].rearrange("s e p -> s p e"), ACT.Copy, scale=ts_slot[:, PACK - 1 : PACK]
+                    h_turned[b][:, u], turned[u][:, b].rearrange("s e p -> s p e"), ACT.Copy, scale=ts_slot[:, 0:1]
                 )
                 nc.tensor.transpose(back[b][:, u, :], h_turned[b][:, u].rearrange("s p e -> s (p e)").bitcast(F32), ident[:])
         h_words = h_bf[1][:, P:, :].rearrange("p i t -> p (i t)").bitcast(F32).rearrange("p (b s u) -> p b s u", b=turns, u=2)

@@ -16,61 +16,84 @@ E5M2 = mybir.dt.float8_e5m2_x4
 E2M1 = mybir.dt.float4_e2m1fn_x4
 ALU = mybir.AluOpType
 ACT = mybir.ActivationFunctionType
+X = mybir.AxisListType.X
 
 P = 128
 PACK = 4
 PASSES = D // (P * PACK)
-BLOCKS = D // P
-WINDOWS = 4
 HALF = N // 2
 KIB = 1024
+LAP = 64
+
+X1 = 96 * KIB
+SCALES = X1 + 8 * KIB - LAP
+WINDOW1 = SCALES + 2 * KIB - LAP
+STAGED567 = 0
+STAGED3 = STAGED567 + 3 * KIB - LAP
+STAGED4 = STAGED3 + KIB - LAP
+WINDOW3 = STAGED4 + KIB - LAP
+H_FIRST = STAGED3
+Y = 24 * KIB
+X0 = Y + 8 * KIB - LAP
+XM01 = X0 + 8 * KIB - LAP
+XBF_LOW = 70 * KIB
+TS_POOL = XBF_LOW + 2 * KIB - LAP
+XBF_HIGH = TS_POOL + 8 * KIB - LAP
+XM47 = XBF_HIGH + 2 * KIB - LAP
+SHARE = 120 * KIB
+LAST_MAX = SHARE + 4 * KIB - LAP
+C23 = LAST_MAX + LAP
+TS_SLOT = 125 * KIB
+STAGED2 = H_FIRST + KIB
+G = 60 * KIB
+TS_COLS = 150 * KIB
+WINDOW2 = TS_COLS
+WINDOW0 = 160 * KIB
+DW_EVEN = (168 * KIB, 169 * KIB)
 
 
 def tile_attend_gkl_w_ts_kernel(tc, xT, w_words, w_scales, y, wt, ts, xm, offs, out):
     nc = tc.nc
     with ExitStack() as ctx:
-        placed = ctx.enter_context(tc.tile_pool(name="placed", bufs=1))
         keep = ctx.enter_context(tc.tile_pool(name="keep", bufs=1))
-        far = ctx.enter_context(tc.tile_pool(name="far", bufs=1))
+        placed = ctx.enter_context(tc.tile_pool(name="placed", bufs=1))
         psum = ctx.enter_context(tc.psum_pool(name="psum", bufs=1))
 
         def in_bank(name, k, shape):
             return psum.tile(shape, F32, name=name, tag="bank%d" % k)
 
-        def held(name, shape, dtype, slot=None):
-            return keep.tile(shape, dtype, name=name, tag=slot or name, align_bytes=64)
+        def held(name, shape, dtype):
+            return keep.tile(shape, dtype, name=name, align_bytes=64)
 
         def fixed(name, shape, dtype, at):
             return placed.tile(shape, dtype, name=name, align_bytes=64, offset=at)
 
         offsets = keep.tile([P, N // 16], U16, name="offsets")
         nc.sync.dma_start(offsets[:], offs)
-        scale_pool = fixed("scale_pool", [P, T // 4], I32, 23 * KIB)
+        scale_pool = fixed("scale_pool", [P, T // 4], I32, SCALES)
         nc.sync.dma_start(scale_pool[0:32, :], w_scales.rearrange("o f t -> (o f) t").bitcast(I32))
-        nc.vector.memset(scale_pool[32:64, :], 0)
-        nc.vector.memset(scale_pool[64:128, :], 0)
-        ts_cols = held("ts_cols", [P, T // P], F32)
+        ts_cols = fixed("ts_cols", [P, T // P], F32, TS_COLS)
         nc.sync.dma_start(ts_cols[:], ts[0:1, :].rearrange("o (p c) -> (o p) c", p=P))
         word_pool = held("word_pool", [P, T], I32)
         nc.sync.dma_start(word_pool[:], w_words[0].rearrange("p t b -> p (t b)").bitcast(I32))
         x_rows = [xT[0, 512 * o : 512 * (o + 1), :].rearrange("(p j) r -> p j r", j=PACK) for o in range(PASSES)]
-        x_first = fixed("x_first", [P, PACK, R], F32, 68 * KIB)
-        nc.sync.dma_start(x_first[:], x_rows[0])
+        x_first = fixed("x_first", [P, PACK, R], F32, X0)
+        for h in range(2):
+            nc.sync.dma_start(x_first[:, 2 * h : 2 * h + 2, :], x_rows[0][:, 2 * h : 2 * h + 2, :])
 
+        nc.gpsimd.memset(scale_pool[32:64, :], 0)
+        nc.gpsimd.memset(scale_pool[64:128, :], 0)
         ident = held("ident", [P, P], F32)
-        plane_first = held("plane_first", [P, N // 4], I32)
-        nc.vector.memset(plane_first[:], 0)
-        h_code = held("h_code", [P, N], U32)
-        h_scale = held("h_scale", [P, N], U8)
-        first_window = far.tile([P, T], F32, name="window0", align_bytes=64, offset=60 * KIB)
-        nc.vector.memset(first_window[:], 0.0)
-        zeros = fixed("zeros", [P, P], F32, 0)
-        nc.vector.memset(zeros[:], 0.0)
+        nc.gpsimd.memset(ident[:], 0.0)
         nc.gpsimd.affine_select(
-            out=ident[:], in_=zeros[:], compare_op=ALU.not_equal, fill=1.0, base=0, pattern=[[-1, P]], channel_multiplier=1
+            out=ident[:], in_=ident[:], compare_op=ALU.not_equal, fill=1.0, base=0, pattern=[[-1, P]], channel_multiplier=1
         )
-        second_window = fixed("window1", [P, T], F32, 0)
-        nc.gpsimd.memset(second_window[:], 0.0)
+
+        planes = [held("plane%d" % o, [P, N // 4], I32) for o in range(PASSES)]
+        for plane in planes:
+            nc.gpsimd.memset(plane[:], 0)
+        windows = [fixed("window0", [P, T], F32, WINDOW0)]
+        nc.vector.memset(windows[0][:], 0.0)
 
         scale_sel = held("scale_sel", [P, N], U8)
         nc.vector.tensor_copy(scale_sel[:], scale_pool[:].bitcast(U8).indirect(offsets[:]))
@@ -80,13 +103,23 @@ def tile_attend_gkl_w_ts_kernel(tc, xT, w_words, w_scales, y, wt, ts, xm, offs, 
                 row = 16 * o + 4 * q
                 nc.sync.dma_start(plane[32 * q : 32 * q + 4, :], scale_sel[:].bitcast(I32)[row : row + 4, :])
 
-        place_scales(plane_first, 0)
-        x_second = fixed("x_second", [P, PACK, R], F32, 16 * KIB)
-        nc.sync.dma_start(x_second[:], x_rows[1])
-        wt_sb = fixed("wt_sb", [P, PACK], F32, 24 * KIB)
-        nc.sync.dma_start(wt_sb[:], wt[0].rearrange("(p t) o -> p (t o)", t=PACK))
+        def zero(name, at):
+            window = fixed(name, [P, T], F32, at)
+            for q in range(T // N):
+                nc.gpsimd.memset(window[:, q * N : (q + 1) * N], 0.0)
+            windows.append(window)
 
-        ts_pool = fixed("ts_pool", [P, T], F32, 33 * KIB)
+        place_scales(planes[0], 0)
+        x_second = fixed("x_second", [P, PACK, R], F32, X1)
+        for h in range(2):
+            nc.sync.dma_start(x_second[:, 2 * h : 2 * h + 2, :], x_rows[1][:, 2 * h : 2 * h + 2, :])
+        place_scales(planes[1], 1)
+        wt_sb = fixed("wt_sb", [P, PACK], F32, SCALES + KIB)
+        nc.sync.dma_start(wt_sb[:], wt[0].rearrange("(p t) o -> p (t o)", t=PACK))
+        windows.append(fixed("window1", [P, T], F32, WINDOW1))
+        nc.vector.memset(windows[1][:], 0.0)
+
+        ts_pool = fixed("ts_pool", [P, T], F32, TS_POOL)
         ts_view = ts_pool[:].rearrange("m (p c) -> m p c", p=P)
         for b in range(4):
             bank = in_bank("ts_spread%d" % b, PACK + b, [P, PACK, P])
@@ -95,12 +128,11 @@ def tile_attend_gkl_w_ts_kernel(tc, xT, w_words, w_scales, y, wt, ts, xm, offs, 
                 nc.tensor.transpose(bank[:, k, :], ts_cols[:, c : c + 1].to_broadcast([P, P]), ident[:])
             nc.scalar.copy(ts_view[:, :, PACK * b : PACK * (b + 1)], bank[:].rearrange("m k p -> m p k"))
 
-        w_pair = fixed("w_pair", [P, N], U32, 84 * KIB)
+        zero("window2", WINDOW2)
+
+        w_pair = held("w_pair", [P, N], U32)
         nc.vector.tensor_copy(w_pair[:], word_pool[:].bitcast(U32).indirect(offsets[:]))
-        plane_second = held("plane_second", [P, N // 4], I32, slot="word_pool")
-        nc.vector.memset(plane_second[:], 0)
-        place_scales(plane_second, 1)
-        w_scale = [plane_first[:].bitcast(U8), plane_second[:].bitcast(U8)]
+        w_scale = [plane[:].bitcast(U8) for plane in planes]
 
         w_code = held("w_code", [P, PASSES * 2 * N], U8)
         nc.vector.tensor_copy(
@@ -108,245 +140,230 @@ def tile_attend_gkl_w_ts_kernel(tc, xT, w_words, w_scales, y, wt, ts, xm, offs, 
             w_pair[:].bitcast(U16).rearrange("p (i o) -> p o i", o=PASSES),
         )
 
+        xm_rows = xm[0].rearrange("(p j) d -> p j d", j=PACK)
+        xm_raw = {}
+
+        def load_xm(lo, hi, at):
+            raw = fixed("xm_raw%d" % lo, [P, PACK, (hi - lo) * P], F32, at)
+            nc.sync.dma_start(raw[:], xm_rows[:, :, lo * P : hi * P])
+            for m in range(lo, hi):
+                xm_raw[m] = raw[:, :, (m - lo) * P : (m - lo + 1) * P]
+
         ts_sel = held("ts_sel", [P, N], F32)
         nc.scalar.activation(ts_sel[:], ts_pool[:].indirect(offsets[:]), ACT.Copy)
+        first, second, whole = slice(0, HALF), slice(HALF, N), slice(0, N)
+        ts_slot = fixed("ts_slot", [P, 32], F32, TS_SLOT)
+        for v in range(2):
+            ts_bank = in_bank("ts_bank%d" % v, v, [P, 2, P])
+            for k in range(2):
+                nc.tensor.transpose(ts_bank[:, k, :], ts_sel[:, (2 * v + k) * P : (2 * v + k + 1) * P], ident[:])
+            nc.scalar.copy(ts_slot[:, 2 * v : 2 * v + 2], ts_bank[:, :, 0])
 
-        xm_rows = xm[0].rearrange("(p j) d -> p j d", j=PACK)
-        xm_spans = ((0, 2), (2, 4), (4, 6), (6, 8))
-        xm_raw = [
-            fixed("xm_raw0", [P, PACK, 2 * P], F32, 80 * KIB + 512),
-            fixed("xm_raw1", [P, PACK, 2 * P], F32, 20 * KIB),
-            fixed("xm_raw2", [P, PACK, 2 * P], F32, 16 * KIB),
-            fixed("xm_raw3", [P, PACK, 2 * P], F32, 68 * KIB),
-        ]
+        x_code = {}
+        x_scale = {}
+        for o in range(PASSES):
+            for u in range(2):
+                x_code[o, u] = held("x_code%d%d" % (o, u), [P, 2 * P], U32)
+                x_scale[o, u] = held("x_scale%d%d" % (o, u), [P, 2 * P], U8)
 
-        def load_xm(c):
-            lo, hi = xm_spans[c]
-            nc.sync.dma_start(xm_raw[c][:], xm_rows[:, :, lo * P : hi * P])
+        def cast_x(copy, staged, raw, u, lo, hi):
+            src = raw[:, lo:hi, :].rearrange("p j (m t) -> p m j t", t=PACK)[:, :, :, 2 * u : 2 * u + 2]
+            copy(staged[:].rearrange("p (t m j) -> p m j t", t=2, j=PACK)[:, :, lo:hi, :], src)
 
-
-        x_bf = {
-            (0, 0): held("x_bf00", [P, 2 * P * PACK], BF16),
-            (0, 1): held("x_bf01", [P, 2 * P * PACK], BF16),
-            (1, 0): held("x_bf10", [P, 2 * P * PACK], BF16, slot="x_bf01"),
-            (1, 1): fixed("x_bf11", [P, 2 * P * PACK], BF16, 40 * KIB),
-        }
-        x_code = {key: held("x_code%d%d" % key, [P, 2 * P], U32) for key in x_bf}
-        x_scale = {key: held("x_scale%d%d" % key, [P, 2 * P], U8) for key in x_bf}
-
-        def cast_x(o, u, raw, lo, hi, on_vector):
-            src = raw[:].rearrange("p j (m t) -> p m j t", t=PACK)[:, lo:hi, :, 2 * u : 2 * u + 2]
-            dst = x_bf[o, u][:].rearrange("p (t m j) -> p m j t", t=2, j=PACK)[:, lo:hi]
-            if on_vector:
-                nc.vector.tensor_copy(dst, src)
-            else:
-                nc.scalar.copy(dst, src)
-
-        def quantise_x(o, u, lo, hi):
+        def quantise_x(o, u, staged, lo, hi):
             nc.vector.quantize_mx(
                 out=x_code[o, u][:, lo:hi].bitcast(E4M3),
                 scales=x_scale[o, u][:, lo:hi],
-                in_=x_bf[o, u][:, PACK * lo : PACK * hi],
+                in_=staged[:, PACK * lo : PACK * hi],
             )
 
-        scores = [in_bank("scores%d" % t, t, [P, N]) for t in range(PACK)]
-
-        def score_pass(t, o):
-            u, k = divmod(t, 2)
-            nc.tensor.matmul_mx(
-                out=scores[t][:],
-                lhsT=x_code[o, u][:, k * P : (k + 1) * P].bitcast(E4M3),
-                lhsT_scale=x_scale[o, u][:, k * P : (k + 1) * P],
-                rhs=w_code[:, o * 2 * N : (o + 1) * 2 * N].bitcast(E2M1),
-                rhs_scale=w_scale[o],
-                start=(o == 0),
-                stop=(o == PASSES - 1),
-            )
-
-        for u in range(2):
-            cast_x(0, u, x_first, 0, P, True)
-        y_sb = fixed("y_sb", [P, PACK, N], F32, 85 * KIB + 512)
+        x_bf00 = held("x_bf00", [P, 2 * P * PACK], BF16)
+        x_bf01 = fixed("x_bf01", [P, 2 * P * PACK], BF16, XBF_LOW)
+        for h in range(2):
+            cast_x(nc.vector.tensor_copy, x_bf00, x_first, 0, 2 * h, 2 * h + 2)
+            cast_x(nc.scalar.copy, x_bf01, x_first, 1, 2 * h, 2 * h + 2)
+        y_sb = fixed("y_sb", [P, PACK, N], F32, Y)
         nc.sync.dma_start(y_sb[:], y[0].rearrange("(p t) i -> p t i", t=PACK))
-        load_xm(0)
-        quantise_x(0, 0, 0, 2 * P)
-        quantise_x(0, 1, 0, 2 * P)
-        cast_x(1, 0, x_second, 0, P, True)
-        cast_x(1, 1, x_second, 0, P, False)
-        load_xm(1)
-        load_xm(2)
-        load_xm(3)
-        quantise_x(1, 0, 0, P)
-        quantise_x(1, 0, P, 2 * P)
-        quantise_x(1, 1, 0, 2 * P)
+        load_xm(0, 2, XM01)
+        quantise_x(0, 0, x_bf00, 0, 2 * P)
+        quantise_x(0, 1, x_bf01, 0, 2 * P)
+        x_bf10 = fixed("x_bf10", [P, 2 * P * PACK], BF16, XBF_LOW)
+        x_bf11 = fixed("x_bf11", [P, 2 * P * PACK], BF16, XBF_HIGH)
+        for h in range(2):
+            cast_x(nc.vector.tensor_copy, x_bf10, x_second, 0, 2 * h, 2 * h + 2)
+            cast_x(nc.scalar.copy, x_bf11, x_second, 1, 2 * h, 2 * h + 2)
+        load_xm(2, 4, X1 - 4 * KIB + LAP)
+        wt_ts = fixed("wt_ts", [P, PACK, HALF], F32, X1 + LAP)
+        for t in range(PACK):
+            nc.scalar.activation(wt_ts[:, t, :], ts_sel[:, first], ACT.Copy, scale=wt_sb[:, t : t + 1])
+        quantise_x(1, 0, x_bf10, 0, P)
+        quantise_x(1, 1, x_bf11, 0, 2 * P)
+        quantise_x(1, 0, x_bf10, P, 2 * P)
+        load_xm(4, 8, XM47)
+
+        scores = [in_bank("scores%d" % t, t, [P, N]) for t in range(2)]
+        slot_scores = [in_bank("slot_scores%d" % v, 2 + v, [P, 2, 2 * P]) for v in range(2)]
         for o in range(PASSES):
-            for t in range(PACK):
-                score_pass(t, o)
-
-        halves = [slice(0, HALF), slice(HALF, N)]
-        turns = 1
-        direct = slice(0, N - P)
-        third = slice(HALF, N - P)
-        aside = slice(N - P, N)
-
-        ts_bank = in_bank("ts_bank", 4, [P, P])
-        nc.tensor.transpose(ts_bank[:], ts_sel[:, aside], ident[:])
-        ts_slot = fixed("ts_slot", [P, 32], F32, 10 * KIB)
-        nc.scalar.copy(ts_slot[:, 0:1], ts_bank[:, 0:1])
-
-        wt_ts = fixed("wt_ts", [P, PACK, N - P], F32, 34 * KIB + 512)
-        for t in range(PACK):
-            nc.scalar.activation(wt_ts[:, t, :], ts_sel[:, direct], ACT.Copy, scale=wt_sb[:, t : t + 1])
-        third_window = far.tile([P, T], F32, name="window2", align_bytes=64, offset=68 * KIB)
-        neg_wt = far.tile([P, PACK], F32, name="neg_wt", align_bytes=64, offset=68 * KIB)
-        nc.gpsimd.tensor_scalar(neg_wt[:], wt_sb[:], -1.0, 0.0, ALU.mult, ALU.add)
-        neg_target = held("neg_target", [P, PACK, P], F32)
-        for t in range(PACK):
-            nc.gpsimd.tensor_scalar(neg_target[:, t, :], y_sb[:, t, aside], neg_wt[:, t : t + 1], 0.0, ALU.mult, ALU.add)
-        for q in range(T // N):
-            nc.gpsimd.memset(third_window[:, q * N : (q + 1) * N], 0.0)
-
-        turned = [in_bank("turned%d" % u, 5 + u, [P, turns, 2, P]) for u in range(2)]
-        for t in range(PACK):
-            for b in range(turns):
-                nc.tensor.matmul(
-                    turned[t // 2][:, b, t % 2, :],
-                    neg_target[:, t, b * P : (b + 1) * P],
-                    ident[:],
-                    start=(t % 2 == 0 and b == 0),
-                    stop=False,
-                    is_transpose=True,
+            for t in range(2):
+                nc.tensor.matmul_mx(
+                    out=scores[t][:],
+                    lhsT=x_code[o, 0][:, t * P : (t + 1) * P].bitcast(E4M3),
+                    lhsT_scale=x_scale[o, 0][:, t * P : (t + 1) * P],
+                    rhs=w_code[:, o * 2 * N : (o + 1) * 2 * N].bitcast(E2M1),
+                    rhs_scale=w_scale[o],
+                    start=(o == 0),
+                    stop=(o == PASSES - 1),
                 )
+                for k in (2 * t, 2 * t + 1):
+                    nc.tensor.matmul_mx(
+                        out=slot_scores[t][:, k % 2, :],
+                        lhsT=w_code[:, o * 2 * N + k * 2 * P : o * 2 * N + (k + 1) * 2 * P].bitcast(E2M1),
+                        lhsT_scale=w_scale[o][:, k * P : (k + 1) * P],
+                        rhs=x_code[o, 1][:].bitcast(E4M3),
+                        rhs_scale=x_scale[o, 1][:],
+                        start=(o == 0 and k % 2 == 0),
+                        stop=(o == PASSES - 1 and k % 2 == 1),
+                    )
 
-        neg_a = [held("neg_a%d" % t, [P, N], F32) for t in range(PACK)]
-        neg_max = [held("neg_max%d" % t, [P, 1], F32) for t in range(PACK)]
-        e = [held("e%d" % t, [P, N], F32) for t in range(PACK)]
+        a_rows = [held("a_rows%d" % t, [P, N], F32) for t in range(2)]
+        for t in range(2):
+            nc.vector.tensor_tensor(a_rows[t][:], scores[t][:], ts_sel[:], ALU.mult)
+        a_turned = [in_bank("a_turned%d" % e, 4 + e, [P, N]) for e in range(2)]
+        for k in range(PACK):
+            a_slots = held("a_slots%d" % k, [P, 2 * P], F32)
+            nc.scalar.activation(a_slots[:], slot_scores[k // 2][:, k % 2, :], ACT.Copy, scale=ts_slot[:, k : k + 1])
+            for e in range(2):
+                nc.tensor.transpose(a_turned[e][:, k * P : (k + 1) * P], a_slots[:, e * P : (e + 1) * P], ident[:])
+        a = a_rows + a_turned
+
+        neg_wt = fixed("neg_wt", [P, PACK], F32, XBF_LOW + KIB)
+        nc.gpsimd.tensor_scalar(neg_wt[:], wt_sb[:], -1.0, 0.0, ALU.mult, ALU.add)
+        neg_target = held("neg_target", [P, PACK, HALF], F32)
+        for t in range(PACK):
+            nc.gpsimd.tensor_scalar(neg_target[:, t, :], y_sb[:, t, second], neg_wt[:, t : t + 1], 0.0, ALU.mult, ALU.add)
+
+        def cast_on_gpsimd(m, staged):
+            nc.gpsimd.tensor_scalar(
+                staged.rearrange("p (c j) -> p c j", j=PACK), xm_raw[m].rearrange("p j c -> p c j"), 1.0, 0.0, ALU.mult, ALU.add
+            )
+
+        staged01 = [held("staged%d" % m, [P, PACK * P], BF16) for m in range(2)]
+        for m in range(2):
+            cast_on_gpsimd(m, staged01[m][:])
+
+        neg_max = [held("neg_max%d" % t, [P, 1], F32) for t in range(PACK - 1)]
+        neg_max.append(fixed("neg_max3", [P, 32], F32, LAST_MAX))
+        e_rows = [held("e%d" % t, [P, N], F32) for t in range(PACK)]
         total = held("total", [P, PACK], F32)
-        inv_first = held("inv0", [P, 2], F32)
-        inv = [inv_first[:, 0:1], inv_first[:, 1:2], held("inv2", [P, 1], F32), held("inv3", [P, 1], F32)]
-        weight = held("weight", [P, PACK], F32)
-        g = held("g", [P, PACK, HALF], F32)
-        g_third = held("g_third", [P, PACK, P], F32)
-        share = held("share", [P, PACK, P], F32)
+        inv = held("inv", [P, PACK], F32)
+        c01 = held("c01", [P, 2], F32)
+        g = fixed("g", [P, PACK, HALF], F32, G)
 
-        def scale_scores(t):
-            nc.vector.scalar_tensor_tensor(neg_a[t][:], scores[t][:], -1.0, ts_sel[:], ALU.mult, ALU.mult)
-
-        def exponentiate(t):
-            nc.vector.tensor_reduce(neg_max[t][:], neg_a[t][:], mybir.AxisListType.X, ALU.min)
-            nc.scalar.activation(e[t][:], neg_a[t][:], ACT.Exp, bias=neg_max[t][:], scale=-1.0, accum_out=total[:, t : t + 1])
+        def maximum(t):
+            nc.vector.tensor_reduce(neg_max[t][:, 0:1], a[t][:], X, ALU.max, negate=True)
+            nc.scalar.activation(
+                e_rows[t][:], a[t][:], ACT.Exp, bias=neg_max[t][:, 0:1], scale=1.0, accum_out=total[:, t : t + 1]
+            )
 
         def invert(t):
-            nc.vector.reciprocal(inv[t][:], total[:, t : t + 1])
-
-        def weigh(t):
-            nc.vector.tensor_tensor(weight[:, t : t + 1], inv[t][:], wt_sb[:, t : t + 1], ALU.mult)
+            nc.vector.reciprocal(inv[:, t : t + 1], total[:, t : t + 1])
 
         def subtract_targets(t):
             nc.vector.scalar_tensor_tensor(
-                g[:, t, :], e[t][:, halves[0]], inv[t][:], y_sb[:, t, halves[0]], ALU.mult, ALU.subtract
+                g[:, t, :], e_rows[t][:, first], inv[:, t : t + 1], y_sb[:, t, first], ALU.mult, ALU.subtract
             )
 
-        def add_share(t):
-            nc.scalar.activation(share[:, t, :], e[t][:, aside], ACT.Copy, scale=weight[:, t : t + 1])
-            for b in range(turns):
+        turned = {}
+
+        def turn(u, t, source, start, stop):
+            for b in range(2):
                 nc.tensor.matmul(
-                    turned[t // 2][:, b, t % 2, :],
-                    share[:, t, b * P : (b + 1) * P],
+                    turned[u][:, b, t % 2, :],
+                    source[:, t, b * P : (b + 1) * P],
                     ident[:],
-                    start=False,
-                    stop=(t % 2 == 1 and b == turns - 1),
+                    start=(start and b == 0),
+                    stop=(stop and b == 1),
                     is_transpose=True,
                 )
 
-        xm_scale = held("xm_scale", [P, D], U8)
-        xm_code = []
+        def turn_targets(u, bank):
+            turned[u] = in_bank("turned%d" % u, bank, [P, 2, 2, P])
+            for t in (2 * u, 2 * u + 1):
+                turn(u, t, neg_target, t % 2 == 0, False)
 
-        def cast_xm(m, staged):
-            c, u = divmod(m, 2)
-            copy = nc.scalar.copy if m < 3 else nc.vector.tensor_copy
-            copy(
-                staged.rearrange("p (c i j) -> p c j i", i=4, j=PACK),
-                xm_raw[c][:, :, u * P : (u + 1) * P].rearrange("p j (c i) -> p c j i", i=4),
-            )
-
-        def quantise_xm(lo, hi, staged, slot=None, at=None):
-            if at is None:
-                code = held("xm_code%d" % lo, [P, (hi - lo) * P], U32, slot=slot)
-            else:
-                code = fixed("xm_code%d" % lo, [P, (hi - lo) * P], U32, at)
-            nc.vector.quantize_mx(out=code[:].bitcast(E4M3), scales=xm_scale[:, lo * P : hi * P], in_=staged[:])
-            xm_code.extend([code[:, k * P : (k + 1) * P] for k in range(hi - lo)])
-
-        def stage_xm(m):
-            staged = held("xm_first%d" % m, [P, PACK * P], BF16, slot="neg_max%d" % m)
-            cast_xm(m, staged[:])
-            return staged
-
-        scale_scores(0)
-        scale_scores(1)
-        exponentiate(0)
-        xm_first = [stage_xm(0)]
-        scale_scores(2)
-        exponentiate(1)
-        xm_first.append(stage_xm(1))
-        scale_scores(3)
-        exponentiate(2)
-        nc.vector.reciprocal(inv_first[:], total[:, 0:2])
-        exponentiate(3)
-        nc.vector.tensor_tensor(weight[:, 0:2], inv_first[:], wt_sb[:, 0:2], ALU.mult)
-        invert(2)
+        turn_targets(0, 3)
+        for t in range(3):
+            maximum(t)
+        turn_targets(1, 4)
+        invert(0)
+        maximum(3)
+        invert(1)
         subtract_targets(0)
-        weigh(2)
-
-        invert(3)
-        quantise_xm(0, 1, xm_first[0], slot="neg_max3")
+        nc.vector.tensor_tensor(c01[:], inv[:, 0:2], wt_sb[:, 0:2], ALU.mult)
+        invert(2)
         subtract_targets(1)
-        weigh(3)
+        invert(3)
         subtract_targets(2)
         subtract_targets(3)
+
+        share = fixed("share", [P, PACK, HALF], F32, SHARE)
+        c23 = fixed("c23", [P, 2], F32, C23)
+        weight = [c01[:, 0:1], c01[:, 1:2], c23[:, 0:1], c23[:, 1:2]]
         for t in range(PACK):
-            add_share(t)
+            nc.scalar.activation(share[:, t, :], e_rows[t][:, second], ACT.Copy, scale=weight[t])
+            if t < 2:
+                nc.scalar.activation(weight[t + 2], wt_sb[:, t + 2 : t + 3], ACT.Copy, scale=inv[:, t + 2 : t + 3])
+            turn(t // 2, t, share, False, t % 2 == 1)
 
-        h_bf = [fixed("h_bf0", [P, HALF, PACK], BF16, 59 * KIB), fixed("h_bf1", [P, HALF, PACK], BF16, 60 * KIB)]
+        xm_scale = held("xm_scale", [P, D], U8)
+        xm_code = {}
 
-        def quantise_h(k):
+        def quantise_xm(lo, hi, staged, at=None):
+            name = "xm_code%d" % lo
+            code = held(name, [P, (hi - lo) * P], U32) if at is None else fixed(name, [P, (hi - lo) * P], U32, at)
+            nc.vector.quantize_mx(out=code[:].bitcast(E4M3), scales=xm_scale[:, lo * P : hi * P], in_=staged[:])
+            for m in range(lo, hi):
+                xm_code[m] = code[:, (m - lo) * P : (m - lo + 1) * P]
+
+        h_code = held("h_code", [P, N], U32)
+        h_scale = held("h_scale", [P, N], U8)
+
+        def quantise_h(s, staged):
             nc.vector.quantize_mx(
-                out=h_code[:, halves[k]].bitcast(E5M2),
-                scales=h_scale[:, halves[k]],
-                in_=h_bf[k][:].rearrange("p i t -> p (i t)"),
+                out=h_code[:, s].bitcast(E5M2), scales=h_scale[:, s], in_=staged[:].rearrange("p i t -> p (i t)")
             )
 
+        quantise_xm(0, 1, staged01[0], at=Y)
+        h_first = fixed("h_first", [P, HALF, PACK], BF16, H_FIRST)
         nc.vector.tensor_tensor(
-            h_bf[0][:].rearrange("p (c i) t -> p c t i", i=2),
+            h_first[:].rearrange("p (c i) t -> p c t i", i=2),
             g[:].rearrange("p t (c i) -> p c t i", i=2),
-            wt_ts[:, :, halves[0]].rearrange("p t (c i) -> p c t i", i=2),
+            wt_ts[:].rearrange("p t (c i) -> p c t i", i=2),
             ALU.mult,
         )
-        quantise_xm(1, 2, xm_first[1], slot="total")
-        quantise_h(0)
+        quantise_xm(1, 2, staged01[1], at=G)
+        quantise_h(first, h_first)
 
-        for t in range(PACK):
-            nc.vector.scalar_tensor_tensor(
-                g_third[:, t, :], e[t][:, third], inv[t][:], y_sb[:, t, third], ALU.mult, ALU.subtract
-            )
-        nc.vector.tensor_tensor(
-            h_bf[1][:, 0:P, :].rearrange("p (c i) t -> p c t i", i=2),
-            g_third[:].rearrange("p t (c i) -> p c t i", i=2),
-            wt_ts[:, :, third].rearrange("p t (c i) -> p c t i", i=2),
-            ALU.mult,
-        )
-
-        h_turned = [held("h_turned%d" % b, [P, 2, P, 2], BF16, slot="weight") for b in range(turns)]
-        back = [in_bank("back%d" % b, b, [P, 2, P]) for b in range(turns)]
+        back = in_bank("back", 0, [P, 2, 2, P])
         for u in range(2):
-            for b in range(turns):
+            for b in range(2):
+                pairs = held("pairs%d%d" % (u, b), [P, P, 2], BF16)
                 nc.scalar.activation(
-                    h_turned[b][:, u], turned[u][:, b].rearrange("s e p -> s p e"), ACT.Copy, scale=ts_slot[:, 0:1]
+                    pairs[:], turned[u][:, b].rearrange("s e p -> s p e"), ACT.Copy, scale=ts_slot[:, 2 + b : 3 + b]
                 )
-                nc.tensor.transpose(back[b][:, u, :], h_turned[b][:, u].rearrange("s p e -> s (p e)").bitcast(F32), ident[:])
-        h_words = h_bf[1][:, P:, :].rearrange("p i t -> p (i t)").bitcast(F32).rearrange("p (b s u) -> p b s u", b=turns, u=2)
-        for b in range(turns):
-            nc.vector.tensor_copy(h_words[:, b], back[b][:].rearrange("p u s -> p s u"))
+                nc.tensor.transpose(back[:, b, u, :], pairs[:].rearrange("s p e -> s (p e)").bitcast(F32), ident[:])
+        h_second = held("h_second", [P, HALF, PACK], BF16)
+        nc.vector.tensor_copy(
+            h_second[:].rearrange("p i t -> p (i t)").bitcast(F32).rearrange("p (b s u) -> p b s u", b=2, u=2),
+            back[:].rearrange("p b u s -> p b s u"),
+        )
+
+        staged2 = fixed("staged2", [P, PACK * P], BF16, STAGED2)
+        nc.vector.tensor_copy(
+            staged2[:].rearrange("p (c i j) -> p c j i", i=4, j=PACK), xm_raw[2].rearrange("p j (c i) -> p c j i", i=4)
+        )
+        staged3 = fixed("staged3", [P, PACK * P], BF16, STAGED3)
+        cast_on_gpsimd(3, staged3[:])
 
         def multiply(m, s, product):
             nc.tensor.matmul_mx(
@@ -359,98 +376,68 @@ def tile_attend_gkl_w_ts_kernel(tc, xT, w_words, w_scales, y, wt, ts, xm, offs, 
                 stop=True,
             )
 
-        windows = [first_window, second_window, third_window]
+        def bring(m, s, bank_index, copy, dw):
+            bank = in_bank("product%d_%d" % (m, s.start), bank_index, [P, s.stop - s.start])
+            multiply(m, s, bank[:])
+            copy(dw, bank[:])
 
-        def scatter(m, s, dw, on_scalar):
-            window = windows[m % WINDOWS][:].indirect(offsets[:, s.start // 16 : s.stop // 16])
-            if on_scalar:
-                nc.scalar.activation(window, dw, ACT.Copy)
-            else:
-                nc.vector.tensor_copy(window, dw)
+        def scatter_on_scalar(m, s, dw):
+            nc.scalar.activation(windows[m % 4][:].indirect(offsets[:, s.start // 16 : s.stop // 16]), dw, ACT.Copy)
+
+        def scatter_on_vector(m, dw):
+            nc.vector.tensor_copy(windows[m % 4][:].indirect(offsets[:]), dw)
 
         def store(m):
-            nc.sync.dma_start(out[m * P : (m + 1) * P, :], windows[m % WINDOWS][:])
+            nc.sync.dma_start(out[m * P : (m + 1) * P, :], windows[m % 4][:])
 
-        def zero(window):
-            for q in range(T // N):
-                nc.gpsimd.memset(window[:, q * N : (q + 1) * N], 0.0)
-            windows.append(window)
+        halves = (first, second)
 
-        def cast_late(pair, staged):
-            for k in range(2):
-                nc.gpsimd.tensor_scalar(
-                    staged[:, k * PACK * P : (k + 1) * PACK * P].rearrange("p (c j) -> p c j", j=PACK),
-                    xm_raw[2 + pair][:, :, k * P : (k + 1) * P].rearrange("p j c -> p c j"),
-                    1.0,
-                    0.0,
-                    ALU.mult,
-                    ALU.add,
-                )
+        def even_tile(m, k):
+            return fixed("dw%d_%d" % (m, k), [P, HALF], F32, DW_EVEN[k])
 
-        def copy_halves(k, banks, places, copy):
-            tiles = [fixed("dw_pair%d%d" % (m, k), [P, HALF], F32, places[m]) for m in range(2)]
-            for m in range(2):
-                bank = in_bank("half_product%d%d" % (m, k), banks[m], [P, HALF])
-                multiply(m, halves[k], bank[:])
-                copy(tiles[m][:], bank[:])
-            return tiles
+        def cast_late(lo, hi, at):
+            staged = fixed("staged%d" % lo, [P, (hi - lo) * PACK * P], BF16, at)
+            for m in range(lo, hi):
+                cast_on_gpsimd(m, staged[:, (m - lo) * PACK * P : (m - lo + 1) * PACK * P])
+            return staged
 
-        def copy_block(m, bank_index, at):
-            bank = in_bank("product%d" % m, bank_index, [P, N])
-            multiply(m, whole, bank[:])
-            dw = fixed("dw_block%d" % m, [P, N], F32, at)
-            if m % 2 == 1:
-                nc.vector.tensor_copy(dw[:], bank[:])
-            else:
-                nc.scalar.copy(dw[:], bank[:])
-            return dw
-
-        whole = slice(0, N)
-        xm_third = held("xm_third", [P, PACK * P], BF16, slot="share")
-        cast_xm(2, xm_third[:])
-        early = copy_halves(0, (2, 1), (10 * KIB - 960, 10 * KIB + 64), nc.scalar.copy)
-        for m in range(2):
-            scatter(m, halves[0], early[m][:], True)
-        quantise_h(1)
-
-        late = copy_halves(1, (3, 4), (50 * KIB, 52 * KIB), nc.vector.tensor_copy)
-        quantise_xm(2, 3, xm_third, at=60 * KIB)
-        xm_fourth = fixed("xm_fourth", [P, PACK * P], BF16, 61 * KIB)
-        cast_xm(3, xm_fourth[:])
-        quantise_xm(3, 4, xm_fourth)
-        scatter(0, halves[1], late[0][:], False)
+        dw0 = even_tile(0, 0)
+        bring(0, first, 4, nc.scalar.copy, dw0[:])
+        dw1 = held("dw1", [P, N], F32)
+        bring(1, first, 3, nc.scalar.copy, dw1[:, first])
+        scatter_on_scalar(0, first, dw0[:])
+        quantise_xm(2, 3, staged2)
+        quantise_h(second, h_second)
+        quantise_xm(3, 4, staged3)
+        dw0 = even_tile(0, 1)
+        bring(0, second, 5, nc.vector.tensor_copy, dw0[:])
+        scatter_on_scalar(0, second, dw0[:])
         store(0)
-
-        staged = fixed("xm_late0", [P, 2 * PACK * P], BF16, 61 * KIB)
-        cast_late(0, staged)
-        zero(fixed("window3", [P, T], F32, 11 * KIB + 512))
-
-        dw = {2: copy_block(2, 7, 54 * KIB), 3: copy_block(3, 5, 50 * KIB)}
-        scatter(1, halves[1], late[1][:], False)
+        bring(1, second, 1, nc.vector.tensor_copy, dw1[:, second])
+        quantise_xm(4, 5, cast_late(4, 5, STAGED4))
+        scatter_on_vector(1, dw1[:])
         store(1)
 
-        scatter(2, halves[0], dw[2][:, halves[0]], True)
-        quantise_xm(4, 6, staged)
-        staged = fixed("xm_late1", [P, 2 * PACK * P], BF16, 61 * KIB)
-        cast_late(1, staged)
-        scatter(2, halves[1], dw[2][:, halves[1]], True)
-        store(2)
-        dw[4] = copy_block(4, 6, 54 * KIB)
-        scatter(3, whole, dw[3][:], False)
-        store(3)
-        dw[5] = copy_block(5, 0, 50 * KIB)
+        def even_block(m, bank_index):
+            bank = in_bank("product%d" % m, bank_index, [P, N])
+            multiply(m, whole, bank[:])
+            for k in range(2):
+                dw = even_tile(m, k)
+                nc.scalar.copy(dw[:], bank[:, halves[k]])
+                scatter_on_scalar(m, halves[k], dw[:])
+            store(m)
 
-        scatter(4, halves[0], dw[4][:, halves[0]], True)
-        quantise_xm(6, 8, staged)
-        scatter(4, halves[1], dw[4][:, halves[1]], True)
-        store(4)
-        dw[6] = copy_block(6, 1, 54 * KIB)
-        dw[7] = copy_block(7, 2, 52 * KIB)
-        scatter(5, whole, dw[5][:], False)
-        store(5)
+        def odd_block(m, bank_index):
+            dw = held("dw%d" % m, [P, N], F32)
+            bring(m, whole, bank_index, nc.vector.tensor_copy, dw[:])
+            scatter_on_vector(m, dw[:])
+            store(m)
 
-        for k in range(2):
-            scatter(6, halves[k], dw[6][:, halves[k]], True)
-        store(6)
-        scatter(7, whole, dw[7][:], False)
-        store(7)
+        even_block(2, 2)
+        quantise_xm(5, 8, cast_late(5, 8, STAGED567))
+        zero("window3", WINDOW3)
+        odd_block(3, 6)
+        even_block(4, 7)
+        odd_block(5, 0)
+        even_block(6, 4)
+        odd_block(7, 3)

@@ -27,29 +27,33 @@ LAP = 64
 
 X1 = 96 * KIB
 SCALES = X1 + 8 * KIB - LAP
-WINDOW1 = SCALES + 2 * KIB - LAP
+WINDOW1 = 14 * KIB
 STAGED567 = 0
 STAGED3 = STAGED567 + 3 * KIB - LAP
 STAGED4 = STAGED3 + KIB - LAP
 WINDOW3 = STAGED4 + KIB - LAP
-H_FIRST = STAGED3
+H_FIRST = STAGED3 - 2 * KIB + LAP
 Y = 24 * KIB
-X0 = Y + 8 * KIB - LAP
-XM01 = X0 + 8 * KIB - LAP
+PAIRS = Y + 8 * KIB - LAP
+XM01 = PAIRS + 2 * KIB - LAP
+XM23 = 38 * KIB
+X0 = XM23 + 4 * KIB - LAP
 XBF_LOW = 70 * KIB
 TS_POOL = XBF_LOW + 2 * KIB - LAP
 XBF_HIGH = TS_POOL + 8 * KIB - LAP
-XM47 = XBF_HIGH + 2 * KIB - LAP
+XM47 = X0 + 8 * KIB - LAP
 SHARE = 120 * KIB
 LAST_MAX = SHARE + 4 * KIB - LAP
 C23 = LAST_MAX + LAP
-TS_SLOT = 125 * KIB
-STAGED2 = H_FIRST + KIB
-G = 60 * KIB
-TS_COLS = 150 * KIB
-WINDOW2 = TS_COLS
-WINDOW0 = 160 * KIB
-DW_EVEN = (168 * KIB, 169 * KIB)
+DW1 = 134 * KIB
+DW_ODD = {3: DW1, 5: DW1 - 2 * KIB + LAP, 7: DW1 + 2 * KIB - LAP}
+H_SECOND = 128 * KIB
+STAGED2 = H_SECOND + 2 * KIB - LAP
+A_ROWS1 = 60 * KIB
+STAGED0 = 138 * KIB + LAP
+WINDOW2 = 140 * KIB
+WINDOW0 = 150 * KIB
+DW_EVEN = (158 * KIB, 159 * KIB)
 
 
 def tile_attend_gkl_w_ts_kernel(tc, xT, w_words, w_scales, y, wt, ts, xm, offs, out):
@@ -72,28 +76,30 @@ def tile_attend_gkl_w_ts_kernel(tc, xT, w_words, w_scales, y, wt, ts, xm, offs, 
         nc.sync.dma_start(offsets[:], offs)
         scale_pool = fixed("scale_pool", [P, T // 4], I32, SCALES)
         nc.sync.dma_start(scale_pool[0:32, :], w_scales.rearrange("o f t -> (o f) t").bitcast(I32))
-        ts_cols = fixed("ts_cols", [P, T // P], F32, TS_COLS)
+        ts_cols = held("ts_cols", [P, T // P], F32)
         nc.sync.dma_start(ts_cols[:], ts[0:1, :].rearrange("o (p c) -> (o p) c", p=P))
+        wt_sb = held("wt_sb", [P, PACK], F32)
+        nc.sync.dma_start(wt_sb[:], wt[0].rearrange("(p t) o -> p (t o)", t=PACK))
         word_pool = held("word_pool", [P, T], I32)
         nc.sync.dma_start(word_pool[:], w_words[0].rearrange("p t b -> p (t b)").bitcast(I32))
         x_rows = [xT[0, 512 * o : 512 * (o + 1), :].rearrange("(p j) r -> p j r", j=PACK) for o in range(PASSES)]
         x_first = fixed("x_first", [P, PACK, R], F32, X0)
-        for h in range(2):
-            nc.sync.dma_start(x_first[:, 2 * h : 2 * h + 2, :], x_rows[0][:, 2 * h : 2 * h + 2, :])
+        nc.sync.dma_start(x_first[:], x_rows[0])
 
         nc.gpsimd.memset(scale_pool[32:64, :], 0)
         nc.gpsimd.memset(scale_pool[64:128, :], 0)
+        windows = [fixed("window0", [P, T], F32, WINDOW0)]
+        nc.vector.memset(windows[0][:], 0.0)
         ident = held("ident", [P, P], F32)
         nc.gpsimd.memset(ident[:], 0.0)
         nc.gpsimd.affine_select(
             out=ident[:], in_=ident[:], compare_op=ALU.not_equal, fill=1.0, base=0, pattern=[[-1, P]], channel_multiplier=1
         )
-
         planes = [held("plane%d" % o, [P, N // 4], I32) for o in range(PASSES)]
         for plane in planes:
             nc.gpsimd.memset(plane[:], 0)
-        windows = [fixed("window0", [P, T], F32, WINDOW0)]
-        nc.vector.memset(windows[0][:], 0.0)
+        windows.append(fixed("window1", [P, T], F32, WINDOW1))
+        nc.gpsimd.memset(windows[1][:], 0.0)
 
         scale_sel = held("scale_sel", [P, N], U8)
         nc.vector.tensor_copy(scale_sel[:], scale_pool[:].bitcast(U8).indirect(offsets[:]))
@@ -111,13 +117,8 @@ def tile_attend_gkl_w_ts_kernel(tc, xT, w_words, w_scales, y, wt, ts, xm, offs, 
 
         place_scales(planes[0], 0)
         x_second = fixed("x_second", [P, PACK, R], F32, X1)
-        for h in range(2):
-            nc.sync.dma_start(x_second[:, 2 * h : 2 * h + 2, :], x_rows[1][:, 2 * h : 2 * h + 2, :])
+        nc.sync.dma_start(x_second[:], x_rows[1])
         place_scales(planes[1], 1)
-        wt_sb = fixed("wt_sb", [P, PACK], F32, SCALES + KIB)
-        nc.sync.dma_start(wt_sb[:], wt[0].rearrange("(p t) o -> p (t o)", t=PACK))
-        windows.append(fixed("window1", [P, T], F32, WINDOW1))
-        nc.vector.memset(windows[1][:], 0.0)
 
         ts_pool = fixed("ts_pool", [P, T], F32, TS_POOL)
         ts_view = ts_pool[:].rearrange("m (p c) -> m p c", p=P)
@@ -128,9 +129,7 @@ def tile_attend_gkl_w_ts_kernel(tc, xT, w_words, w_scales, y, wt, ts, xm, offs, 
                 nc.tensor.transpose(bank[:, k, :], ts_cols[:, c : c + 1].to_broadcast([P, P]), ident[:])
             nc.scalar.copy(ts_view[:, :, PACK * b : PACK * (b + 1)], bank[:].rearrange("m k p -> m p k"))
 
-        zero("window2", WINDOW2)
-
-        w_pair = held("w_pair", [P, N], U32)
+        w_pair = fixed("w_pair", [P, N], U32, PAIRS)
         nc.vector.tensor_copy(w_pair[:], word_pool[:].bitcast(U32).indirect(offsets[:]))
         w_scale = [plane[:].bitcast(U8) for plane in planes]
 
@@ -149,15 +148,22 @@ def tile_attend_gkl_w_ts_kernel(tc, xT, w_words, w_scales, y, wt, ts, xm, offs, 
             for m in range(lo, hi):
                 xm_raw[m] = raw[:, :, (m - lo) * P : (m - lo + 1) * P]
 
+        y_sb = fixed("y_sb", [P, PACK, N], F32, Y)
+        nc.sync.dma_start(y_sb[:], y[0].rearrange("(p t) i -> p t i", t=PACK))
+        load_xm(0, 2, XM01)
+
         ts_sel = held("ts_sel", [P, N], F32)
         nc.scalar.activation(ts_sel[:], ts_pool[:].indirect(offsets[:]), ACT.Copy)
         first, second, whole = slice(0, HALF), slice(HALF, N), slice(0, N)
-        ts_slot = fixed("ts_slot", [P, 32], F32, TS_SLOT)
-        for v in range(2):
-            ts_bank = in_bank("ts_bank%d" % v, v, [P, 2, P])
-            for k in range(2):
-                nc.tensor.transpose(ts_bank[:, k, :], ts_sel[:, (2 * v + k) * P : (2 * v + k + 1) * P], ident[:])
-            nc.scalar.copy(ts_slot[:, 2 * v : 2 * v + 2], ts_bank[:, :, 0])
+        ts_slot = held("ts_slot", [P, PACK], F32)
+        for k in range(PACK):
+            ts_bank = in_bank("ts_bank%d" % k, k, [P, P])
+            nc.tensor.transpose(ts_bank[:], ts_sel[:, k * P : (k + 1) * P], ident[:])
+            nc.scalar.copy(ts_slot[:, k : k + 1], ts_bank[:, 0:1])
+
+        wt_ts = held("wt_ts", [P, PACK, HALF], F32)
+        for t in range(PACK):
+            nc.scalar.activation(wt_ts[:, t, :], ts_sel[:, first], ACT.Copy, scale=wt_sb[:, t : t + 1])
 
         x_code = {}
         x_scale = {}
@@ -166,9 +172,9 @@ def tile_attend_gkl_w_ts_kernel(tc, xT, w_words, w_scales, y, wt, ts, xm, offs, 
                 x_code[o, u] = held("x_code%d%d" % (o, u), [P, 2 * P], U32)
                 x_scale[o, u] = held("x_scale%d%d" % (o, u), [P, 2 * P], U8)
 
-        def cast_x(copy, staged, raw, u, lo, hi):
-            src = raw[:, lo:hi, :].rearrange("p j (m t) -> p m j t", t=PACK)[:, :, :, 2 * u : 2 * u + 2]
-            copy(staged[:].rearrange("p (t m j) -> p m j t", t=2, j=PACK)[:, :, lo:hi, :], src)
+        def cast_x(copy, staged, raw, u):
+            src = raw[:].rearrange("p j (m t) -> p m j t", t=PACK)[:, :, :, 2 * u : 2 * u + 2]
+            copy(staged[:].rearrange("p (t m j) -> p m j t", t=2, j=PACK), src)
 
         def quantise_x(o, u, staged, lo, hi):
             nc.vector.quantize_mx(
@@ -178,28 +184,20 @@ def tile_attend_gkl_w_ts_kernel(tc, xT, w_words, w_scales, y, wt, ts, xm, offs, 
             )
 
         x_bf00 = held("x_bf00", [P, 2 * P * PACK], BF16)
-        x_bf01 = fixed("x_bf01", [P, 2 * P * PACK], BF16, XBF_LOW)
-        for h in range(2):
-            cast_x(nc.vector.tensor_copy, x_bf00, x_first, 0, 2 * h, 2 * h + 2)
-            cast_x(nc.scalar.copy, x_bf01, x_first, 1, 2 * h, 2 * h + 2)
-        y_sb = fixed("y_sb", [P, PACK, N], F32, Y)
-        nc.sync.dma_start(y_sb[:], y[0].rearrange("(p t) i -> p t i", t=PACK))
-        load_xm(0, 2, XM01)
+        x_bf01 = fixed("x_bf01", [P, 2 * P * PACK], BF16, XBF_LOW - KIB)
+        cast_x(nc.vector.tensor_copy, x_bf00, x_first, 0)
+        cast_x(nc.vector.tensor_copy, x_bf01, x_first, 1)
+        load_xm(2, 4, XM23)
+        load_xm(4, 8, XM47)
         quantise_x(0, 0, x_bf00, 0, 2 * P)
         quantise_x(0, 1, x_bf01, 0, 2 * P)
-        x_bf10 = fixed("x_bf10", [P, 2 * P * PACK], BF16, XBF_LOW)
+        x_bf10 = fixed("x_bf10", [P, 2 * P * PACK], BF16, XBF_LOW - KIB)
         x_bf11 = fixed("x_bf11", [P, 2 * P * PACK], BF16, XBF_HIGH)
-        for h in range(2):
-            cast_x(nc.vector.tensor_copy, x_bf10, x_second, 0, 2 * h, 2 * h + 2)
-            cast_x(nc.scalar.copy, x_bf11, x_second, 1, 2 * h, 2 * h + 2)
-        load_xm(2, 4, X1 - 4 * KIB + LAP)
-        wt_ts = fixed("wt_ts", [P, PACK, HALF], F32, X1 + LAP)
-        for t in range(PACK):
-            nc.scalar.activation(wt_ts[:, t, :], ts_sel[:, first], ACT.Copy, scale=wt_sb[:, t : t + 1])
+        cast_x(nc.vector.tensor_copy, x_bf10, x_second, 0)
+        cast_x(nc.scalar.copy, x_bf11, x_second, 1)
         quantise_x(1, 0, x_bf10, 0, P)
-        quantise_x(1, 1, x_bf11, 0, 2 * P)
         quantise_x(1, 0, x_bf10, P, 2 * P)
-        load_xm(4, 8, XM47)
+        quantise_x(1, 1, x_bf11, 0, 2 * P)
 
         scores = [in_bank("scores%d" % t, t, [P, N]) for t in range(2)]
         slot_scores = [in_bank("slot_scores%d" % v, 2 + v, [P, 2, 2 * P]) for v in range(2)]
@@ -225,7 +223,7 @@ def tile_attend_gkl_w_ts_kernel(tc, xT, w_words, w_scales, y, wt, ts, xm, offs, 
                         stop=(o == PASSES - 1 and k % 2 == 1),
                     )
 
-        a_rows = [held("a_rows%d" % t, [P, N], F32) for t in range(2)]
+        a_rows = [fixed("a_rows0", [P, N], F32, XBF_HIGH - 2 * KIB + LAP), fixed("a_rows1", [P, N], F32, A_ROWS1)]
         for t in range(2):
             nc.vector.tensor_tensor(a_rows[t][:], scores[t][:], ts_sel[:], ALU.mult)
         a_turned = [in_bank("a_turned%d" % e, 4 + e, [P, N]) for e in range(2)]
@@ -236,7 +234,7 @@ def tile_attend_gkl_w_ts_kernel(tc, xT, w_words, w_scales, y, wt, ts, xm, offs, 
                 nc.tensor.transpose(a_turned[e][:, k * P : (k + 1) * P], a_slots[:, e * P : (e + 1) * P], ident[:])
         a = a_rows + a_turned
 
-        neg_wt = fixed("neg_wt", [P, PACK], F32, XBF_LOW + KIB)
+        neg_wt = fixed("neg_wt", [P, PACK], F32, XBF_HIGH + KIB)
         nc.gpsimd.tensor_scalar(neg_wt[:], wt_sb[:], -1.0, 0.0, ALU.mult, ALU.add)
         neg_target = held("neg_target", [P, PACK, HALF], F32)
         for t in range(PACK):
@@ -247,9 +245,9 @@ def tile_attend_gkl_w_ts_kernel(tc, xT, w_words, w_scales, y, wt, ts, xm, offs, 
                 staged.rearrange("p (c j) -> p c j", j=PACK), xm_raw[m].rearrange("p j c -> p c j"), 1.0, 0.0, ALU.mult, ALU.add
             )
 
-        staged01 = [held("staged%d" % m, [P, PACK * P], BF16) for m in range(2)]
+        staged01 = fixed("staged0", [P, 2 * PACK * P], BF16, STAGED0)
         for m in range(2):
-            cast_on_gpsimd(m, staged01[m][:])
+            cast_on_gpsimd(m, staged01[:, m * PACK * P : (m + 1) * PACK * P])
 
         neg_max = [held("neg_max%d" % t, [P, 1], F32) for t in range(PACK - 1)]
         neg_max.append(fixed("neg_max3", [P, 32], F32, LAST_MAX))
@@ -257,7 +255,7 @@ def tile_attend_gkl_w_ts_kernel(tc, xT, w_words, w_scales, y, wt, ts, xm, offs, 
         total = held("total", [P, PACK], F32)
         inv = held("inv", [P, PACK], F32)
         c01 = held("c01", [P, 2], F32)
-        g = fixed("g", [P, PACK, HALF], F32, G)
+        g = held("g", [P, PACK, HALF], F32)
 
         def maximum(t):
             nc.vector.tensor_reduce(neg_max[t][:, 0:1], a[t][:], X, ALU.max, negate=True)
@@ -268,10 +266,20 @@ def tile_attend_gkl_w_ts_kernel(tc, xT, w_words, w_scales, y, wt, ts, xm, offs, 
         def invert(t):
             nc.vector.reciprocal(inv[:, t : t + 1], total[:, t : t + 1])
 
-        def subtract_targets(t):
+        def subtract_targets(t, s):
             nc.vector.scalar_tensor_tensor(
-                g[:, t, :], e_rows[t][:, first], inv[:, t : t + 1], y_sb[:, t, first], ALU.mult, ALU.subtract
+                g[:, t, s], e_rows[t][:, s], inv[:, t : t + 1], y_sb[:, t, s], ALU.mult, ALU.subtract
             )
+
+        xm_scale = held("xm_scale", [P, D], U8)
+        xm_code = {}
+
+        def quantise_xm(lo, hi, staged, at=None):
+            name = "xm_code%d" % lo
+            code = held(name, [P, (hi - lo) * P], U32) if at is None else fixed(name, [P, (hi - lo) * P], U32, at)
+            nc.vector.quantize_mx(out=code[:].bitcast(E4M3), scales=xm_scale[:, lo * P : hi * P], in_=staged[:])
+            for m in range(lo, hi):
+                xm_code[m] = code[:, (m - lo) * P : (m - lo + 1) * P]
 
         turned = {}
 
@@ -298,13 +306,17 @@ def tile_attend_gkl_w_ts_kernel(tc, xT, w_words, w_scales, y, wt, ts, xm, offs, 
         invert(0)
         maximum(3)
         invert(1)
-        subtract_targets(0)
+        quantise_xm(0, 2, staged01, at=A_ROWS1)
+        zero("window2", WINDOW2)
+        subtract_targets(0, first)
         nc.vector.tensor_tensor(c01[:], inv[:, 0:2], wt_sb[:, 0:2], ALU.mult)
         invert(2)
-        subtract_targets(1)
+        subtract_targets(1, first)
         invert(3)
-        subtract_targets(2)
-        subtract_targets(3)
+        subtract_targets(2, first)
+        quarters = (slice(0, P), slice(P, HALF))
+        for s in quarters:
+            subtract_targets(3, s)
 
         share = fixed("share", [P, PACK, HALF], F32, SHARE)
         c23 = fixed("c23", [P, 2], F32, C23)
@@ -315,48 +327,43 @@ def tile_attend_gkl_w_ts_kernel(tc, xT, w_words, w_scales, y, wt, ts, xm, offs, 
                 nc.scalar.activation(weight[t + 2], wt_sb[:, t + 2 : t + 3], ACT.Copy, scale=inv[:, t + 2 : t + 3])
             turn(t // 2, t, share, False, t % 2 == 1)
 
-        xm_scale = held("xm_scale", [P, D], U8)
-        xm_code = {}
-
-        def quantise_xm(lo, hi, staged, at=None):
-            name = "xm_code%d" % lo
-            code = held(name, [P, (hi - lo) * P], U32) if at is None else fixed(name, [P, (hi - lo) * P], U32, at)
-            nc.vector.quantize_mx(out=code[:].bitcast(E4M3), scales=xm_scale[:, lo * P : hi * P], in_=staged[:])
-            for m in range(lo, hi):
-                xm_code[m] = code[:, (m - lo) * P : (m - lo + 1) * P]
-
         h_code = held("h_code", [P, N], U32)
         h_scale = held("h_scale", [P, N], U8)
 
         def quantise_h(s, staged):
             nc.vector.quantize_mx(
-                out=h_code[:, s].bitcast(E5M2), scales=h_scale[:, s], in_=staged[:].rearrange("p i t -> p (i t)")
+                out=h_code[:, s].bitcast(E5M2), scales=h_scale[:, s], in_=staged.rearrange("p i t -> p (i t)")
             )
 
-        quantise_xm(0, 1, staged01[0], at=Y)
         h_first = fixed("h_first", [P, HALF, PACK], BF16, H_FIRST)
-        nc.vector.tensor_tensor(
-            h_first[:].rearrange("p (c i) t -> p c t i", i=2),
-            g[:].rearrange("p t (c i) -> p c t i", i=2),
-            wt_ts[:].rearrange("p t (c i) -> p c t i", i=2),
-            ALU.mult,
-        )
-        quantise_xm(1, 2, staged01[1], at=G)
-        quantise_h(first, h_first)
+        for s in quarters:
+            nc.vector.tensor_tensor(
+                h_first[:, s, :].rearrange("p (c i) t -> p c t i", i=2),
+                g[:, :, s].rearrange("p t (c i) -> p c t i", i=2),
+                wt_ts[:, :, s].rearrange("p t (c i) -> p c t i", i=2),
+                ALU.mult,
+            )
+        for s in quarters:
+            quantise_h(s, h_first[:, s, :])
 
-        back = in_bank("back", 0, [P, 2, 2, P])
+        back = [in_bank("back%d" % b, b, [P, 2, P]) for b in range(2)]
         for u in range(2):
             for b in range(2):
                 pairs = held("pairs%d%d" % (u, b), [P, P, 2], BF16)
-                nc.scalar.activation(
-                    pairs[:], turned[u][:, b].rearrange("s e p -> s p e"), ACT.Copy, scale=ts_slot[:, 2 + b : 3 + b]
-                )
-                nc.tensor.transpose(back[:, b, u, :], pairs[:].rearrange("s p e -> s (p e)").bitcast(F32), ident[:])
-        h_second = held("h_second", [P, HALF, PACK], BF16)
-        nc.vector.tensor_copy(
-            h_second[:].rearrange("p i t -> p (i t)").bitcast(F32).rearrange("p (b s u) -> p b s u", b=2, u=2),
-            back[:].rearrange("p b u s -> p b s u"),
-        )
+                sums = turned[u][:, b].rearrange("s e p -> s p e")
+                if u == 1 and b == 1:
+                    nc.vector.tensor_scalar(pairs[:], sums, ts_slot[:, 2 + b : 3 + b], None, ALU.mult)
+                else:
+                    nc.scalar.activation(pairs[:], sums, ACT.Copy, scale=ts_slot[:, 2 + b : 3 + b])
+                nc.tensor.transpose(back[b][:, u, :], pairs[:].rearrange("s p e -> s (p e)").bitcast(F32), ident[:])
+        h_second = [fixed("h_second%d" % b, [P, P, PACK], BF16, H_SECOND + b * KIB) for b in range(2)]
+        for b in range(2):
+            nc.vector.tensor_copy(
+                h_second[b][:].rearrange("p i t -> p (i t)").bitcast(F32).rearrange("p (s u) -> p s u", u=2),
+                back[b][:].rearrange("p u s -> p s u"),
+            )
+        for b in range(2):
+            quantise_h(slice(HALF + b * P, HALF + (b + 1) * P), h_second[b][:])
 
         staged2 = fixed("staged2", [P, PACK * P], BF16, STAGED2)
         nc.vector.tensor_copy(
@@ -402,18 +409,18 @@ def tile_attend_gkl_w_ts_kernel(tc, xT, w_words, w_scales, y, wt, ts, xm, offs, 
             return staged
 
         dw0 = even_tile(0, 0)
-        bring(0, first, 4, nc.scalar.copy, dw0[:])
-        dw1 = held("dw1", [P, N], F32)
-        bring(1, first, 3, nc.scalar.copy, dw1[:, first])
+        for s, bank_index in zip(quarters, (3, 5)):
+            bring(0, s, bank_index, nc.scalar.copy, dw0[:, s])
+        dw1 = fixed("dw1", [P, N], F32, DW1)
+        bring(1, first, 4, nc.scalar.copy, dw1[:, first])
         scatter_on_scalar(0, first, dw0[:])
         quantise_xm(2, 3, staged2)
-        quantise_h(second, h_second)
         quantise_xm(3, 4, staged3)
         dw0 = even_tile(0, 1)
-        bring(0, second, 5, nc.vector.tensor_copy, dw0[:])
+        bring(0, second, 6, nc.scalar.copy, dw0[:])
+        bring(1, second, 7, nc.scalar.copy, dw1[:, second])
         scatter_on_scalar(0, second, dw0[:])
         store(0)
-        bring(1, second, 1, nc.vector.tensor_copy, dw1[:, second])
         quantise_xm(4, 5, cast_late(4, 5, STAGED4))
         scatter_on_vector(1, dw1[:])
         store(1)
@@ -428,7 +435,7 @@ def tile_attend_gkl_w_ts_kernel(tc, xT, w_words, w_scales, y, wt, ts, xm, offs, 
             store(m)
 
         def odd_block(m, bank_index):
-            dw = held("dw%d" % m, [P, N], F32)
+            dw = fixed("dw%d" % m, [P, N], F32, DW_ODD[m])
             bring(m, whole, bank_index, nc.vector.tensor_copy, dw[:])
             scatter_on_vector(m, dw[:])
             store(m)
@@ -436,8 +443,8 @@ def tile_attend_gkl_w_ts_kernel(tc, xT, w_words, w_scales, y, wt, ts, xm, offs, 
         even_block(2, 2)
         quantise_xm(5, 8, cast_late(5, 8, STAGED567))
         zero("window3", WINDOW3)
-        odd_block(3, 6)
-        even_block(4, 7)
+        odd_block(3, 1)
+        even_block(4, 5)
         odd_block(5, 0)
-        even_block(6, 4)
-        odd_block(7, 3)
+        even_block(6, 3)
+        odd_block(7, 4)

@@ -49,9 +49,9 @@ DW1 = 134 * KIB
 DW_ODD = {3: DW1, 5: DW1 - 2 * KIB + LAP, 7: DW1 + 2 * KIB - LAP}
 H_SECOND = 128 * KIB
 STAGED2 = H_SECOND + 2 * KIB - LAP
-A_ROWS1 = 60 * KIB
-STAGED0 = 138 * KIB + LAP
-WINDOW2 = 140 * KIB
+TS_SEL = 60 * KIB
+STAGED0 = XBF_HIGH + 2 * KIB - LAP
+WINDOW2 = STAGED0 + 2 * KIB - LAP
 WINDOW0 = 150 * KIB
 DW_EVEN = (158 * KIB, 159 * KIB)
 
@@ -148,11 +148,11 @@ def tile_attend_gkl_w_ts_kernel(tc, xT, w_words, w_scales, y, wt, ts, xm, offs, 
             for m in range(lo, hi):
                 xm_raw[m] = raw[:, :, (m - lo) * P : (m - lo + 1) * P]
 
+        load_xm(0, 2, XM01)
         y_sb = fixed("y_sb", [P, PACK, N], F32, Y)
         nc.sync.dma_start(y_sb[:], y[0].rearrange("(p t) i -> p t i", t=PACK))
-        load_xm(0, 2, XM01)
 
-        ts_sel = held("ts_sel", [P, N], F32)
+        ts_sel = fixed("ts_sel", [P, N], F32, TS_SEL)
         nc.scalar.activation(ts_sel[:], ts_pool[:].indirect(offsets[:]), ACT.Copy)
         first, second, whole = slice(0, HALF), slice(HALF, N), slice(0, N)
         ts_slot = held("ts_slot", [P, PACK], F32)
@@ -223,7 +223,7 @@ def tile_attend_gkl_w_ts_kernel(tc, xT, w_words, w_scales, y, wt, ts, xm, offs, 
                         stop=(o == PASSES - 1 and k % 2 == 1),
                     )
 
-        a_rows = [fixed("a_rows0", [P, N], F32, XBF_HIGH - 2 * KIB + LAP), fixed("a_rows1", [P, N], F32, A_ROWS1)]
+        a_rows = [fixed("a_rows0", [P, N], F32, XBF_HIGH - 2 * KIB + LAP), held("a_rows1", [P, N], F32)]
         for t in range(2):
             nc.vector.tensor_tensor(a_rows[t][:], scores[t][:], ts_sel[:], ALU.mult)
         a_turned = [in_bank("a_turned%d" % e, 4 + e, [P, N]) for e in range(2)]
@@ -234,12 +234,6 @@ def tile_attend_gkl_w_ts_kernel(tc, xT, w_words, w_scales, y, wt, ts, xm, offs, 
                 nc.tensor.transpose(a_turned[e][:, k * P : (k + 1) * P], a_slots[:, e * P : (e + 1) * P], ident[:])
         a = a_rows + a_turned
 
-        neg_wt = fixed("neg_wt", [P, PACK], F32, XBF_HIGH + KIB)
-        nc.gpsimd.tensor_scalar(neg_wt[:], wt_sb[:], -1.0, 0.0, ALU.mult, ALU.add)
-        neg_target = held("neg_target", [P, PACK, HALF], F32)
-        for t in range(PACK):
-            nc.gpsimd.tensor_scalar(neg_target[:, t, :], y_sb[:, t, second], neg_wt[:, t : t + 1], 0.0, ALU.mult, ALU.add)
-
         def cast_on_gpsimd(m, staged):
             nc.gpsimd.tensor_scalar(
                 staged.rearrange("p (c j) -> p c j", j=PACK), xm_raw[m].rearrange("p j c -> p c j"), 1.0, 0.0, ALU.mult, ALU.add
@@ -248,6 +242,11 @@ def tile_attend_gkl_w_ts_kernel(tc, xT, w_words, w_scales, y, wt, ts, xm, offs, 
         staged01 = fixed("staged0", [P, 2 * PACK * P], BF16, STAGED0)
         for m in range(2):
             cast_on_gpsimd(m, staged01[:, m * PACK * P : (m + 1) * PACK * P])
+        neg_wt = held("neg_wt", [P, PACK], F32)
+        nc.gpsimd.tensor_scalar(neg_wt[:], wt_sb[:], -1.0, 0.0, ALU.mult, ALU.add)
+        neg_target = held("neg_target", [P, PACK, HALF], F32)
+        for t in range(PACK):
+            nc.gpsimd.tensor_scalar(neg_target[:, t, :], y_sb[:, t, second], neg_wt[:, t : t + 1], 0.0, ALU.mult, ALU.add)
 
         neg_max = [held("neg_max%d" % t, [P, 1], F32) for t in range(PACK - 1)]
         neg_max.append(fixed("neg_max3", [P, 32], F32, LAST_MAX))
@@ -283,31 +282,34 @@ def tile_attend_gkl_w_ts_kernel(tc, xT, w_words, w_scales, y, wt, ts, xm, offs, 
 
         turned = {}
 
-        def turn(u, t, source, start, stop):
-            for b in range(2):
-                nc.tensor.matmul(
-                    turned[u][:, b, t % 2, :],
-                    source[:, t, b * P : (b + 1) * P],
-                    ident[:],
-                    start=(start and b == 0),
-                    stop=(stop and b == 1),
-                    is_transpose=True,
-                )
+        def turn(t, b, source, start, stop):
+            nc.tensor.matmul(
+                turned[t // 2, b][:, t % 2, :],
+                source[:, t, b * P : (b + 1) * P],
+                ident[:],
+                start=start,
+                stop=stop,
+                is_transpose=True,
+            )
 
-        def turn_targets(u, bank):
-            turned[u] = in_bank("turned%d" % u, bank, [P, 2, 2, P])
-            for t in (2 * u, 2 * u + 1):
-                turn(u, t, neg_target, t % 2 == 0, False)
+        def turn_targets(u, slot_tiles, bank_index):
+            bank = in_bank("turned%d%d" % (u, slot_tiles[0]), bank_index, [P, len(slot_tiles), 2, P])
+            for k, b in enumerate(slot_tiles):
+                turned[u, b] = bank[:, k]
+                for t in (2 * u, 2 * u + 1):
+                    turn(t, b, neg_target, k == 0 and t % 2 == 0, False)
 
-        turn_targets(0, 3)
-        for t in range(3):
-            maximum(t)
-        turn_targets(1, 4)
+        turn_targets(0, (0, 1), 3)
+        maximum(0)
+        maximum(1)
+        quantise_xm(0, 2, staged01, at=TS_SEL)
+        zero("window2", WINDOW2)
+        maximum(2)
+        turn_targets(1, (0,), 4)
         invert(0)
         maximum(3)
+        turn_targets(1, (1,), 5)
         invert(1)
-        quantise_xm(0, 2, staged01, at=A_ROWS1)
-        zero("window2", WINDOW2)
         subtract_targets(0, first)
         nc.vector.tensor_tensor(c01[:], inv[:, 0:2], wt_sb[:, 0:2], ALU.mult)
         invert(2)
@@ -325,7 +327,8 @@ def tile_attend_gkl_w_ts_kernel(tc, xT, w_words, w_scales, y, wt, ts, xm, offs, 
             nc.scalar.activation(share[:, t, :], e_rows[t][:, second], ACT.Copy, scale=weight[t])
             if t < 2:
                 nc.scalar.activation(weight[t + 2], wt_sb[:, t + 2 : t + 3], ACT.Copy, scale=inv[:, t + 2 : t + 3])
-            turn(t // 2, t, share, False, t % 2 == 1)
+            for b in range(2):
+                turn(t, b, share, False, t == 3 or (t == 1 and b == 1))
 
         h_code = held("h_code", [P, N], U32)
         h_scale = held("h_scale", [P, N], U8)
@@ -350,28 +353,12 @@ def tile_attend_gkl_w_ts_kernel(tc, xT, w_words, w_scales, y, wt, ts, xm, offs, 
         for u in range(2):
             for b in range(2):
                 pairs = held("pairs%d%d" % (u, b), [P, P, 2], BF16)
-                sums = turned[u][:, b].rearrange("s e p -> s p e")
-                if u == 1 and b == 1:
+                sums = turned[u, b].rearrange("s e p -> s p e")
+                if u == 1:
                     nc.vector.tensor_scalar(pairs[:], sums, ts_slot[:, 2 + b : 3 + b], None, ALU.mult)
                 else:
                     nc.scalar.activation(pairs[:], sums, ACT.Copy, scale=ts_slot[:, 2 + b : 3 + b])
                 nc.tensor.transpose(back[b][:, u, :], pairs[:].rearrange("s p e -> s (p e)").bitcast(F32), ident[:])
-        h_second = [fixed("h_second%d" % b, [P, P, PACK], BF16, H_SECOND + b * KIB) for b in range(2)]
-        for b in range(2):
-            nc.vector.tensor_copy(
-                h_second[b][:].rearrange("p i t -> p (i t)").bitcast(F32).rearrange("p (s u) -> p s u", u=2),
-                back[b][:].rearrange("p u s -> p s u"),
-            )
-        for b in range(2):
-            quantise_h(slice(HALF + b * P, HALF + (b + 1) * P), h_second[b][:])
-
-        staged2 = fixed("staged2", [P, PACK * P], BF16, STAGED2)
-        nc.vector.tensor_copy(
-            staged2[:].rearrange("p (c i j) -> p c j i", i=4, j=PACK), xm_raw[2].rearrange("p j (c i) -> p c j i", i=4)
-        )
-        staged3 = fixed("staged3", [P, PACK * P], BF16, STAGED3)
-        cast_on_gpsimd(3, staged3[:])
-
         def multiply(m, s, product):
             nc.tensor.matmul_mx(
                 out=product,
@@ -409,15 +396,31 @@ def tile_attend_gkl_w_ts_kernel(tc, xT, w_words, w_scales, y, wt, ts, xm, offs, 
             return staged
 
         dw0 = even_tile(0, 0)
-        for s, bank_index in zip(quarters, (3, 5)):
+        for s, bank_index in zip(quarters, (3, 2)):
             bring(0, s, bank_index, nc.scalar.copy, dw0[:, s])
         dw1 = fixed("dw1", [P, N], F32, DW1)
-        bring(1, first, 4, nc.scalar.copy, dw1[:, first])
+        bring(1, first, 6, nc.scalar.copy, dw1[:, first])
         scatter_on_scalar(0, first, dw0[:])
+        h_second = [fixed("h_second%d" % b, [P, P, PACK], BF16, H_SECOND + b * KIB) for b in range(2)]
+        for b in range(2):
+            nc.vector.tensor_copy(
+                h_second[b][:].rearrange("p i t -> p (i t)").bitcast(F32).rearrange("p (s u) -> p s u", u=2),
+                back[b][:].rearrange("p u s -> p s u"),
+            )
+        for b in range(2):
+            quantise_h(slice(HALF + b * P, HALF + (b + 1) * P), h_second[b][:])
+
+        staged2 = fixed("staged2", [P, PACK * P], BF16, STAGED2)
+        nc.vector.tensor_copy(
+            staged2[:].rearrange("p (c i j) -> p c j i", i=4, j=PACK), xm_raw[2].rearrange("p j (c i) -> p c j i", i=4)
+        )
+        staged3 = fixed("staged3", [P, PACK * P], BF16, STAGED3)
+        cast_on_gpsimd(3, staged3[:])
+
         quantise_xm(2, 3, staged2)
         quantise_xm(3, 4, staged3)
         dw0 = even_tile(0, 1)
-        bring(0, second, 6, nc.scalar.copy, dw0[:])
+        bring(0, second, 4, nc.vector.tensor_copy, dw0[:])
         bring(1, second, 7, nc.scalar.copy, dw1[:, second])
         scatter_on_scalar(0, second, dw0[:])
         store(0)
@@ -440,11 +443,11 @@ def tile_attend_gkl_w_ts_kernel(tc, xT, w_words, w_scales, y, wt, ts, xm, offs, 
             scatter_on_vector(m, dw[:])
             store(m)
 
-        even_block(2, 2)
+        even_block(2, 5)
         quantise_xm(5, 8, cast_late(5, 8, STAGED567))
         zero("window3", WINDOW3)
         odd_block(3, 1)
-        even_block(4, 5)
+        even_block(4, 2)
         odd_block(5, 0)
         even_block(6, 3)
-        odd_block(7, 4)
+        odd_block(7, 6)

@@ -38,14 +38,14 @@ PAIRS = Y + 8 * KIB - LAP
 XM01 = PAIRS + 2 * KIB - LAP
 XM23 = 38 * KIB
 X0 = XM23 + 4 * KIB - LAP
-XBF_LOW = 70 * KIB
+XBF_LOW = 128 * KIB + 4 * LAP
 TS_POOL = XBF_LOW + 2 * KIB - LAP
 XBF_HIGH = TS_POOL + 8 * KIB - LAP
 XM47 = X0 + 8 * KIB - LAP
 SHARE = 120 * KIB
 LAST_MAX = SHARE + 4 * KIB - LAP
 C23 = LAST_MAX + LAP
-DW1 = 134 * KIB
+DW1 = 24 * KIB
 DW_ODD = {3: DW1, 5: DW1 - 2 * KIB + LAP, 7: DW1 + 2 * KIB - LAP}
 H_SECOND = 128 * KIB
 STAGED2 = H_SECOND + 2 * KIB - LAP

from contextlib import ExitStack

import concourse.mybir as mybir

N, T, D, R = 512, 2048, 1024, 512
FLOPS = 2 * 2 * D * R * N

F32 = mybir.dt.float32
BF16 = mybir.dt.bfloat16
I32 = mybir.dt.int32
U32 = mybir.dt.uint32
U16 = mybir.dt.uint16
U8 = mybir.dt.uint8
E4M3 = mybir.dt.float8_e4m3fn_x4
E5M2 = mybir.dt.float8_e5m2_x4
E2M1 = mybir.dt.float4_e2m1fn_x4
ALU = mybir.AluOpType
ACT = mybir.ActivationFunctionType
X = mybir.AxisListType.X

P = 128
PACK = 4
PASSES = D // (P * PACK)
HALF = N // 2
KIB = 1024
LAP = 64

X1 = 96 * KIB
SCALES = X1 + 8 * KIB - LAP
WINDOW1 = 14 * KIB
STAGED567 = 0
STAGED3 = STAGED567 + 3 * KIB - LAP
STAGED4 = STAGED3 + KIB - LAP
WINDOW3 = STAGED4 + KIB - LAP
H_FIRST = STAGED3 - 2 * KIB + LAP
Y = 24 * KIB
PAIRS = Y + 8 * KIB - LAP
XM01 = PAIRS + 2 * KIB - LAP
XM23 = 38 * KIB
X0 = XM23 + 4 * KIB - LAP
XBF_LOW = 128 * KIB + 4 * LAP
TS_POOL = XBF_LOW + 2 * KIB - LAP
XBF_HIGH = TS_POOL + 8 * KIB - LAP
XM47 = X0 + 8 * KIB - LAP
SHARE = 120 * KIB
LAST_MAX = SHARE + 4 * KIB - LAP
C23 = LAST_MAX + LAP
DW1 = 24 * KIB
DW_ODD = {3: DW1, 5: DW1 - 2 * KIB + LAP, 7: DW1 + 2 * KIB - LAP}
H_SECOND = 128 * KIB
STAGED2 = H_SECOND + 2 * KIB - LAP
TS_SEL = 60 * KIB
STAGED0 = XBF_HIGH + 2 * KIB - LAP
WINDOW2 = STAGED0 + 2 * KIB - LAP
WINDOW0 = 150 * KIB
DW_EVEN = (158 * KIB, 159 * KIB)


def tile_attend_gkl_w_ts_kernel(tc, xT, w_words, w_scales, y, wt, ts, xm, offs, out):
    nc = tc.nc
    with ExitStack() as ctx:
        keep = ctx.enter_context(tc.tile_pool(name="keep", bufs=1))
        placed = ctx.enter_context(tc.tile_pool(name="placed", bufs=1))
        psum = ctx.enter_context(tc.psum_pool(name="psum", bufs=1))

        def in_bank(name, k, shape):
            return psum.tile(shape, F32, name=name, tag="bank%d" % k)

        def held(name, shape, dtype):
            return keep.tile(shape, dtype, name=name, align_bytes=64)

        def fixed(name, shape, dtype, at):
            return placed.tile(shape, dtype, name=name, align_bytes=64, offset=at)

        offsets = keep.tile([P, N // 16], U16, name="offsets")
        nc.sync.dma_start(offsets[:], offs)
        scale_pool = fixed("scale_pool", [P, T // 4], I32, SCALES)
        nc.sync.dma_start(scale_pool[0:32, :], w_scales.rearrange("o f t -> (o f) t").bitcast(I32))
        ts_cols = held("ts_cols", [P, T // P], F32)
        nc.sync.dma_start(ts_cols[:], ts[0:1, :].rearrange("o (p c) -> (o p) c", p=P))
        wt_sb = held("wt_sb", [P, PACK], F32)
        nc.sync.dma_start(wt_sb[:], wt[0].rearrange("(p t) o -> p (t o)", t=PACK))
        word_pool = held("word_pool", [P, T], I32)
        nc.sync.dma_start(word_pool[:], w_words[0].rearrange("p t b -> p (t b)").bitcast(I32))
        x_rows = [xT[0, 512 * o : 512 * (o + 1), :].rearrange("(p j) r -> p j r", j=PACK) for o in range(PASSES)]
        x_first = fixed("x_first", [P, PACK, R], F32, X0)
        nc.sync.dma_start(x_first[:], x_rows[0])

        nc.gpsimd.memset(scale_pool[32:64, :], 0)
        nc.gpsimd.memset(scale_pool[64:128, :], 0)
        windows = [fixed("window0", [P, T], F32, WINDOW0)]
        nc.vector.memset(windows[0][:], 0.0)
        ident = held("ident", [P, P], F32)
        nc.gpsimd.memset(ident[:], 0.0)
        nc.gpsimd.affine_select(
            out=ident[:], in_=ident[:], compare_op=ALU.not_equal, fill=1.0, base=0, pattern=[[-1, P]], channel_multiplier=1
        )
        planes = [held("plane%d" % o, [P, N // 4], I32) for o in range(PASSES)]
        for plane in planes:
            nc.gpsimd.memset(plane[:], 0)
        windows.append(fixed("window1", [P, T], F32, WINDOW1))
        nc.gpsimd.memset(windows[1][:], 0.0)

        scale_sel = held("scale_sel", [P, N], U8)
        nc.vector.tensor_copy(scale_sel[:], scale_pool[:].bitcast(U8).indirect(offsets[:]))

        def place_scales(plane, o):
            for q in range(4):
                row = 16 * o + 4 * q
                nc.sync.dma_start(plane[32 * q : 32 * q + 4, :], scale_sel[:].bitcast(I32)[row : row + 4, :])

        def zero(name, at):
            window = fixed(name, [P, T], F32, at)
            for q in range(T // N):
                nc.gpsimd.memset(window[:, q * N : (q + 1) * N], 0.0)
            windows.append(window)

        place_scales(planes[0], 0)
        x_second = fixed("x_second", [P, PACK, R], F32, X1)
        nc.sync.dma_start(x_second[:], x_rows[1])
        place_scales(planes[1], 1)

        ts_pool = fixed("ts_pool", [P, T], F32, TS_POOL)
        ts_view = ts_pool[:].rearrange("m (p c) -> m p c", p=P)
        for b in range(4):
            bank = in_bank("ts_spread%d" % b, PACK + b, [P, PACK, P])
            for k in range(PACK):
                c = PACK * b + k
                nc.tensor.transpose(bank[:, k, :], ts_cols[:, c : c + 1].to_broadcast([P, P]), ident[:])
            nc.scalar.copy(ts_view[:, :, PACK * b : PACK * (b + 1)], bank[:].rearrange("m k p -> m p k"))

        w_pair = fixed("w_pair", [P, N], U32, PAIRS)
        nc.vector.tensor_copy(w_pair[:], word_pool[:].bitcast(U32).indirect(offsets[:]))
        w_scale = [plane[:].bitcast(U8) for plane in planes]

        w_code = held("w_code", [P, PASSES * 2 * N], U8)
        nc.vector.tensor_copy(
            w_code[:].bitcast(U16).rearrange("p (o i) -> p o i", o=PASSES),
            w_pair[:].bitcast(U16).rearrange("p (i o) -> p o i", o=PASSES),
        )

        xm_rows = xm[0].rearrange("(p j) d -> p j d", j=PACK)
        xm_raw = {}

        def load_xm(lo, hi, at):
            raw = fixed("xm_raw%d" % lo, [P, PACK, (hi - lo) * P], F32, at)
            nc.sync.dma_start(raw[:], xm_rows[:, :, lo * P : hi * P])
            for m in range(lo, hi):
                xm_raw[m] = raw[:, :, (m - lo) * P : (m - lo + 1) * P]

        load_xm(0, 2, XM01)
        y_sb = fixed("y_sb", [P, PACK, N], F32, Y)
        nc.sync.dma_start(y_sb[:], y[0].rearrange("(p t) i -> p t i", t=PACK))

        ts_sel = fixed("ts_sel", [P, N], F32, TS_SEL)
        nc.scalar.activation(ts_sel[:], ts_pool[:].indirect(offsets[:]), ACT.Copy)
        first, second, whole = slice(0, HALF), slice(HALF, N), slice(0, N)
        ts_slot = held("ts_slot", [P, PACK], F32)
        for k in range(PACK):
            ts_bank = in_bank("ts_bank%d" % k, k, [P, P])
            nc.tensor.transpose(ts_bank[:], ts_sel[:, k * P : (k + 1) * P], ident[:])
            nc.scalar.copy(ts_slot[:, k : k + 1], ts_bank[:, 0:1])

        wt_ts = held("wt_ts", [P, PACK, HALF], F32)
        for t in range(PACK):
            nc.scalar.activation(wt_ts[:, t, :], ts_sel[:, first], ACT.Copy, scale=wt_sb[:, t : t + 1])

        x_code = {}
        x_scale = {}
        for o in range(PASSES):
            for u in range(2):
                x_code[o, u] = held("x_code%d%d" % (o, u), [P, 2 * P], U32)
                x_scale[o, u] = held("x_scale%d%d" % (o, u), [P, 2 * P], U8)

        def cast_x(copy, staged, raw, u):
            src = raw[:].rearrange("p j (m t) -> p m j t", t=PACK)[:, :, :, 2 * u : 2 * u + 2]
            copy(staged[:].rearrange("p (t m j) -> p m j t", t=2, j=PACK), src)

        def quantise_x(o, u, staged, lo, hi):
            nc.vector.quantize_mx(
                out=x_code[o, u][:, lo:hi].bitcast(E4M3),
                scales=x_scale[o, u][:, lo:hi],
                in_=staged[:, PACK * lo : PACK * hi],
            )

        x_bf00 = held("x_bf00", [P, 2 * P * PACK], BF16)
        x_bf01 = fixed("x_bf01", [P, 2 * P * PACK], BF16, XBF_LOW - KIB)
        cast_x(nc.vector.tensor_copy, x_bf00, x_first, 0)
        cast_x(nc.vector.tensor_copy, x_bf01, x_first, 1)
        load_xm(2, 4, XM23)
        load_xm(4, 8, XM47)
        quantise_x(0, 0, x_bf00, 0, 2 * P)
        quantise_x(0, 1, x_bf01, 0, 2 * P)
        x_bf10 = fixed("x_bf10", [P, 2 * P * PACK], BF16, XBF_LOW - KIB)
        x_bf11 = fixed("x_bf11", [P, 2 * P * PACK], BF16, XBF_HIGH)
        cast_x(nc.vector.tensor_copy, x_bf10, x_second, 0)
        cast_x(nc.scalar.copy, x_bf11, x_second, 1)
        quantise_x(1, 0, x_bf10, 0, P)
        quantise_x(1, 0, x_bf10, P, 2 * P)
        quantise_x(1, 1, x_bf11, 0, 2 * P)

        scores = [in_bank("scores%d" % t, t, [P, N]) for t in range(2)]
        slot_scores = [in_bank("slot_scores%d" % v, 2 + v, [P, 2, 2 * P]) for v in range(2)]
        for o in range(PASSES):
            for t in range(2):
                nc.tensor.matmul_mx(
                    out=scores[t][:],
                    lhsT=x_code[o, 0][:, t * P : (t + 1) * P].bitcast(E4M3),
                    lhsT_scale=x_scale[o, 0][:, t * P : (t + 1) * P],
                    rhs=w_code[:, o * 2 * N : (o + 1) * 2 * N].bitcast(E2M1),
                    rhs_scale=w_scale[o],
                    start=(o == 0),
                    stop=(o == PASSES - 1),
                )
                for k in (2 * t, 2 * t + 1):
                    nc.tensor.matmul_mx(
                        out=slot_scores[t][:, k % 2, :],
                        lhsT=w_code[:, o * 2 * N + k * 2 * P : o * 2 * N + (k + 1) * 2 * P].bitcast(E2M1),
                        lhsT_scale=w_scale[o][:, k * P : (k + 1) * P],
                        rhs=x_code[o, 1][:].bitcast(E4M3),
                        rhs_scale=x_scale[o, 1][:],
                        start=(o == 0 and k % 2 == 0),
                        stop=(o == PASSES - 1 and k % 2 == 1),
                    )

        a_rows = [fixed("a_rows0", [P, N], F32, XBF_HIGH - 2 * KIB + LAP), held("a_rows1", [P, N], F32)]
        for t in range(2):
            nc.vector.tensor_tensor(a_rows[t][:], scores[t][:], ts_sel[:], ALU.mult)
        a_turned = [in_bank("a_turned%d" % e, 4 + e, [P, N]) for e in range(2)]
        for k in range(PACK):
            a_slots = held("a_slots%d" % k, [P, 2 * P], F32)
            nc.scalar.activation(a_slots[:], slot_scores[k // 2][:, k % 2, :], ACT.Copy, scale=ts_slot[:, k : k + 1])
            for e in range(2):
                nc.tensor.transpose(a_turned[e][:, k * P : (k + 1) * P], a_slots[:, e * P : (e + 1) * P], ident[:])
        a = a_rows + a_turned

        def cast_on_gpsimd(m, staged):
            nc.gpsimd.tensor_scalar(
                staged.rearrange("p (c j) -> p c j", j=PACK), xm_raw[m].rearrange("p j c -> p c j"), 1.0, 0.0, ALU.mult, ALU.add
            )

        staged01 = fixed("staged0", [P, 2 * PACK * P], BF16, STAGED0)
        for m in range(2):
            cast_on_gpsimd(m, staged01[:, m * PACK * P : (m + 1) * PACK * P])
        neg_wt = held("neg_wt", [P, PACK], F32)
        nc.gpsimd.tensor_scalar(neg_wt[:], wt_sb[:], -1.0, 0.0, ALU.mult, ALU.add)
        neg_target = held("neg_target", [P, PACK, HALF], F32)
        for t in range(PACK):
            nc.gpsimd.tensor_scalar(neg_target[:, t, :], y_sb[:, t, second], neg_wt[:, t : t + 1], 0.0, ALU.mult, ALU.add)

        neg_max = [held("neg_max%d" % t, [P, 1], F32) for t in range(PACK - 1)]
        neg_max.append(fixed("neg_max3", [P, 32], F32, LAST_MAX))
        e_rows = [held("e%d" % t, [P, N], F32) for t in range(PACK)]
        total = held("total", [P, PACK], F32)
        inv = held("inv", [P, PACK], F32)
        c01 = held("c01", [P, 2], F32)
        g = held("g", [P, PACK, HALF], F32)

        def maximum(t):
            nc.vector.tensor_reduce(neg_max[t][:, 0:1], a[t][:], X, ALU.max, negate=True)
            nc.scalar.activation(
                e_rows[t][:], a[t][:], ACT.Exp, bias=neg_max[t][:, 0:1], scale=1.0, accum_out=total[:, t : t + 1]
            )

        def invert(t):
            nc.vector.reciprocal(inv[:, t : t + 1], total[:, t : t + 1])

        def subtract_targets(t, s):
            nc.vector.scalar_tensor_tensor(
                g[:, t, s], e_rows[t][:, s], inv[:, t : t + 1], y_sb[:, t, s], ALU.mult, ALU.subtract
            )

        xm_scale = held("xm_scale", [P, D], U8)
        xm_code = {}

        def quantise_xm(lo, hi, staged, at=None):
            name = "xm_code%d" % lo
            code = held(name, [P, (hi - lo) * P], U32) if at is None else fixed(name, [P, (hi - lo) * P], U32, at)
            nc.vector.quantize_mx(out=code[:].bitcast(E4M3), scales=xm_scale[:, lo * P : hi * P], in_=staged[:])
            for m in range(lo, hi):
                xm_code[m] = code[:, (m - lo) * P : (m - lo + 1) * P]

        turned = {}

        def turn(t, b, source, start, stop):
            nc.tensor.matmul(
                turned[t // 2, b][:, t % 2, :],
                source[:, t, b * P : (b + 1) * P],
                ident[:],
                start=start,
                stop=stop,
                is_transpose=True,
            )

        def turn_targets(u, slot_tiles, bank_index):
            bank = in_bank("turned%d%d" % (u, slot_tiles[0]), bank_index, [P, len(slot_tiles), 2, P])
            for k, b in enumerate(slot_tiles):
                turned[u, b] = bank[:, k]
                for t in (2 * u, 2 * u + 1):
                    turn(t, b, neg_target, k == 0 and t % 2 == 0, False)

        turn_targets(0, (0, 1), 3)
        maximum(0)
        maximum(1)
        quantise_xm(0, 2, staged01, at=TS_SEL)
        zero("window2", WINDOW2)
        maximum(2)
        turn_targets(1, (0,), 4)
        invert(0)
        maximum(3)
        turn_targets(1, (1,), 5)
        invert(1)
        subtract_targets(0, first)
        nc.vector.tensor_tensor(c01[:], inv[:, 0:2], wt_sb[:, 0:2], ALU.mult)
        invert(2)
        subtract_targets(1, first)
        invert(3)
        subtract_targets(2, first)
        quarters = (slice(0, P), slice(P, HALF))
        for s in quarters:
            subtract_targets(3, s)

        share = fixed("share", [P, PACK, HALF], F32, SHARE)
        c23 = fixed("c23", [P, 2], F32, C23)
        weight = [c01[:, 0:1], c01[:, 1:2], c23[:, 0:1], c23[:, 1:2]]
        for t in range(PACK):
            nc.scalar.activation(share[:, t, :], e_rows[t][:, second], ACT.Copy, scale=weight[t])
            if t < 2:
                nc.scalar.activation(weight[t + 2], wt_sb[:, t + 2 : t + 3], ACT.Copy, scale=inv[:, t + 2 : t + 3])
            for b in range(2):
                turn(t, b, share, False, t == 3 or (t == 1 and b == 1))

        h_code = held("h_code", [P, N], U32)
        h_scale = held("h_scale", [P, N], U8)

        def quantise_h(s, staged):
            nc.vector.quantize_mx(
                out=h_code[:, s].bitcast(E5M2), scales=h_scale[:, s], in_=staged.rearrange("p i t -> p (i t)")
            )

        h_first = fixed("h_first", [P, HALF, PACK], BF16, H_FIRST)
        for s in quarters:
            nc.vector.tensor_tensor(
                h_first[:, s, :].rearrange("p (c i) t -> p c t i", i=2),
                g[:, :, s].rearrange("p t (c i) -> p c t i", i=2),
                wt_ts[:, :, s].rearrange("p t (c i) -> p c t i", i=2),
                ALU.mult,
            )
        for s in quarters:
            quantise_h(s, h_first[:, s, :])

        back = [in_bank("back%d" % b, b, [P, 2, P]) for b in range(2)]
        for u in range(2):
            for b in range(2):
                pairs = held("pairs%d%d" % (u, b), [P, P, 2], BF16)
                sums = turned[u, b].rearrange("s e p -> s p e")
                if u == 1:
                    nc.vector.tensor_scalar(pairs[:], sums, ts_slot[:, 2 + b : 3 + b], None, ALU.mult)
                else:
                    nc.scalar.activation(pairs[:], sums, ACT.Copy, scale=ts_slot[:, 2 + b : 3 + b])
                nc.tensor.transpose(back[b][:, u, :], pairs[:].rearrange("s p e -> s (p e)").bitcast(F32), ident[:])
        def multiply(m, s, product):
            nc.tensor.matmul_mx(
                out=product,
                lhsT=xm_code[m].bitcast(E4M3),
                lhsT_scale=xm_scale[:, m * P : (m + 1) * P],
                rhs=h_code[:, s].bitcast(E5M2),
                rhs_scale=h_scale[:, s],
                start=True,
                stop=True,
            )

        def bring(m, s, bank_index, copy, dw):
            bank = in_bank("product%d_%d" % (m, s.start), bank_index, [P, s.stop - s.start])
            multiply(m, s, bank[:])
            copy(dw, bank[:])

        def scatter_on_scalar(m, s, dw):
            nc.scalar.activation(windows[m % 4][:].indirect(offsets[:, s.start // 16 : s.stop // 16]), dw, ACT.Copy)

        def scatter_on_vector(m, dw):
            nc.vector.tensor_copy(windows[m % 4][:].indirect(offsets[:]), dw)

        def store(m):
            nc.sync.dma_start(out[m * P : (m + 1) * P, :], windows[m % 4][:])

        halves = (first, second)

        def even_tile(m, k):
            return fixed("dw%d_%d" % (m, k), [P, HALF], F32, DW_EVEN[k])

        def cast_late(lo, hi, at):
            staged = fixed("staged%d" % lo, [P, (hi - lo) * PACK * P], BF16, at)
            for m in range(lo, hi):
                cast_on_gpsimd(m, staged[:, (m - lo) * PACK * P : (m - lo + 1) * PACK * P])
            return staged

        dw0 = even_tile(0, 0)
        for s, bank_index in zip(quarters, (3, 2)):
            bring(0, s, bank_index, nc.scalar.copy, dw0[:, s])
        dw1 = fixed("dw1", [P, N], F32, DW1)
        bring(1, first, 6, nc.scalar.copy, dw1[:, first])
        scatter_on_scalar(0, first, dw0[:])
        h_second = [fixed("h_second%d" % b, [P, P, PACK], BF16, H_SECOND + b * KIB) for b in range(2)]
        for b in range(2):
            nc.vector.tensor_copy(
                h_second[b][:].rearrange("p i t -> p (i t)").bitcast(F32).rearrange("p (s u) -> p s u", u=2),
                back[b][:].rearrange("p u s -> p s u"),
            )
        for b in range(2):
            quantise_h(slice(HALF + b * P, HALF + (b + 1) * P), h_second[b][:])

        staged2 = fixed("staged2", [P, PACK * P], BF16, STAGED2)
        nc.vector.tensor_copy(
            staged2[:].rearrange("p (c i j) -> p c j i", i=4, j=PACK), xm_raw[2].rearrange("p j (c i) -> p c j i", i=4)
        )
        staged3 = fixed("staged3", [P, PACK * P], BF16, STAGED3)
        cast_on_gpsimd(3, staged3[:])

        quantise_xm(2, 3, staged2)
        quantise_xm(3, 4, staged3)
        dw0 = even_tile(0, 1)
        bring(0, second, 4, nc.vector.tensor_copy, dw0[:])
        bring(1, second, 7, nc.scalar.copy, dw1[:, second])
        scatter_on_scalar(0, second, dw0[:])
        store(0)
        quantise_xm(4, 5, cast_late(4, 5, STAGED4))
        scatter_on_vector(1, dw1[:])
        store(1)

        def even_block(m, bank_index):
            bank = in_bank("product%d" % m, bank_index, [P, N])
            multiply(m, whole, bank[:])
            for k in range(2):
                dw = even_tile(m, k)
                nc.scalar.copy(dw[:], bank[:, halves[k]])
                scatter_on_scalar(m, halves[k], dw[:])
            store(m)

        def odd_block(m, bank_index):
            dw = fixed("dw%d" % m, [P, N], F32, DW_ODD[m])
            bring(m, whole, bank_index, nc.vector.tensor_copy, dw[:])
            scatter_on_vector(m, dw[:])
            store(m)

        even_block(2, 5)
        quantise_xm(5, 8, cast_late(5, 8, STAGED567))
        zero("window3", WINDOW3)
        odd_block(3, 1)
        even_block(4, 2)
        odd_block(5, 0)
        even_block(6, 3)
        odd_block(7, 6)
